import numpy as np
import ml_dtypes


def mxq(x, axis, fmt="e4m3"):
    dtype, down = {"e4m3": (ml_dtypes.float8_e4m3fn, 7), "e5m2": (ml_dtypes.float8_e5m2, 14)}[fmt]
    v = np.moveaxis(np.asarray(x, np.float32).astype(ml_dtypes.bfloat16).astype(np.float64), axis, -1)
    blocks = v.reshape(v.shape[:-1] + (-1, 32))
    amax = np.abs(blocks).max(-1, keepdims=True)
    byte = np.maximum(np.where(amax > 0, np.frexp(amax)[1] - 1 + 127, 0) - down, 1)
    scale = np.exp2(byte - 127.0)
    codes = (blocks / scale).astype(np.float32).astype(dtype).astype(np.float64)
    return np.moveaxis((codes * scale).reshape(v.shape), -1, axis)


WIDE = False


def mx_kscale(k):
    if not WIDE:
        return np.ones(k)
    levels = np.array([10, -10, 5, -5, 0])
    if k % 512:
        return np.exp2(np.random.permutation(np.resize(levels, k // 32))).repeat(32)
    a = np.empty((k // 512, 16))
    for p in range(k // 512):
        a[p, :8] = np.random.permutation(np.resize(levels, 8))
        for g in range(8):
            far = levels[np.abs(levels - a[p, g]) >= 10]
            a[p, g + 8] = far[np.random.randint(len(far))]
    return np.exp2(a.ravel()).repeat(32)


def f64(x):
    return np.asarray(x).astype(np.float64)


def striped(idx):
    return np.tile(idx.reshape(-1, 16).T, (8, 1)).astype(np.uint16)


def unstriped(offs):
    return offs[:16].T.reshape(-1).astype(np.int64)


E2M1 = np.array([0.0, 0.5, 1.0, 1.5, 2.0, 3.0, 4.0, 6.0, -0.0, -0.5, -1.0, -1.5, -2.0, -3.0, -4.0, -6.0])


def pack_weight(w, fmt):
    k, n = w.shape
    w = f64(np.asarray(w, np.float32).astype(ml_dtypes.bfloat16)).reshape(k // 32, 32, n)
    amax = np.abs(w).max(1)
    if fmt == "e4m3":
        byte = np.frexp(amax)[1] - 1 + 127 - 7
    else:
        mant, ex = np.frexp(amax / 6.0)
        byte = np.where(mant > 0.5, ex, ex - 1) + 127
    byte = np.clip(np.where(amax > 0, byte, 1), 1, 254)
    scaled = (w * np.exp2(127.0 - byte)[:, None, :]).reshape(k, n).astype(np.float32)
    by_word = np.ascontiguousarray(scaled.reshape(k // 512, 128, 4, n).transpose(0, 1, 3, 2))
    if fmt == "e4m3":
        words = by_word.astype(ml_dtypes.float8_e4m3fn).view(np.uint8)
    else:
        c = by_word.astype(ml_dtypes.float4_e2m1fn).view(np.uint8) & 0xF
        words = (c[..., 0::2] | (c[..., 1::2] << 4)).reshape(k // 512, 128, 2 * n)
    return np.ascontiguousarray(words), np.ascontiguousarray(byte.astype(np.uint8).reshape(k // 512, 16, n))


def unpack_weight(words, scales, fmt):
    g, _, n = scales.shape
    words = np.ascontiguousarray(words).reshape(g, 128, n, -1)
    if fmt == "e4m3":
        vals = words.view(ml_dtypes.float8_e4m3fn).astype(np.float64)
    else:
        nib = np.empty((g, 128, n, 4), np.uint8)
        nib[..., 0::2] = words & 0xF
        nib[..., 1::2] = words >> 4
        vals = E2M1[nib]
    vals = vals * np.repeat(np.exp2(scales.astype(np.float64) - 127.0), 8, axis=1)[..., None]
    return vals.transpose(0, 1, 3, 2).reshape(g * 512, n)


def gelu(v):
    return 0.5 * v * (1.0 + np.tanh(np.sqrt(2.0 / np.pi) * (v + 0.044715 * v**3)))


K, K2, T, T2, S, H, N = 1024, 512, 2048, 4096, 1024, 1024, 768

def setup_inputs():
    n = np.random.standard_normal
    s = mx_kscale(K)[:, None]
    s2 = mx_kscale(K2)[:, None]
    u = mx_kscale(H)[:, None]
    tab_words, tab_scales = pack_weight(n((K, T)) * s, "e4m3")
    tab2_words, tab2_scales = pack_weight(n((K2, T2)) * s2, "e4m3")
    w2_words, w2_scales = pack_weight(n((K2, H)) / np.sqrt(K2) / s2, "e2m1")
    wm_words, wm_scales = pack_weight(n((H, N)) / np.sqrt(H) / u, "e4m3")
    return {
        "tab_words": tab_words, "tab_scales": tab_scales,
        "tab2_words": tab2_words, "tab2_scales": tab2_scales,
        "offs": striped(np.random.permutation(T)[:S]),
        "offs2": striped(np.random.permutation(T2)[:S]),
        "w1": (n((K, H)) / np.sqrt(K) / s).astype(np.float32),
        "w2_words": w2_words, "w2_scales": w2_scales,
        "gain": (0.45 * np.exp(0.3 * n(H)) * u[:, 0]).astype(np.float32),
        "wm_words": wm_words, "wm_scales": wm_scales,
    }

def reference(tab_words, tab_scales, tab2_words, tab2_scales, offs, offs2, w1, w2_words, w2_scales, gain, wm_words, wm_scales):
    v = unpack_weight(tab_words, tab_scales, "e4m3")[:, unstriped(offs)]
    v2 = unpack_weight(tab2_words, tab2_scales, "e4m3")[:, unstriped(offs2)]
    w2 = unpack_weight(w2_words, w2_scales, "e2m1")
    wm = unpack_weight(wm_words, wm_scales, "e4m3")
    p = mxq(f64(w1), 0, "e4m3").T @ v
    q = w2.T @ v2
    h = f64(gain)[:, None] * (p * q) * np.abs(p - q)
    return wm.T @ mxq(h, 0, "e4m3")

@@ -1,0 +1,256 @@
+from contextlib import ExitStack
+
+import concourse.mybir as mybir
+
+K, K2, T, T2, S, H, N = 1024, 512, 2048, 4096, 1024, 1024, 768
+FLOPS = 2 * S * (K * H + K2 * H + H * N)
+
+F32 = mybir.dt.float32
+BF16 = mybir.dt.bfloat16
+I32 = mybir.dt.int32
+U32 = mybir.dt.uint32
+U16 = mybir.dt.uint16
+U8 = mybir.dt.uint8
+FP8X4 = mybir.dt.float8_e4m3fn_x4
+FP4X4 = mybir.dt.float4_e2m1fn_x4
+ALU = mybir.AluOpType
+ACT = mybir.ActivationFunctionType
+
+P = 128
+PACK = 4
+PASS = P * PACK
+BANK = 512
+LIST_ROWS = 16
+
+CHUNKS = [(0, 256), (256, 256), (512, 256), (768, 128), (896, 128)]
+GROUPS = [(0, 0), (0, 1), (1, 0), (1, 1), (0, 2), (1, 2), (0, 3), (1, 3), (0, 4), (1, 4)]
+
+
+def tile_list_entity_merge_scores_kernel(
+    tc, tab_words, tab_scales, tab2_words, tab2_scales, offs, offs2, w1, w2_words, w2_scales, gain, wm_words, wm_scales, out
+):
+    nc = tc.nc
+    with ExitStack() as ctx:
+        lists = ctx.enter_context(tc.tile_pool(name="lists", bufs=1))
+        keep = ctx.enter_context(tc.tile_pool(name="keep", bufs=1))
+        ring = ctx.enter_context(tc.tile_pool(name="ring", bufs=3))
+        psum_p = ctx.enter_context(tc.psum_pool(name="psum_p", bufs=4))
+        psum_qo = ctx.enter_context(tc.psum_pool(name="psum_qo", bufs=4))
+
+        idx = lists.tile([P, S // LIST_ROWS], U16, name="idx")
+        idx2 = lists.tile([P, S // LIST_ROWS], U16, name="idx2")
+
+        tab_w = [keep.tile([P, T], I32, name="tab_w%d" % a, align_bytes=64) for a in range(2)]
+        tab_s = keep.tile([P, T // 4], I32, name="tab_s", align_bytes=64)
+        tab2_w = keep.tile([P, T2], I32, name="tab2_w", align_bytes=64)
+        tab2_s = keep.tile([P, T2 // 4], I32, name="tab2_s", align_bytes=64)
+        v_w = [keep.tile([P, S], U32, name="v_w%d" % a, align_bytes=64) for a in range(2)]
+        v_s = keep.tile([P, S], U8, name="v_s", align_bytes=64)
+        v2_w = keep.tile([P, S], U32, name="v2_w", align_bytes=64)
+        v2_s = keep.tile([P, S], U8, name="v2_s", align_bytes=64)
+        w2_raw_w = keep.tile([P, H // 2], I32, name="w2_raw_w", align_bytes=64)
+        w2_raw_s = keep.tile([P, H // 4], I32, name="w2_raw_s", align_bytes=64)
+        w2_w = keep.tile([P, 2 * H], U8, name="w2_w", align_bytes=64)
+        w2_s = keep.tile([P, H], U8, name="w2_s", align_bytes=64)
+        w1_raw = [[keep.tile([P, PACK, PASS], F32, name="w1_raw%d%d" % (a, c), align_bytes=64) for c in range(2)] for a in range(2)]
+        w1_bf = [[keep.tile([P, PACK * PASS], BF16, name="w1_bf%d%d" % (a, c), align_bytes=64) for c in range(2)] for a in range(2)]
+        w1_w = [[keep.tile([P, PASS], U32, name="w1_w%d%d" % (a, c), align_bytes=64) for c in range(2)] for a in range(2)]
+        w1_s = [[keep.tile([P, PASS], U8, name="w1_s%d%d" % (a, c), align_bytes=64) for c in range(2)] for a in range(2)]
+        wm_w = keep.tile([P, 2, N], I32, name="wm_w", align_bytes=64)
+        wm_s = keep.tile([P, 2, N // 4], I32, name="wm_s", align_bytes=64)
+        gain_sb = keep.tile([P, 2, PACK], F32, name="gain_sb")
+        gain_recip = keep.tile([P, 2, PACK], F32, name="gain_recip")
+        gain_inv = keep.tile([P, 2, PACK], F32, name="gain_inv")
+        q_sb = [[keep.tile([P, PACK, BANK], F32, name="q_sb%d%d" % (a, hf), align_bytes=64) for hf in range(2)] for a in range(2)]
+        h_w = [[keep.tile([P, w], U32, name="h_w%d%d" % (a, c), align_bytes=64) for c, (j0, w) in enumerate(CHUNKS)] for a in range(2)]
+        h_s = [[keep.tile([P, w], U8, name="h_s%d%d" % (a, c), align_bytes=64) for c, (j0, w) in enumerate(CHUNKS)] for a in range(2)]
+
+        nc.vector.memset(tab_s[:], 0)
+        nc.vector.memset(tab2_s[:], 0)
+        nc.vector.memset(w2_raw_s[:], 0)
+        nc.vector.memset(wm_s[:], 0)
+
+        def load_w1(a, c):
+            rows = w1[c * PASS : (c + 1) * PASS, a * PASS : (a + 1) * PASS]
+            nc.sync.dma_start(out=w1_raw[a][c][:], in_=rows.rearrange("(p j) r -> p j r", j=PACK))
+
+        def load_tab(c):
+            nc.sync.dma_start(out=tab_w[c][:], in_=tab_words[c].rearrange("p t i -> p (t i)").bitcast(I32))
+
+        nc.sync.dma_start(idx2[:], offs2)
+        nc.sync.dma_start(out=w2_raw_w[:], in_=w2_words[0].bitcast(I32))
+        nc.sync.dma_start(out=tab2_w[:], in_=tab2_words[0].rearrange("p t i -> p (t i)").bitcast(I32))
+        for quad in range(4):
+            nc.gpsimd.dma_start(out=tab2_s[32 * quad : 32 * quad + 4, :], in_=tab2_scales[0, 4 * quad : 4 * quad + 4, :].bitcast(I32))
+        for quad in range(4):
+            nc.gpsimd.dma_start(out=w2_raw_s[32 * quad : 32 * quad + 4, :], in_=w2_scales[0, 4 * quad : 4 * quad + 4, :].bitcast(I32))
+        nc.sync.dma_start(idx[:], offs)
+        nc.sync.dma_start(out=gain_sb[:], in_=gain.rearrange("(a p t) -> p a t", a=2, t=PACK))
+        load_w1(0, 0)
+        for quad in range(4):
+            nc.sync.dma_start(out=tab_s[32 * quad : 32 * quad + 8, :], in_=tab_scales[:, 4 * quad : 4 * quad + 4, :].bitcast(I32))
+        load_w1(0, 1)
+        load_tab(0)
+        load_tab(1)
+        load_w1(1, 0)
+        load_w1(1, 1)
+        for quad in range(4):
+            nc.sync.dma_start(
+                out=wm_s[32 * quad : 32 * quad + 4, :, :],
+                in_=wm_scales[:, 4 * quad : 4 * quad + 4, :].bitcast(I32).rearrange("a r n -> r a n"),
+            )
+        nc.sync.dma_start(out=wm_w[:], in_=wm_words.rearrange("a p n i -> p a (n i)").bitcast(I32))
+
+        def gather(dst, window, dtype, offsets, j0, width):
+            picked = window[:].bitcast(dtype).indirect(offsets[:, j0 // LIST_ROWS : (j0 + width) // LIST_ROWS])
+            nc.vector.tensor_copy(out=dst[:, j0 : j0 + width], in_=picked)
+
+        def permute_w2():
+            nc.vector.tensor_copy(
+                out=w2_w[:].bitcast(U16).rearrange("p (a t m) -> p a t m", a=2, t=PACK),
+                in_=w2_raw_w[:].bitcast(U16).rearrange("p (a m t) -> p a t m", a=2, t=PACK),
+            )
+            nc.vector.tensor_copy(
+                out=w2_s[:].rearrange("p (a t m) -> p a t m", a=2, t=PACK),
+                in_=w2_raw_s[:].bitcast(U8).rearrange("p (a m t) -> p a t m", a=2, t=PACK),
+            )
+
+        def cast_w1(a, c, on_gpsimd):
+            order = "m t j" if on_gpsimd else "m j t"
+            dst = w1_bf[a][c][:].rearrange("p (t m j) -> p " + order, t=PACK, j=PACK)
+            src = w1_raw[a][c][:].rearrange("p j (m t) -> p " + order, t=PACK)
+            if on_gpsimd:
+                nc.gpsimd.tensor_scalar(out=dst, in0=src, scalar1=1.0, scalar2=0.0, op0=ALU.mult, op1=ALU.add)
+            else:
+                nc.scalar.copy(out=dst, in_=src)
+
+        def quantize_w1(a, c):
+            nc.vector.quantize_mx(out=w1_w[a][c][:].bitcast(FP8X4), scales=w1_s[a][c][:], in_=w1_bf[a][c][:])
+
+        def project_candidates(a, hf):
+            cols = slice(hf * BANK, (hf + 1) * BANK)
+            for t in range(PACK):
+                r0 = a * PASS + t * P
+                bank = psum_qo.tile([P, BANK], F32, name="qo")
+                nc.tensor.matmul_mx(
+                    out=bank[:],
+                    lhsT=w2_w[:, 2 * r0 : 2 * (r0 + P)].bitcast(FP4X4),
+                    lhsT_scale=w2_s[:, r0 : r0 + P],
+                    rhs=v2_w[:, cols].bitcast(FP8X4),
+                    rhs_scale=v2_s[:, cols],
+                    start=True,
+                    stop=True,
+                )
+                nc.scalar.activation(out=q_sb[a][hf][:, t, :], in_=bank[:], func=ACT.Copy, scale=gain_sb[:, a, t : t + 1])
+
+        def pair_terms(a, c):
+            j0, width = CHUNKS[c]
+            cols = slice(j0, j0 + width)
+            per_bank = BANK // width
+            q = q_sb[a][j0 // BANK][:, :, j0 % BANK : j0 % BANK + width]
+            diff = ring.tile([P, PACK, width], F32, name="diff", align_bytes=64)
+            dist = ring.tile([P, 2, width, 2], F32, name="dist", align_bytes=64)
+            prod = ring.tile([P, 2, width, 2], F32, name="prod", align_bytes=64)
+            for t0 in range(0, PACK, per_bank):
+                ts = slice(t0, t0 + per_bank)
+                bank = psum_p.tile([P, per_bank, width], F32, name="pp")
+                for t in range(t0, t0 + per_bank):
+                    for k in range(2):
+                        nc.tensor.matmul_mx(
+                            out=bank[:, t - t0, :],
+                            lhsT=w1_w[a][k][:, t * P : (t + 1) * P].bitcast(FP8X4),
+                            lhsT_scale=w1_s[a][k][:, t * P : (t + 1) * P],
+                            rhs=v_w[k][:, cols].bitcast(FP8X4),
+                            rhs_scale=v_s[4 * k :, cols],
+                            start=(k == 0),
+                            stop=(k == 1),
+                        )
+                for t in range(t0, t0 + per_bank):
+                    nc.vector.scalar_tensor_tensor(
+                        out=diff[:, t, :], in0=q[:, t, :], scalar=gain_inv[:, a, t : t + 1], in1=bank[:, t - t0, :], op0=ALU.mult, op1=ALU.subtract
+                    )
+                us = slice(t0 // 2, (t0 + per_bank) // 2)
+                paired = "p (u e) n -> p u n e"
+                nc.scalar.activation(out=dist[:, us, :, :], in_=diff[:, ts, :].rearrange(paired, e=2), func=ACT.Abs)
+                nc.vector.tensor_tensor(out=prod[:, us, :, :], in0=bank[:].rearrange(paired, e=2), in1=q[:, ts, :].rearrange(paired, e=2), op=ALU.mult)
+            return prod, dist
+
+        def pair_feature(c, prod, dist, engine):
+            width = CHUNKS[c][1]
+            h_bf = ring.tile([P, PACK * width], BF16, name="h_bf", align_bytes=64)
+            engine.tensor_tensor(
+                out=h_bf[:].rearrange("p (n u e) -> p n u e", u=2, e=2),
+                in0=prod[:].rearrange("p u n e -> p n u e"),
+                in1=dist[:].rearrange("p u n e -> p n u e"),
+                op=ALU.mult,
+            )
+            return h_bf
+
+        def quantize_h(a, c, h_bf):
+            nc.vector.quantize_mx(out=h_w[a][c][:].bitcast(FP8X4), scales=h_s[a][c][:], in_=h_bf[:])
+
+        def scores(c, last):
+            j0, width = CHUNKS[c]
+            per_bank = 2 if width == 256 else 3
+            for b, n0 in enumerate(range(0, N // P, per_bank)):
+                bank = psum_qo.tile([P, per_bank, width], F32, name="qo")
+                for g in range(per_bank):
+                    ncols = slice((n0 + g) * P, (n0 + g + 1) * P)
+                    for a in range(2):
+                        nc.tensor.matmul_mx(
+                            out=bank[:, g, :],
+                            lhsT=wm_w[:, a, ncols].bitcast(FP8X4),
+                            lhsT_scale=wm_s[:, a, :].bitcast(U8)[:, ncols],
+                            rhs=h_w[a][c][:].bitcast(FP8X4),
+                            rhs_scale=h_s[a][c][:],
+                            start=(a == 0),
+                            stop=(a == 1),
+                        )
+                staged = keep.tile([P, per_bank, width], F32, name="staged%d_%d" % (c, b))
+                if last and b == 1:
+                    nc.vector.tensor_copy(out=staged[:], in_=bank[:])
+                else:
+                    nc.scalar.copy(out=staged[:], in_=bank[:])
+                rows = out[n0 * P : (n0 + per_bank) * P, j0 : j0 + width]
+                nc.sync.dma_start(out=rows.rearrange("(g p) j -> p g j", p=P), in_=staged[:])
+
+        permute_w2()
+        nc.vector.reciprocal(out=gain_recip[:], in_=gain_sb[:])
+        nc.vector.tensor_scalar(out=gain_inv[:], in0=gain_recip[:], scalar1=3.0e38, scalar2=-3.0e38, op0=ALU.min, op1=ALU.max)
+        gather(v2_s, tab2_s, U8, idx2, 0, 512)
+        gather(v2_w, tab2_w, U32, idx2, 0, 512)
+        project_candidates(0, 0)
+        gather(v_s, tab_s, U8, idx, 0, 512)
+        for k in range(2):
+            cast_w1(0, k, True)
+            quantize_w1(0, k)
+        gather(v_w[0], tab_w[0], U32, idx, 0, 256)
+        gather(v_w[1], tab_w[1], U32, idx, 0, 256)
+
+        before = {
+            1: lambda: (gather(v_w[0], tab_w[0], U32, idx, 256, 256), gather(v_w[1], tab_w[1], U32, idx, 256, 256)),
+            2: lambda: (project_candidates(1, 0), cast_w1(1, 0, False), quantize_w1(1, 0), cast_w1(1, 1, False), quantize_w1(1, 1)),
+            4: lambda: (
+                gather(v2_s, tab2_s, U8, idx2, 512, 512),
+                gather(v2_w, tab2_w, U32, idx2, 512, 512),
+                project_candidates(0, 1),
+                gather(v_s, tab_s, U8, idx, 512, 512),
+                gather(v_w[0], tab_w[0], U32, idx, 512, 512),
+                gather(v_w[1], tab_w[1], U32, idx, 512, 512),
+            ),
+            5: lambda: project_candidates(1, 1),
+        }
+
+        pending = None
+        for g, (a, c) in enumerate(GROUPS):
+            if g in before:
+                before[g]()
+            prod, dist = pair_terms(a, c)
+            if pending is not None:
+                quantize_h(*pending)
+                if pending[0] == 1:
+                    scores(pending[1], False)
+            last = g == len(GROUPS) - 1
+            pending = (a, c, pair_feature(c, prod, dist, nc.vector if last else nc.gpsimd))
+        quantize_h(*pending)
+        scores(pending[1], True)

@@ -40,23 +40,23 @@ def tile_list_entity_merge_scores_kernel(
         idx = lists.tile([P, S // LIST_ROWS], U16, name="idx")
         idx2 = lists.tile([P, S // LIST_ROWS], U16, name="idx2")
 
-        tab_w = [keep.tile([P, T], I32, name="tab_w%d" % a, align_bytes=64) for a in range(2)]
+        tab_w = {}
+        w1_raw = {}
         tab_s = keep.tile([P, T // 4], I32, name="tab_s", align_bytes=64)
         tab2_w = keep.tile([P, T2], I32, name="tab2_w", align_bytes=64)
-        tab2_s = keep.tile([P, T2 // 4], I32, name="tab2_s", align_bytes=64)
+        tab2_s = keep.tile([P, T2 // 4], I32, name="tab2_s", tag="slot_b", align_bytes=64)
         v_w = [keep.tile([P, S], U32, name="v_w%d" % a, align_bytes=64) for a in range(2)]
         v_s = keep.tile([P, S], U8, name="v_s", align_bytes=64)
         v2_w = keep.tile([P, S], U32, name="v2_w", align_bytes=64)
         v2_s = keep.tile([P, S], U8, name="v2_s", align_bytes=64)
         w2_raw_w = keep.tile([P, H // 2], I32, name="w2_raw_w", align_bytes=64)
-        w2_raw_s = keep.tile([P, H // 4], I32, name="w2_raw_s", align_bytes=64)
+        w2_raw_s = keep.tile([P, H // 4], I32, name="w2_raw_s", tag="slot_a", align_bytes=64)
         w2_w = keep.tile([P, 2 * H], U8, name="w2_w", align_bytes=64)
         w2_s = keep.tile([P, H], U8, name="w2_s", align_bytes=64)
-        w1_raw = [[keep.tile([P, PACK, PASS], F32, name="w1_raw%d%d" % (a, c), align_bytes=64) for c in range(2)] for a in range(2)]
         w1_bf = [[keep.tile([P, PACK * PASS], BF16, name="w1_bf%d%d" % (a, c), align_bytes=64) for c in range(2)] for a in range(2)]
         w1_w = [[keep.tile([P, PASS], U32, name="w1_w%d%d" % (a, c), align_bytes=64) for c in range(2)] for a in range(2)]
         w1_s = [[keep.tile([P, PASS], U8, name="w1_s%d%d" % (a, c), align_bytes=64) for c in range(2)] for a in range(2)]
-        wm_w = keep.tile([P, 2, N], I32, name="wm_w", align_bytes=64)
+        wm_w = {}
         wm_s = keep.tile([P, 2, N // 4], I32, name="wm_s", align_bytes=64)
         gain_sb = keep.tile([P, 2, PACK], F32, name="gain_sb")
         gain_recip = keep.tile([P, 2, PACK], F32, name="gain_recip")
@@ -65,41 +65,44 @@ def tile_list_entity_merge_scores_kernel(
         h_w = [[keep.tile([P, w], U32, name="h_w%d%d" % (a, c), align_bytes=64) for c, (j0, w) in enumerate(CHUNKS)] for a in range(2)]
         h_s = [[keep.tile([P, w], U8, name="h_s%d%d" % (a, c), align_bytes=64) for c, (j0, w) in enumerate(CHUNKS)] for a in range(2)]
 
-        nc.vector.memset(tab_s[:], 0)
-        nc.vector.memset(tab2_s[:], 0)
         nc.vector.memset(w2_raw_s[:], 0)
+        nc.vector.memset(tab2_s[:], 0)
+        nc.vector.memset(tab_s[:], 0)
         nc.vector.memset(wm_s[:], 0)
 
-        def load_w1(a, c):
-            rows = w1[c * PASS : (c + 1) * PASS, a * PASS : (a + 1) * PASS]
-            nc.sync.dma_start(out=w1_raw[a][c][:], in_=rows.rearrange("(p j) r -> p j r", j=PACK))
+        def load_w1(a, tag):
+            w1_raw[a] = keep.tile([P, 2, PACK, PASS], F32, name="w1_raw%d" % a, tag=tag, align_bytes=64)
+            for c in range(2):
+                rows = w1[c * PASS : (c + 1) * PASS, a * PASS : (a + 1) * PASS]
+                nc.sync.dma_start(out=w1_raw[a][:, c, :, :], in_=rows.rearrange("(p j) r -> p j r", j=PACK))
 
-        def load_tab(c):
+        def load_tab(c, tag):
+            tab_w[c] = keep.tile([P, T], I32, name="tab_w%d" % c, tag=tag, align_bytes=64)
             nc.sync.dma_start(out=tab_w[c][:], in_=tab_words[c].rearrange("p t i -> p (t i)").bitcast(I32))
+
+        def load_wm(tag):
+            wm_w[0] = keep.tile([P, 2, N], I32, name="wm_w", tag=tag, align_bytes=64)
+            nc.sync.dma_start(out=wm_w[0][:], in_=wm_words.rearrange("a p n i -> p a (n i)").bitcast(I32))
 
         nc.sync.dma_start(idx2[:], offs2)
         nc.sync.dma_start(out=w2_raw_w[:], in_=w2_words[0].bitcast(I32))
-        nc.sync.dma_start(out=tab2_w[:], in_=tab2_words[0].rearrange("p t i -> p (t i)").bitcast(I32))
-        for quad in range(4):
-            nc.gpsimd.dma_start(out=tab2_s[32 * quad : 32 * quad + 4, :], in_=tab2_scales[0, 4 * quad : 4 * quad + 4, :].bitcast(I32))
-        for quad in range(4):
-            nc.gpsimd.dma_start(out=w2_raw_s[32 * quad : 32 * quad + 4, :], in_=w2_scales[0, 4 * quad : 4 * quad + 4, :].bitcast(I32))
         nc.sync.dma_start(idx[:], offs)
         nc.sync.dma_start(out=gain_sb[:], in_=gain.rearrange("(a p t) -> p a t", a=2, t=PACK))
-        load_w1(0, 0)
+        load_w1(0, "w1_first")
+        for hf in range(2):
+            cols = slice(hf * T2 // 2, (hf + 1) * T2 // 2)
+            nc.sync.dma_start(out=tab2_w[:, cols], in_=tab2_words[0].rearrange("p t i -> p (t i)").bitcast(I32)[:, cols])
         for quad in range(4):
-            nc.sync.dma_start(out=tab_s[32 * quad : 32 * quad + 8, :], in_=tab_scales[:, 4 * quad : 4 * quad + 4, :].bitcast(I32))
-        load_w1(0, 1)
-        load_tab(0)
-        load_tab(1)
-        load_w1(1, 0)
-        load_w1(1, 1)
+            nc.gpsimd.dma_start(out=w2_raw_s[32 * quad : 32 * quad + 4, :], in_=w2_scales[0, 4 * quad : 4 * quad + 4, :].bitcast(I32))
         for quad in range(4):
-            nc.sync.dma_start(
+            nc.scalar.dma_start(out=tab2_s[32 * quad : 32 * quad + 4, :], in_=tab2_scales[0, 4 * quad : 4 * quad + 4, :].bitcast(I32))
+        for quad in range(4):
+            nc.gpsimd.dma_start(out=tab_s[32 * quad : 32 * quad + 8, :], in_=tab_scales[:, 4 * quad : 4 * quad + 4, :].bitcast(I32))
+        for quad in range(4):
+            nc.gpsimd.dma_start(
                 out=wm_s[32 * quad : 32 * quad + 4, :, :],
                 in_=wm_scales[:, 4 * quad : 4 * quad + 4, :].bitcast(I32).rearrange("a r n -> r a n"),
             )
-        nc.sync.dma_start(out=wm_w[:], in_=wm_words.rearrange("a p n i -> p a (n i)").bitcast(I32))
 
         def gather(dst, window, dtype, offsets, j0, width):
             picked = window[:].bitcast(dtype).indirect(offsets[:, j0 // LIST_ROWS : (j0 + width) // LIST_ROWS])
@@ -115,14 +118,11 @@ def tile_list_entity_merge_scores_kernel(
                 in_=w2_raw_s[:].bitcast(U8).rearrange("p (a m t) -> p a t m", a=2, t=PACK),
             )
 
-        def cast_w1(a, c, on_gpsimd):
-            order = "m t j" if on_gpsimd else "m j t"
-            dst = w1_bf[a][c][:].rearrange("p (t m j) -> p " + order, t=PACK, j=PACK)
-            src = w1_raw[a][c][:].rearrange("p j (m t) -> p " + order, t=PACK)
-            if on_gpsimd:
-                nc.gpsimd.tensor_scalar(out=dst, in0=src, scalar1=1.0, scalar2=0.0, op0=ALU.mult, op1=ALU.add)
-            else:
-                nc.scalar.copy(out=dst, in_=src)
+        def cast_w1(a, c):
+            nc.scalar.copy(
+                out=w1_bf[a][c][:].rearrange("p (t m j) -> p m t j", t=PACK, j=PACK),
+                in_=w1_raw[a][:, c, :, :].rearrange("p j (m t) -> p m t j", t=PACK),
+            )
 
         def quantize_w1(a, c):
             nc.vector.quantize_mx(out=w1_w[a][c][:].bitcast(FP8X4), scales=w1_s[a][c][:], in_=w1_bf[a][c][:])
@@ -199,7 +199,7 @@ def tile_list_entity_merge_scores_kernel(
                     for a in range(2):
                         nc.tensor.matmul_mx(
                             out=bank[:, g, :],
-                            lhsT=wm_w[:, a, ncols].bitcast(FP8X4),
+                            lhsT=wm_w[0][:, a, ncols].bitcast(FP8X4),
                             lhsT_scale=wm_s[:, a, :].bitcast(U8)[:, ncols],
                             rhs=h_w[a][c][:].bitcast(FP8X4),
                             rhs_scale=h_s[a][c][:],
@@ -214,43 +214,42 @@ def tile_list_entity_merge_scores_kernel(
                 rows = out[n0 * P : (n0 + per_bank) * P, j0 : j0 + width]
                 nc.sync.dma_start(out=rows.rearrange("(g p) j -> p g j", p=P), in_=staged[:])
 
-        permute_w2()
         nc.vector.reciprocal(out=gain_recip[:], in_=gain_sb[:])
         nc.vector.tensor_scalar(out=gain_inv[:], in0=gain_recip[:], scalar1=3.0e38, scalar2=-3.0e38, op0=ALU.min, op1=ALU.max)
+        permute_w2()
+        load_tab(0, "slot_a")
         gather(v2_s, tab2_s, U8, idx2, 0, 512)
+        gather(v2_s, tab2_s, U8, idx2, 512, 512)
+        load_tab(1, "slot_b")
         gather(v2_w, tab2_w, U32, idx2, 0, 512)
+        for k in range(2):
+            cast_w1(0, k)
+            quantize_w1(0, k)
         project_candidates(0, 0)
         gather(v_s, tab_s, U8, idx, 0, 512)
-        for k in range(2):
-            cast_w1(0, k, True)
-            quantize_w1(0, k)
-        gather(v_w[0], tab_w[0], U32, idx, 0, 256)
+        gather(v_w[0], tab_w[0], U32, idx, 0, 512)
         gather(v_w[1], tab_w[1], U32, idx, 0, 256)
+        gather(v_w[0], tab_w[0], U32, idx, 512, 512)
+        load_w1(1, "slot_a")
 
         before = {
-            1: lambda: (gather(v_w[0], tab_w[0], U32, idx, 256, 256), gather(v_w[1], tab_w[1], U32, idx, 256, 256)),
-            2: lambda: (project_candidates(1, 0), cast_w1(1, 0, False), quantize_w1(1, 0), cast_w1(1, 1, False), quantize_w1(1, 1)),
-            4: lambda: (
-                gather(v2_s, tab2_s, U8, idx2, 512, 512),
-                gather(v2_w, tab2_w, U32, idx2, 512, 512),
-                project_candidates(0, 1),
-                gather(v_s, tab_s, U8, idx, 512, 512),
-                gather(v_w[0], tab_w[0], U32, idx, 512, 512),
-                gather(v_w[1], tab_w[1], U32, idx, 512, 512),
-            ),
+            1: lambda: (gather(v_w[1], tab_w[1], U32, idx, 256, 256), gather(v_w[1], tab_w[1], U32, idx, 512, 512), load_wm("slot_b")),
+            2: lambda: (project_candidates(1, 0), cast_w1(1, 0), quantize_w1(1, 0), cast_w1(1, 1), quantize_w1(1, 1)),
+            4: lambda: (gather(v2_w, tab2_w, U32, idx2, 512, 512), project_candidates(0, 1), gather(v_s, tab_s, U8, idx, 512, 512)),
             5: lambda: project_candidates(1, 1),
         }
 
-        pending = None
-        for g, (a, c) in enumerate(GROUPS):
+        terms = {}
+        feats = {}
+        for g in range(len(GROUPS) + 2):
             if g in before:
                 before[g]()
-            prod, dist = pair_terms(a, c)
-            if pending is not None:
-                quantize_h(*pending)
-                if pending[0] == 1:
-                    scores(pending[1], False)
-            last = g == len(GROUPS) - 1
-            pending = (a, c, pair_feature(c, prod, dist, nc.vector if last else nc.gpsimd))
-        quantize_h(*pending)
-        scores(pending[1], True)
+            if g < len(GROUPS):
+                terms[g] = pair_terms(*GROUPS[g])
+            if 2 <= g:
+                a, c = GROUPS[g - 2]
+                quantize_h(a, c, feats[g - 2])
+            if 1 <= g <= len(GROUPS):
+                feats[g - 1] = pair_feature(GROUPS[g - 1][1], terms[g - 1][0], terms[g - 1][1], nc.vector)
+            if 2 <= g and GROUPS[g - 2][0] == 1:
+                scores(GROUPS[g - 2][1], g == len(GROUPS) + 1)

@@ -20,10 +20,12 @@ P = 128
 PACK = 4
 PASS = P * PACK
 BANK = 512
-LIST_ROWS = 16
+PER_COLUMN = 16
+QUADS = 4
+BIG = 3.0e38
 
 CHUNKS = [(0, 256), (256, 256), (512, 256), (768, 128), (896, 128)]
-GROUPS = [(0, 0), (0, 1), (1, 0), (1, 1), (0, 2), (1, 2), (0, 3), (1, 3), (0, 4), (1, 4)]
+STEPS = [(0, 0), (0, 1), (1, 0), (1, 1), (0, 2), (1, 2), (0, 3), (1, 3), (0, 4), (1, 4)]
 
 
 def tile_list_entity_merge_scores_kernel(
@@ -37,98 +39,71 @@ def tile_list_entity_merge_scores_kernel(
         psum_p = ctx.enter_context(tc.psum_pool(name="psum_p", bufs=4))
         psum_qo = ctx.enter_context(tc.psum_pool(name="psum_qo", bufs=4))
 
-        idx = lists.tile([P, S // LIST_ROWS], U16, name="idx")
-        idx2 = lists.tile([P, S // LIST_ROWS], U16, name="idx2")
+        def held(name, shape, dtype, slot=None):
+            return keep.tile(shape, dtype, name=name, tag=slot or name, align_bytes=64)
 
-        tab_w = {}
-        w1_raw = {}
-        tab_s = keep.tile([P, T // 4], I32, name="tab_s", align_bytes=64)
-        tab2_w = keep.tile([P, T2], I32, name="tab2_w", align_bytes=64)
-        tab2_s = keep.tile([P, T2 // 4], I32, name="tab2_s", tag="slot_b", align_bytes=64)
-        v_w = [keep.tile([P, S], U32, name="v_w%d" % a, align_bytes=64) for a in range(2)]
-        v_s = keep.tile([P, S], U8, name="v_s", align_bytes=64)
-        v2_w = keep.tile([P, S], U32, name="v2_w", align_bytes=64)
-        v2_s = keep.tile([P, S], U8, name="v2_s", align_bytes=64)
-        w2_raw_w = keep.tile([P, H // 2], I32, name="w2_raw_w", align_bytes=64)
-        w2_raw_s = keep.tile([P, H // 4], I32, name="w2_raw_s", tag="slot_a", align_bytes=64)
-        w2_w = keep.tile([P, 2 * H], U8, name="w2_w", align_bytes=64)
-        w2_s = keep.tile([P, H], U8, name="w2_s", align_bytes=64)
-        w1_bf = [[keep.tile([P, PACK * PASS], BF16, name="w1_bf%d%d" % (a, c), align_bytes=64) for c in range(2)] for a in range(2)]
-        w1_w = [[keep.tile([P, PASS], U32, name="w1_w%d%d" % (a, c), align_bytes=64) for c in range(2)] for a in range(2)]
-        w1_s = [[keep.tile([P, PASS], U8, name="w1_s%d%d" % (a, c), align_bytes=64) for c in range(2)] for a in range(2)]
-        wm_w = {}
-        wm_s = keep.tile([P, 2, N // 4], I32, name="wm_s", align_bytes=64)
-        gain_sb = keep.tile([P, 2, PACK], F32, name="gain_sb")
-        gain_recip = keep.tile([P, 2, PACK], F32, name="gain_recip")
-        gain_inv = keep.tile([P, 2, PACK], F32, name="gain_inv")
-        q_sb = [[keep.tile([P, PACK, BANK], F32, name="q_sb%d%d" % (a, hf), align_bytes=64) for hf in range(2)] for a in range(2)]
-        h_w = [[keep.tile([P, w], U32, name="h_w%d%d" % (a, c), align_bytes=64) for c, (j0, w) in enumerate(CHUNKS)] for a in range(2)]
-        h_s = [[keep.tile([P, w], U8, name="h_s%d%d" % (a, c), align_bytes=64) for c, (j0, w) in enumerate(CHUNKS)] for a in range(2)]
+        idx = lists.tile([P, S // PER_COLUMN], U16, name="idx")
+        idx2 = lists.tile([P, S // PER_COLUMN], U16, name="idx2")
 
-        nc.vector.memset(w2_raw_s[:], 0)
-        nc.vector.memset(tab2_s[:], 0)
-        nc.vector.memset(tab_s[:], 0)
-        nc.vector.memset(wm_s[:], 0)
+        tab_s = held("tab_s", [P, T // 4], I32, "slot_b")
+        tab2_s = held("tab2_s", [P, T2 // 4], I32)
+        v_w = [held("v_w%d" % k, [P, S], U32) for k in range(2)]
+        v_s = held("v_s", [P, S], U8)
+        v2_w = held("v2_w", [P, S], U32)
+        v2_s = held("v2_s", [P, S], U8)
+        w2_raw_w = held("w2_raw_w", [P, H // 2], I32, "slot_a")
+        w2_raw_s = held("w2_raw_s", [P, H // 4], I32)
+        w2_w = held("w2_w", [P, 2 * H], U8)
+        w2_s = held("w2_s", [P, H], U8)
+        w1_bf = [[held("w1_bf%d%d" % (a, k), [P, PACK * PASS], BF16) for k in range(2)] for a in range(2)]
+        w1_w = [[held("w1_w%d%d" % (a, k), [P, PASS], U32) for k in range(2)] for a in range(2)]
+        w1_s = [[held("w1_s%d%d" % (a, k), [P, PASS], U8) for k in range(2)] for a in range(2)]
+        wm_s = held("wm_s", [P, 2, N // 4], I32)
+        gain_sb = held("gain_sb", [P, 2, PACK], F32)
+        gain_recip = held("gain_recip", [P, 2, PACK], F32, "slot_c")
+        gain_inv = held("gain_inv", [P, 2, PACK], F32)
+        gq = [[held("gq%d%d" % (a, half), [P, PACK, BANK], F32) for half in range(2)] for a in range(2)]
+        h_w = [[held("h_w%d%d" % (a, c), [P, width], U32) for c, (j0, width) in enumerate(CHUNKS)] for a in range(2)]
+        h_s = [[held("h_s%d%d" % (a, c), [P, width], U8) for c, (j0, width) in enumerate(CHUNKS)] for a in range(2)]
+        late = {}
 
-        def load_w1(a, tag):
-            w1_raw[a] = keep.tile([P, 2, PACK, PASS], F32, name="w1_raw%d" % a, tag=tag, align_bytes=64)
-            for c in range(2):
-                rows = w1[c * PASS : (c + 1) * PASS, a * PASS : (a + 1) * PASS]
-                nc.sync.dma_start(out=w1_raw[a][:, c, :, :], in_=rows.rearrange("(p j) r -> p j r", j=PACK))
+        def load_scales(tile, rows, source):
+            for quad in range(QUADS):
+                nc.sync.dma_start(out=tile[32 * quad : 32 * quad + rows], in_=source(slice(4 * quad, 4 * quad + 4)))
 
-        def load_tab(c, tag):
-            tab_w[c] = keep.tile([P, T], I32, name="tab_w%d" % c, tag=tag, align_bytes=64)
-            nc.sync.dma_start(out=tab_w[c][:], in_=tab_words[c].rearrange("p t i -> p (t i)").bitcast(I32))
+        def load_tab(k, slot):
+            late["tab", k] = held("tab_w%d" % k, [P, T], I32, slot)
+            nc.sync.dma_start(out=late["tab", k][:], in_=tab_words[k].rearrange("p t i -> p (t i)").bitcast(I32))
 
-        def load_wm(tag):
-            wm_w[0] = keep.tile([P, 2, N], I32, name="wm_w", tag=tag, align_bytes=64)
-            nc.sync.dma_start(out=wm_w[0][:], in_=wm_words.rearrange("a p n i -> p a (n i)").bitcast(I32))
+        def load_w1(a, k):
+            if k == 0:
+                late["w1", a] = held("w1_raw%d" % a, [P, 2, PACK, PASS], F32, "slot_c")
+            rows = w1[k * PASS : (k + 1) * PASS, a * PASS : (a + 1) * PASS]
+            nc.sync.dma_start(out=late["w1", a][:, k, :, :], in_=rows.rearrange("(p j) r -> p j r", j=PACK))
 
-        nc.sync.dma_start(idx2[:], offs2)
-        nc.sync.dma_start(out=w2_raw_w[:], in_=w2_words[0].bitcast(I32))
-        nc.sync.dma_start(idx[:], offs)
-        nc.sync.dma_start(out=gain_sb[:], in_=gain.rearrange("(a p t) -> p a t", a=2, t=PACK))
-        load_w1(0, "w1_first")
-        for hf in range(2):
-            cols = slice(hf * T2 // 2, (hf + 1) * T2 // 2)
-            nc.sync.dma_start(out=tab2_w[:, cols], in_=tab2_words[0].rearrange("p t i -> p (t i)").bitcast(I32)[:, cols])
-        for quad in range(4):
-            nc.gpsimd.dma_start(out=w2_raw_s[32 * quad : 32 * quad + 4, :], in_=w2_scales[0, 4 * quad : 4 * quad + 4, :].bitcast(I32))
-        for quad in range(4):
-            nc.scalar.dma_start(out=tab2_s[32 * quad : 32 * quad + 4, :], in_=tab2_scales[0, 4 * quad : 4 * quad + 4, :].bitcast(I32))
-        for quad in range(4):
-            nc.gpsimd.dma_start(out=tab_s[32 * quad : 32 * quad + 8, :], in_=tab_scales[:, 4 * quad : 4 * quad + 4, :].bitcast(I32))
-        for quad in range(4):
-            nc.gpsimd.dma_start(
-                out=wm_s[32 * quad : 32 * quad + 4, :, :],
-                in_=wm_scales[:, 4 * quad : 4 * quad + 4, :].bitcast(I32).rearrange("a r n -> r a n"),
-            )
+        def load_wm():
+            late["wm"] = held("wm_w", [P, 2, N], I32, "slot_a")
+            nc.sync.dma_start(out=late["wm"][:], in_=wm_words.rearrange("a p n i -> p a (n i)").bitcast(I32))
 
-        def gather(dst, window, dtype, offsets, j0, width):
-            picked = window[:].bitcast(dtype).indirect(offsets[:, j0 // LIST_ROWS : (j0 + width) // LIST_ROWS])
-            nc.vector.tensor_copy(out=dst[:, j0 : j0 + width], in_=picked)
+        def gather(picked, table, dtype, offsets, j0, width):
+            window = table[:].bitcast(dtype).indirect(offsets[:, j0 // PER_COLUMN : (j0 + width) // PER_COLUMN])
+            nc.vector.tensor_copy(out=picked[:, j0 : j0 + width], in_=window)
 
-        def permute_w2():
+        def reorder_w2(ordered, loaded):
             nc.vector.tensor_copy(
-                out=w2_w[:].bitcast(U16).rearrange("p (a t m) -> p a t m", a=2, t=PACK),
-                in_=w2_raw_w[:].bitcast(U16).rearrange("p (a m t) -> p a t m", a=2, t=PACK),
-            )
-            nc.vector.tensor_copy(
-                out=w2_s[:].rearrange("p (a t m) -> p a t m", a=2, t=PACK),
-                in_=w2_raw_s[:].bitcast(U8).rearrange("p (a m t) -> p a t m", a=2, t=PACK),
+                out=ordered.rearrange("p (a t m) -> p a t m", a=2, t=PACK),
+                in_=loaded.rearrange("p (a m t) -> p a t m", a=2, t=PACK),
             )
 
-        def cast_w1(a, c):
+        def quantize_w1(a, k):
             nc.scalar.copy(
-                out=w1_bf[a][c][:].rearrange("p (t m j) -> p m t j", t=PACK, j=PACK),
-                in_=w1_raw[a][:, c, :, :].rearrange("p j (m t) -> p m t j", t=PACK),
+                out=w1_bf[a][k][:].rearrange("p (t m j) -> p m t j", t=PACK, j=PACK),
+                in_=late["w1", a][:, k, :, :].rearrange("p j (m t) -> p m t j", t=PACK),
             )
+            nc.vector.quantize_mx(out=w1_w[a][k][:].bitcast(FP8X4), scales=w1_s[a][k][:], in_=w1_bf[a][k][:])
 
-        def quantize_w1(a, c):
-            nc.vector.quantize_mx(out=w1_w[a][c][:].bitcast(FP8X4), scales=w1_s[a][c][:], in_=w1_bf[a][c][:])
-
-        def project_candidates(a, hf):
-            cols = slice(hf * BANK, (hf + 1) * BANK)
+        def project_candidates(a, half):
+            cols = slice(half * BANK, (half + 1) * BANK)
             for t in range(PACK):
                 r0 = a * PASS + t * P
                 bank = psum_qo.tile([P, BANK], F32, name="qo")
@@ -141,18 +116,20 @@ def tile_list_entity_merge_scores_kernel(
                     start=True,
                     stop=True,
                 )
-                nc.scalar.activation(out=q_sb[a][hf][:, t, :], in_=bank[:], func=ACT.Copy, scale=gain_sb[:, a, t : t + 1])
+                nc.scalar.activation(out=gq[a][half][:, t, :], in_=bank[:], func=ACT.Copy, scale=gain_sb[:, a, t : t + 1])
 
         def pair_terms(a, c):
             j0, width = CHUNKS[c]
             cols = slice(j0, j0 + width)
             per_bank = BANK // width
-            q = q_sb[a][j0 // BANK][:, :, j0 % BANK : j0 % BANK + width]
+            gq_chunk = gq[a][j0 // BANK][:, :, j0 % BANK : j0 % BANK + width]
             diff = ring.tile([P, PACK, width], F32, name="diff", align_bytes=64)
             dist = ring.tile([P, 2, width, 2], F32, name="dist", align_bytes=64)
             prod = ring.tile([P, 2, width, 2], F32, name="prod", align_bytes=64)
+            in_pairs = "p (u e) n -> p u n e"
             for t0 in range(0, PACK, per_bank):
-                ts = slice(t0, t0 + per_bank)
+                planes = slice(t0, t0 + per_bank)
+                pairs = slice(t0 // 2, (t0 + per_bank) // 2)
                 bank = psum_p.tile([P, per_bank, width], F32, name="pp")
                 for t in range(t0, t0 + per_bank):
                     for k in range(2):
@@ -167,18 +144,25 @@ def tile_list_entity_merge_scores_kernel(
                         )
                 for t in range(t0, t0 + per_bank):
                     nc.vector.scalar_tensor_tensor(
-                        out=diff[:, t, :], in0=q[:, t, :], scalar=gain_inv[:, a, t : t + 1], in1=bank[:, t - t0, :], op0=ALU.mult, op1=ALU.subtract
+                        out=diff[:, t, :],
+                        in0=gq_chunk[:, t, :],
+                        scalar=gain_inv[:, a, t : t + 1],
+                        in1=bank[:, t - t0, :],
+                        op0=ALU.mult,
+                        op1=ALU.subtract,
                     )
-                us = slice(t0 // 2, (t0 + per_bank) // 2)
-                paired = "p (u e) n -> p u n e"
-                nc.scalar.activation(out=dist[:, us, :, :], in_=diff[:, ts, :].rearrange(paired, e=2), func=ACT.Abs)
-                nc.vector.tensor_tensor(out=prod[:, us, :, :], in0=bank[:].rearrange(paired, e=2), in1=q[:, ts, :].rearrange(paired, e=2), op=ALU.mult)
+                nc.scalar.activation(out=dist[:, pairs, :, :], in_=diff[:, planes, :].rearrange(in_pairs, e=2), func=ACT.Abs)
+                nc.vector.tensor_tensor(
+                    out=prod[:, pairs, :, :],
+                    in0=bank[:].rearrange(in_pairs, e=2),
+                    in1=gq_chunk[:, planes, :].rearrange(in_pairs, e=2),
+                    op=ALU.mult,
+                )
             return prod, dist
 
-        def pair_feature(c, prod, dist, engine):
-            width = CHUNKS[c][1]
-            h_bf = ring.tile([P, PACK * width], BF16, name="h_bf", align_bytes=64)
-            engine.tensor_tensor(
+        def pair_feature(c, prod, dist):
+            h_bf = ring.tile([P, PACK * CHUNKS[c][1]], BF16, name="h_bf", align_bytes=64)
+            nc.vector.tensor_tensor(
                 out=h_bf[:].rearrange("p (n u e) -> p n u e", u=2, e=2),
                 in0=prod[:].rearrange("p u n e -> p n u e"),
                 in1=dist[:].rearrange("p u n e -> p n u e"),
@@ -186,10 +170,7 @@ def tile_list_entity_merge_scores_kernel(
             )
             return h_bf
 
-        def quantize_h(a, c, h_bf):
-            nc.vector.quantize_mx(out=h_w[a][c][:].bitcast(FP8X4), scales=h_s[a][c][:], in_=h_bf[:])
-
-        def scores(c, last):
+        def scores(c):
             j0, width = CHUNKS[c]
             per_bank = 2 if width == 256 else 3
             for b, n0 in enumerate(range(0, N // P, per_bank)):
@@ -199,57 +180,81 @@ def tile_list_entity_merge_scores_kernel(
                     for a in range(2):
                         nc.tensor.matmul_mx(
                             out=bank[:, g, :],
-                            lhsT=wm_w[0][:, a, ncols].bitcast(FP8X4),
+                            lhsT=late["wm"][:, a, ncols].bitcast(FP8X4),
                             lhsT_scale=wm_s[:, a, :].bitcast(U8)[:, ncols],
                             rhs=h_w[a][c][:].bitcast(FP8X4),
                             rhs_scale=h_s[a][c][:],
                             start=(a == 0),
                             stop=(a == 1),
                         )
-                staged = keep.tile([P, per_bank, width], F32, name="staged%d_%d" % (c, b))
-                if last and b == 1:
+                staged = held("staged%d_%d" % (c, b), [P, per_bank, width], F32)
+                if c == len(CHUNKS) - 1 and b == 1:
                     nc.vector.tensor_copy(out=staged[:], in_=bank[:])
                 else:
                     nc.scalar.copy(out=staged[:], in_=bank[:])
                 rows = out[n0 * P : (n0 + per_bank) * P, j0 : j0 + width]
                 nc.sync.dma_start(out=rows.rearrange("(g p) j -> p g j", p=P), in_=staged[:])
 
-        nc.vector.reciprocal(out=gain_recip[:], in_=gain_sb[:])
-        nc.vector.tensor_scalar(out=gain_inv[:], in0=gain_recip[:], scalar1=3.0e38, scalar2=-3.0e38, op0=ALU.min, op1=ALU.max)
-        permute_w2()
-        load_tab(0, "slot_a")
-        gather(v2_s, tab2_s, U8, idx2, 0, 512)
-        gather(v2_s, tab2_s, U8, idx2, 512, 512)
-        load_tab(1, "slot_b")
-        gather(v2_w, tab2_w, U32, idx2, 0, 512)
-        for k in range(2):
-            cast_w1(0, k)
-            quantize_w1(0, k)
-        project_candidates(0, 0)
-        gather(v_s, tab_s, U8, idx, 0, 512)
-        gather(v_w[0], tab_w[0], U32, idx, 0, 512)
-        gather(v_w[1], tab_w[1], U32, idx, 0, 256)
-        gather(v_w[0], tab_w[0], U32, idx, 512, 512)
-        load_w1(1, "slot_a")
+        for tile in (tab_s, tab2_s, w2_raw_s, wm_s):
+            nc.vector.memset(tile[:], 0)
 
-        before = {
-            1: lambda: (gather(v_w[1], tab_w[1], U32, idx, 256, 256), gather(v_w[1], tab_w[1], U32, idx, 512, 512), load_wm("slot_b")),
-            2: lambda: (project_candidates(1, 0), cast_w1(1, 0), quantize_w1(1, 0), cast_w1(1, 1), quantize_w1(1, 1)),
-            4: lambda: (gather(v2_w, tab2_w, U32, idx2, 512, 512), project_candidates(0, 1), gather(v_s, tab_s, U8, idx, 512, 512)),
-            5: lambda: project_candidates(1, 1),
-        }
+        nc.sync.dma_start(out=gain_sb[:], in_=gain.rearrange("(a p t) -> p a t", a=2, t=PACK))
+        nc.sync.dma_start(idx[:], offs)
+        nc.sync.dma_start(out=w2_raw_w[:], in_=w2_words[0].bitcast(I32))
+        nc.sync.dma_start(idx2[:], offs2)
+        load_tab(0, None)
+        load_scales(tab_s, 8, lambda rows: tab_scales[:, rows, :].bitcast(I32))
+        nc.vector.reciprocal(out=gain_recip[:], in_=gain_sb[:])
+        nc.vector.tensor_scalar(out=gain_inv[:], in0=gain_recip[:], scalar1=BIG, scalar2=-BIG, op0=ALU.min, op1=ALU.max)
+        load_w1(0, 0)
+        load_scales(tab2_s, 4, lambda rows: tab2_scales[0, rows, :].bitcast(I32))
+        load_w1(0, 1)
+        load_scales(w2_raw_s, 4, lambda rows: w2_scales[0, rows, :].bitcast(I32))
+        reorder_w2(w2_w[:].bitcast(U16), w2_raw_w[:].bitcast(U16))
+        tab2_w = held("tab2_w", [P, T2], I32, "slot_a")
+        for half in range(2):
+            cols = slice(half * T2 // 2, (half + 1) * T2 // 2)
+            nc.sync.dma_start(out=tab2_w[:, cols], in_=tab2_words[0].rearrange("p t i -> p (t i)").bitcast(I32)[:, cols])
+
+        gather(v_s, tab_s, U8, idx, 0, S)
+        load_tab(1, "slot_b")
+        gather(v_w[0], late["tab", 0], U32, idx, 0, S)
+        gather(v2_s, tab2_s, U8, idx2, 0, S)
+        reorder_w2(w2_s[:], w2_raw_s[:].bitcast(U8))
+        gather(v2_w, tab2_w, U32, idx2, 0, BANK)
+        for k in range(2):
+            quantize_w1(0, k)
+        for k in range(2):
+            load_w1(1, k)
+        load_scales(wm_s, 4, lambda rows: wm_scales[:, rows, :].bitcast(I32).rearrange("a r n -> r a n"))
+        project_candidates(0, 0)
+        gather(v_w[1], late["tab", 1], U32, idx, *CHUNKS[0])
+
+        def prepare(g):
+            if g == 1:
+                gather(v_w[1], late["tab", 1], U32, idx, *CHUNKS[1])
+                gather(v2_w, tab2_w, U32, idx2, BANK, BANK)
+                load_wm()
+            if g == 2:
+                project_candidates(1, 0)
+                for k in range(2):
+                    quantize_w1(1, k)
+            if g == 4:
+                project_candidates(0, 1)
+                gather(v_w[1], late["tab", 1], U32, idx, BANK, BANK)
+            if g == 5:
+                project_candidates(1, 1)
 
         terms = {}
-        feats = {}
-        for g in range(len(GROUPS) + 2):
-            if g in before:
-                before[g]()
-            if g < len(GROUPS):
-                terms[g] = pair_terms(*GROUPS[g])
-            if 2 <= g:
-                a, c = GROUPS[g - 2]
-                quantize_h(a, c, feats[g - 2])
-            if 1 <= g <= len(GROUPS):
-                feats[g - 1] = pair_feature(GROUPS[g - 1][1], terms[g - 1][0], terms[g - 1][1], nc.vector)
-            if 2 <= g and GROUPS[g - 2][0] == 1:
-                scores(GROUPS[g - 2][1], g == len(GROUPS) + 1)
+        features = {}
+        for g in range(len(STEPS) + 2):
+            prepare(g)
+            if g < len(STEPS):
+                terms[g] = pair_terms(*STEPS[g])
+            if g >= 2:
+                a, c = STEPS[g - 2]
+                nc.vector.quantize_mx(out=h_w[a][c][:].bitcast(FP8X4), scales=h_s[a][c][:], in_=features[g - 2][:])
+            if 1 <= g <= len(STEPS):
+                features[g - 1] = pair_feature(STEPS[g - 1][1], *terms[g - 1])
+            if g >= 2 and STEPS[g - 2][0] == 1:
+                scores(STEPS[g - 2][1])

@@ -24,8 +24,8 @@ PER_COLUMN = 16
 QUADS = 4
 BIG = 3.0e38
 
-CHUNKS = [(0, 256), (256, 256), (512, 256), (768, 128), (896, 128)]
-STEPS = [(0, 0), (0, 1), (1, 0), (1, 1), (0, 2), (1, 2), (0, 3), (1, 3), (0, 4), (1, 4)]
+STEP = 256
+NARROW = 128
 
 
 def tile_list_entity_merge_scores_kernel(
@@ -45,45 +45,42 @@ def tile_list_entity_merge_scores_kernel(
         idx = lists.tile([P, S // PER_COLUMN], U16, name="idx")
         idx2 = lists.tile([P, S // PER_COLUMN], U16, name="idx2")
 
-        tab_s = held("tab_s", [P, T // 4], I32, "slot_b")
-        tab2_s = held("tab2_s", [P, T2 // 4], I32)
+        tab2_s = held("tab2_s", [P, T2 // 4], I32, "slot_d")
         v_w = [held("v_w%d" % k, [P, S], U32) for k in range(2)]
         v_s = held("v_s", [P, S], U8)
         v2_w = held("v2_w", [P, S], U32)
         v2_s = held("v2_s", [P, S], U8)
-        w2_raw_w = held("w2_raw_w", [P, H // 2], I32, "slot_a")
+        w2_raw_w = held("w2_raw_w", [P, H // 2], I32, "slot_b")
         w2_raw_s = held("w2_raw_s", [P, H // 4], I32)
         w2_w = held("w2_w", [P, 2 * H], U8)
         w2_s = held("w2_s", [P, H], U8)
         w1_bf = [[held("w1_bf%d%d" % (a, k), [P, PACK * PASS], BF16) for k in range(2)] for a in range(2)]
         w1_w = [[held("w1_w%d%d" % (a, k), [P, PASS], U32) for k in range(2)] for a in range(2)]
-        w1_s = [[held("w1_s%d%d" % (a, k), [P, PASS], U8) for k in range(2)] for a in range(2)]
-        wm_s = held("wm_s", [P, 2, N // 4], I32)
+        h_w = [held("h_w%d" % a, [P, S], U32) for a in range(2)]
+        h_s = [[held("h_s%d%d" % (a, half), [P, BANK], U8) for half in range(2)] for a in range(2)]
+        w1_s = [[held("w1_s0%d" % k, [P, PASS], U8)[:] for k in range(2)], [h_s[0][0][4:, :], h_s[0][0][8:, :]]]
         gain_sb = held("gain_sb", [P, 2, PACK], F32)
         gain_recip = held("gain_recip", [P, 2, PACK], F32, "slot_c")
         gain_inv = held("gain_inv", [P, 2, PACK], F32)
         gq = [[held("gq%d%d" % (a, half), [P, PACK, BANK], F32) for half in range(2)] for a in range(2)]
-        h_w = [[held("h_w%d%d" % (a, c), [P, width], U32) for c, (j0, width) in enumerate(CHUNKS)] for a in range(2)]
-        h_s = [[held("h_s%d%d" % (a, c), [P, width], U8) for c, (j0, width) in enumerate(CHUNKS)] for a in range(2)]
         late = {}
 
-        def load_scales(tile, rows, source):
+        def load_rows_by_quadrant(tile, source):
             for quad in range(QUADS):
-                nc.sync.dma_start(out=tile[32 * quad : 32 * quad + rows], in_=source(slice(4 * quad, 4 * quad + 4)))
+                nc.sync.dma_start(out=tile[32 * quad : 32 * quad + 8], in_=source[:, 4 * quad : 4 * quad + 4, :].bitcast(I32))
+
+        def load_rows_by_place(tile, source):
+            for r in range(4):
+                nc.sync.dma_start(out=tile[r:P:32], in_=source[0, r:16:4, :].bitcast(I32))
 
         def load_tab(k, slot):
             late["tab", k] = held("tab_w%d" % k, [P, T], I32, slot)
             nc.sync.dma_start(out=late["tab", k][:], in_=tab_words[k].rearrange("p t i -> p (t i)").bitcast(I32))
 
         def load_w1(a, k):
-            if k == 0:
-                late["w1", a] = held("w1_raw%d" % a, [P, 2, PACK, PASS], F32, "slot_c")
+            late["w1", a, k] = held("w1_raw%d%d" % (a, k), [P, PACK, PASS], F32, ("slot_c", "slot_d")[k])
             rows = w1[k * PASS : (k + 1) * PASS, a * PASS : (a + 1) * PASS]
-            nc.sync.dma_start(out=late["w1", a][:, k, :, :], in_=rows.rearrange("(p j) r -> p j r", j=PACK))
-
-        def load_wm():
-            late["wm"] = held("wm_w", [P, 2, N], I32, "slot_a")
-            nc.sync.dma_start(out=late["wm"][:], in_=wm_words.rearrange("a p n i -> p a (n i)").bitcast(I32))
+            nc.sync.dma_start(out=late["w1", a, k][:], in_=rows.rearrange("(p j) r -> p j r", j=PACK))
 
         def gather(picked, table, dtype, offsets, j0, width):
             window = table[:].bitcast(dtype).indirect(offsets[:, j0 // PER_COLUMN : (j0 + width) // PER_COLUMN])
@@ -95,12 +92,14 @@ def tile_list_entity_merge_scores_kernel(
                 in_=loaded.rearrange("p (a m t) -> p a t m", a=2, t=PACK),
             )
 
+        def round_w1(a, k, copy, pieces):
+            rounded = w1_bf[a][k][:].rearrange("p (t m j) -> p m t j", t=PACK, j=PACK)
+            loaded = late["w1", a, k][:].rearrange("p j (m t) -> p m t j", t=PACK)
+            for m0 in range(0, P, P // pieces):
+                copy(out=rounded[:, m0 : m0 + P // pieces], in_=loaded[:, m0 : m0 + P // pieces])
+
         def quantize_w1(a, k):
-            nc.scalar.copy(
-                out=w1_bf[a][k][:].rearrange("p (t m j) -> p m t j", t=PACK, j=PACK),
-                in_=late["w1", a][:, k, :, :].rearrange("p j (m t) -> p m t j", t=PACK),
-            )
-            nc.vector.quantize_mx(out=w1_w[a][k][:].bitcast(FP8X4), scales=w1_s[a][k][:], in_=w1_bf[a][k][:])
+            nc.vector.quantize_mx(out=w1_w[a][k][:].bitcast(FP8X4), scales=w1_s[a][k], in_=w1_bf[a][k][:])
 
         def project_candidates(a, half):
             cols = slice(half * BANK, (half + 1) * BANK)
@@ -118,8 +117,7 @@ def tile_list_entity_merge_scores_kernel(
                 )
                 nc.scalar.activation(out=gq[a][half][:, t, :], in_=bank[:], func=ACT.Copy, scale=gain_sb[:, a, t : t + 1])
 
-        def pair_terms(a, c):
-            j0, width = CHUNKS[c]
+        def pair_terms(a, j0, width):
             cols = slice(j0, j0 + width)
             per_bank = BANK // width
             gq_chunk = gq[a][j0 // BANK][:, :, j0 % BANK : j0 % BANK + width]
@@ -127,10 +125,12 @@ def tile_list_entity_merge_scores_kernel(
             dist = ring.tile([P, 2, width, 2], F32, name="dist", align_bytes=64)
             prod = ring.tile([P, 2, width, 2], F32, name="prod", align_bytes=64)
             in_pairs = "p (u e) n -> p u n e"
+            banks = []
             for t0 in range(0, PACK, per_bank):
                 planes = slice(t0, t0 + per_bank)
                 pairs = slice(t0 // 2, (t0 + per_bank) // 2)
                 bank = psum_p.tile([P, per_bank, width], F32, name="pp")
+                banks.append((bank, planes, pairs))
                 for t in range(t0, t0 + per_bank):
                     for k in range(2):
                         nc.tensor.matmul_mx(
@@ -152,6 +152,7 @@ def tile_list_entity_merge_scores_kernel(
                         op1=ALU.subtract,
                     )
                 nc.scalar.activation(out=dist[:, pairs, :, :], in_=diff[:, planes, :].rearrange(in_pairs, e=2), func=ACT.Abs)
+            for bank, planes, pairs in banks:
                 nc.vector.tensor_tensor(
                     out=prod[:, pairs, :, :],
                     in0=bank[:].rearrange(in_pairs, e=2),
@@ -160,101 +161,146 @@ def tile_list_entity_merge_scores_kernel(
                 )
             return prod, dist
 
-        def pair_feature(c, prod, dist):
-            h_bf = ring.tile([P, PACK * CHUNKS[c][1]], BF16, name="h_bf", align_bytes=64)
-            nc.vector.tensor_tensor(
-                out=h_bf[:].rearrange("p (n u e) -> p n u e", u=2, e=2),
+        def pair_feature(engine, h_bf, terms):
+            prod, dist = terms
+            engine.tensor_tensor(
+                out=h_bf.rearrange("p (n u e) -> p n u e", u=2, e=2),
                 in0=prod[:].rearrange("p u n e -> p n u e"),
                 in1=dist[:].rearrange("p u n e -> p n u e"),
                 op=ALU.mult,
             )
-            return h_bf
 
-        def scores(c):
-            j0, width = CHUNKS[c]
-            per_bank = 2 if width == 256 else 3
-            for b, n0 in enumerate(range(0, N // P, per_bank)):
-                bank = psum_qo.tile([P, per_bank, width], F32, name="qo")
-                for g in range(per_bank):
-                    ncols = slice((n0 + g) * P, (n0 + g + 1) * P)
-                    for a in range(2):
-                        nc.tensor.matmul_mx(
-                            out=bank[:, g, :],
-                            lhsT=late["wm"][:, a, ncols].bitcast(FP8X4),
-                            lhsT_scale=wm_s[:, a, :].bitcast(U8)[:, ncols],
-                            rhs=h_w[a][c][:].bitcast(FP8X4),
-                            rhs_scale=h_s[a][c][:],
-                            start=(a == 0),
-                            stop=(a == 1),
-                        )
-                staged = held("staged%d_%d" % (c, b), [P, per_bank, width], F32)
-                if c == len(CHUNKS) - 1 and b == 1:
-                    nc.vector.tensor_copy(out=staged[:], in_=bank[:])
-                else:
-                    nc.scalar.copy(out=staged[:], in_=bank[:])
-                rows = out[n0 * P : (n0 + per_bank) * P, j0 : j0 + width]
-                nc.sync.dma_start(out=rows.rearrange("(g p) j -> p g j", p=P), in_=staged[:])
+        def quantize_h(a, j0, width, h_bf):
+            scales = h_s[a][j0 // BANK][:, j0 % BANK : j0 % BANK + width]
+            nc.vector.quantize_mx(out=h_w[a][:, j0 : j0 + width].bitcast(FP8X4), scales=scales, in_=h_bf)
 
-        for tile in (tab_s, tab2_s, w2_raw_s, wm_s):
+        def score_pass(bank, a, n0, j0):
+            per_bank, width = bank.shape[1], bank.shape[2]
+            for g in range(per_bank):
+                ncols = slice((n0 + g) * P, (n0 + g + 1) * P)
+                nc.tensor.matmul_mx(
+                    out=bank[:, g, :],
+                    lhsT=late["wm"][:, a, ncols].bitcast(FP8X4),
+                    lhsT_scale=late["wm_s"][:].bitcast(U8)[4 * a :, ncols],
+                    rhs=h_w[a][:, j0 : j0 + width].bitcast(FP8X4),
+                    rhs_scale=h_s[a][j0 // BANK][:, j0 % BANK : j0 % BANK + width],
+                    start=(a == 0 and g == 0),
+                    stop=(a == 1 and g == per_bank - 1),
+                )
+
+        def store_scores(bank, n0, j0, copy):
+            per_bank, width = bank.shape[1], bank.shape[2]
+            staged = held("staged%d_%d" % (j0, n0), [P, per_bank, width], F32)
+            copy(out=staged[:], in_=bank[:])
+            rows = out[n0 * P : (n0 + per_bank) * P, j0 : j0 + width]
+            nc.sync.dma_start(out=rows.rearrange("(g p) j -> p g j", p=P), in_=staged[:])
+
+        def scores(j0):
+            for n0 in (0, 2, 4):
+                bank = psum_qo.tile([P, 2, STEP], F32, name="qo")
+                for a in range(2):
+                    score_pass(bank, a, n0, j0)
+                store_scores(bank, n0, j0, nc.scalar.copy)
+
+        for tile in (tab2_s, w2_raw_s):
             nc.vector.memset(tile[:], 0)
 
-        nc.sync.dma_start(out=gain_sb[:], in_=gain.rearrange("(a p t) -> p a t", a=2, t=PACK))
         nc.sync.dma_start(idx[:], offs)
         nc.sync.dma_start(out=w2_raw_w[:], in_=w2_words[0].bitcast(I32))
+        nc.sync.dma_start(out=gain_sb[:], in_=gain.rearrange("(a p t) -> p a t", a=2, t=PACK))
         nc.sync.dma_start(idx2[:], offs2)
-        load_tab(0, None)
-        load_scales(tab_s, 8, lambda rows: tab_scales[:, rows, :].bitcast(I32))
+        load_tab(0, "slot_a")
+        load_rows_by_place(tab2_s, tab2_scales)
+        load_rows_by_place(w2_raw_s, w2_scales)
         nc.vector.reciprocal(out=gain_recip[:], in_=gain_sb[:])
         nc.vector.tensor_scalar(out=gain_inv[:], in0=gain_recip[:], scalar1=BIG, scalar2=-BIG, op0=ALU.min, op1=ALU.max)
         load_w1(0, 0)
-        load_scales(tab2_s, 4, lambda rows: tab2_scales[0, rows, :].bitcast(I32))
-        load_w1(0, 1)
-        load_scales(w2_raw_s, 4, lambda rows: w2_scales[0, rows, :].bitcast(I32))
         reorder_w2(w2_w[:].bitcast(U16), w2_raw_w[:].bitcast(U16))
+        tab_s = held("tab_s", [P, T // 4], I32, "slot_b")
+        nc.vector.memset(tab_s[:], 0)
+        load_rows_by_quadrant(tab_s, tab_scales)
+        gather(v_w[0], late["tab", 0], U32, idx, 0, S)
         tab2_w = held("tab2_w", [P, T2], I32, "slot_a")
-        for half in range(2):
-            cols = slice(half * T2 // 2, (half + 1) * T2 // 2)
-            nc.sync.dma_start(out=tab2_w[:, cols], in_=tab2_words[0].rearrange("p t i -> p (t i)").bitcast(I32)[:, cols])
-
+        nc.sync.dma_start(out=tab2_w[:], in_=tab2_words[0].rearrange("p t i -> p (t i)").bitcast(I32))
+        gather(v2_s, tab2_s, U8, idx2, 0, S)
+        load_w1(0, 1)
+        reorder_w2(w2_s[:], w2_raw_s[:].bitcast(U8))
         gather(v_s, tab_s, U8, idx, 0, S)
         load_tab(1, "slot_b")
-        gather(v_w[0], late["tab", 0], U32, idx, 0, S)
-        gather(v2_s, tab2_s, U8, idx2, 0, S)
-        reorder_w2(w2_s[:], w2_raw_s[:].bitcast(U8))
+        round_w1(0, 0, nc.scalar.copy, 1)
+        load_w1(1, 0)
+        quantize_w1(0, 0)
         gather(v2_w, tab2_w, U32, idx2, 0, BANK)
-        for k in range(2):
-            quantize_w1(0, k)
-        for k in range(2):
-            load_w1(1, k)
-        load_scales(wm_s, 4, lambda rows: wm_scales[:, rows, :].bitcast(I32).rearrange("a r n -> r a n"))
         project_candidates(0, 0)
-        gather(v_w[1], late["tab", 1], U32, idx, *CHUNKS[0])
+        gather(v2_w, tab2_w, U32, idx2, BANK, BANK)
+        round_w1(0, 1, nc.vector.tensor_copy, 1)
+        load_w1(1, 1)
+        quantize_w1(0, 1)
+        late["wm_s"] = held("wm_s", [P, N // 4], I32, "slot_a")
+        nc.vector.memset(late["wm_s"][:], 0)
+        load_rows_by_quadrant(late["wm_s"], wm_scales)
+        for j0, width in ((0, STEP), (STEP, STEP), (BANK, BANK)):
+            gather(v_w[1], late["tab", 1], U32, idx, j0, width)
+        late["wm"] = held("wm_w", [P, 2, N], I32, "slot_b")
+        nc.sync.dma_start(out=late["wm"][:], in_=wm_words.rearrange("a p n i -> p a (n i)").bitcast(I32))
 
-        def prepare(g):
-            if g == 1:
-                gather(v_w[1], late["tab", 1], U32, idx, *CHUNKS[1])
-                gather(v2_w, tab2_w, U32, idx2, BANK, BANK)
-                load_wm()
-            if g == 2:
-                project_candidates(1, 0)
-                for k in range(2):
-                    quantize_w1(1, k)
-            if g == 4:
-                project_candidates(0, 1)
-                gather(v_w[1], late["tab", 1], U32, idx, BANK, BANK)
-            if g == 5:
-                project_candidates(1, 1)
+        def h_tile():
+            return keep.tile([P, PACK * BANK], BF16, name="h_bf", tag="h_bf", align_bytes=64)
 
-        terms = {}
-        features = {}
-        for g in range(len(STEPS) + 2):
-            prepare(g)
-            if g < len(STEPS):
-                terms[g] = pair_terms(*STEPS[g])
-            if g >= 2:
-                a, c = STEPS[g - 2]
-                nc.vector.quantize_mx(out=h_w[a][c][:].bitcast(FP8X4), scales=h_s[a][c][:], in_=features[g - 2][:])
-            if 1 <= g <= len(STEPS):
-                features[g - 1] = pair_feature(STEPS[g - 1][1], *terms[g - 1])
-            if g >= 2 and STEPS[g - 2][0] == 1:
-                scores(STEPS[g - 2][1])
+        FINAL = nc.gpsimd
+        step0 = pair_terms(0, 0, STEP)
+        project_candidates(0, 1)
+        step1 = pair_terms(0, STEP, STEP)
+        h_bf = h_tile()
+        pair_feature(FINAL, h_bf[:, : PACK * STEP], step0)
+        round_w1(1, 0, nc.scalar.copy, 4)
+        step2 = pair_terms(0, 2 * STEP, STEP)
+        pair_feature(FINAL, h_bf[:, PACK * STEP :], step1)
+        round_w1(1, 1, nc.scalar.copy, 4)
+        quantize_h(0, 0, BANK, h_bf[:])
+        for k in range(2):
+            quantize_w1(1, k)
+        step3 = pair_terms(0, 3 * STEP, STEP)
+        project_candidates(1, 0)
+        h_bf = h_tile()
+        pair_feature(FINAL, h_bf[:, : PACK * STEP], step2)
+        step4 = pair_terms(1, 0, STEP)
+        pair_feature(FINAL, h_bf[:, PACK * STEP :], step3)
+        quantize_h(0, BANK, BANK, h_bf[:])
+        step5 = pair_terms(1, STEP, STEP)
+        project_candidates(1, 1)
+        h_bf = h_tile()
+        pair_feature(FINAL, h_bf[:, : PACK * STEP], step4)
+        quantize_h(1, 0, STEP, h_bf[:, : PACK * STEP])
+        step6 = pair_terms(1, 2 * STEP, STEP)
+        scores(0)
+        h_bf = h_tile()
+        pair_feature(FINAL, h_bf[:, : PACK * STEP], step5)
+        quantize_h(1, STEP, STEP, h_bf[:, : PACK * STEP])
+        last = [pair_terms(1, 3 * STEP + i * NARROW, NARROW) for i in range(2)]
+        scores(STEP)
+        h_bf = h_tile()
+        pair_feature(FINAL, h_bf[:, : PACK * STEP], step6)
+        wide = [(psum_qo.tile([P, 2, STEP], F32, name="qo"), n0) for n0 in (0, 2, 4)]
+        narrow = [
+            [(psum_qo.tile([P, 3, NARROW], F32, name="qo"), 0), (psum_p.tile([P, 3, NARROW], F32, name="pp"), 3)],
+            [(psum_p.tile([P, 3, NARROW], F32, name="pp"), n0) for n0 in (0, 3)],
+        ]
+        for bank, n0 in wide:
+            score_pass(bank, 0, n0, 2 * STEP)
+        for i in range(2):
+            for bank, n0 in narrow[i]:
+                score_pass(bank, 0, n0, 3 * STEP + i * NARROW)
+        quantize_h(1, 2 * STEP, STEP, h_bf[:, : PACK * STEP])
+        for bank, n0 in wide:
+            score_pass(bank, 1, n0, 2 * STEP)
+            store_scores(bank, n0, 2 * STEP, nc.scalar.copy)
+        h_bf = h_tile()
+        for i in range(2):
+            pair_feature(nc.vector, h_bf[:, i * PACK * NARROW : (i + 1) * PACK * NARROW], last[i])
+        for i in range(2):
+            j0 = 3 * STEP + i * NARROW
+            quantize_h(1, j0, NARROW, h_bf[:, i * PACK * NARROW : (i + 1) * PACK * NARROW])
+            for bank, n0 in narrow[i]:
+                score_pass(bank, 1, n0, j0)
+                store_scores(bank, n0, j0, nc.vector.tensor_copy if n0 == 3 else nc.scalar.copy)

@@ -49,8 +49,10 @@ def tile_list_entity_merge_scores_kernel(
         v_w = [held("v_w%d" % k, [P, S], U32) for k in range(2)]
         v_s = held("v_s", [P, S], U8)
         v2_w = held("v2_w", [P, S], U32)
+        v2_spread = held("v2_spread", [P, S], U8)
         v2_s = held("v2_s", [P, S], U8)
-        w2_raw_w = held("w2_raw_w", [P, H // 2], I32, "slot_b")
+        tab_s = held("tab_s", [P, T // 4], I32, "slot_b")
+        w2_raw_w = held("w2_raw_w", [P, H // 2], I32)
         w2_raw_s = held("w2_raw_s", [P, H // 4], I32)
         w2_w = held("w2_w", [P, 2 * H], U8)
         w2_s = held("w2_s", [P, H], U8)
@@ -60,7 +62,7 @@ def tile_list_entity_merge_scores_kernel(
         h_s = [[held("h_s%d%d" % (a, half), [P, BANK], U8) for half in range(2)] for a in range(2)]
         w1_s = [[held("w1_s0%d" % k, [P, PASS], U8)[:] for k in range(2)], [h_s[0][0][4:, :], h_s[0][0][8:, :]]]
         gain_sb = held("gain_sb", [P, 2, PACK], F32)
-        gain_recip = held("gain_recip", [P, 2, PACK], F32, "slot_c")
+        gain_recip = held("gain_recip", [P, 2, PACK], F32, "slot_a")
         gain_inv = held("gain_inv", [P, 2, PACK], F32)
         gq = [[held("gq%d%d" % (a, half), [P, PACK, BANK], F32) for half in range(2)] for a in range(2)]
         late = {}
@@ -155,8 +157,8 @@ def tile_list_entity_merge_scores_kernel(
             for bank, planes, pairs in banks:
                 nc.vector.tensor_tensor(
                     out=prod[:, pairs, :, :],
-                    in0=bank[:].rearrange(in_pairs, e=2),
-                    in1=gq_chunk[:, planes, :].rearrange(in_pairs, e=2),
+                    in0=gq_chunk[:, planes, :].rearrange(in_pairs, e=2),
+                    in1=bank[:].rearrange(in_pairs, e=2),
                     op=ALU.mult,
                 )
             return prod, dist
@@ -202,27 +204,28 @@ def tile_list_entity_merge_scores_kernel(
                     score_pass(bank, a, n0, j0)
                 store_scores(bank, n0, j0, nc.scalar.copy)
 
-        for tile in (tab2_s, w2_raw_s):
+        for tile in (tab2_s, tab_s, w2_raw_s):
             nc.vector.memset(tile[:], 0)
+        nc.vector.memset(v2_s[:].bitcast(I32), 0)
 
         nc.sync.dma_start(idx[:], offs)
         nc.sync.dma_start(out=w2_raw_w[:], in_=w2_words[0].bitcast(I32))
         nc.sync.dma_start(out=gain_sb[:], in_=gain.rearrange("(a p t) -> p a t", a=2, t=PACK))
         nc.sync.dma_start(idx2[:], offs2)
-        load_tab(0, "slot_a")
-        load_rows_by_place(tab2_s, tab2_scales)
+        load_tab(0, None)
+        load_w1(0, 0)
+        nc.sync.dma_start(out=tab2_s[0:P:8], in_=tab2_scales[0].bitcast(I32))
+        load_rows_by_quadrant(tab_s, tab_scales)
         load_rows_by_place(w2_raw_s, w2_scales)
         nc.vector.reciprocal(out=gain_recip[:], in_=gain_sb[:])
         nc.vector.tensor_scalar(out=gain_inv[:], in0=gain_recip[:], scalar1=BIG, scalar2=-BIG, op0=ALU.min, op1=ALU.max)
-        load_w1(0, 0)
-        reorder_w2(w2_w[:].bitcast(U16), w2_raw_w[:].bitcast(U16))
-        tab_s = held("tab_s", [P, T // 4], I32, "slot_b")
-        nc.vector.memset(tab_s[:], 0)
-        load_rows_by_quadrant(tab_s, tab_scales)
-        gather(v_w[0], late["tab", 0], U32, idx, 0, S)
         tab2_w = held("tab2_w", [P, T2], I32, "slot_a")
         nc.sync.dma_start(out=tab2_w[:], in_=tab2_words[0].rearrange("p t i -> p (t i)").bitcast(I32))
-        gather(v2_s, tab2_s, U8, idx2, 0, S)
+        reorder_w2(w2_w[:].bitcast(U16), w2_raw_w[:].bitcast(U16))
+        gather(v_w[0], late["tab", 0], U32, idx, 0, S)
+        gather(v2_spread, tab2_s, U8, idx2, 0, S)
+        for r in range(4):
+            nc.sync.dma_start(out=v2_s[:].bitcast(I32)[r:P:32], in_=v2_spread[:].bitcast(I32)[8 * r : P : 32])
         load_w1(0, 1)
         reorder_w2(w2_s[:], w2_raw_s[:].bitcast(U8))
         gather(v_s, tab_s, U8, idx, 0, S)

@@ -127,6 +127,7 @@ def tile_list_entity_merge_scores_kernel(
             dist = ring.tile([P, 2, width, 2], F32, name="dist", align_bytes=64)
             prod = ring.tile([P, 2, width, 2], F32, name="prod", align_bytes=64)
             in_pairs = "p (u e) n -> p u n e"
+            by_twos = "p e (c i) -> p c e i"
             banks = []
             for t0 in range(0, PACK, per_bank):
                 planes = slice(t0, t0 + per_bank)
@@ -155,12 +156,14 @@ def tile_list_entity_merge_scores_kernel(
                     )
                 nc.scalar.activation(out=dist[:, pairs, :, :], in_=diff[:, planes, :].rearrange(in_pairs, e=2), func=ACT.Abs)
             for bank, planes, pairs in banks:
-                nc.vector.tensor_tensor(
-                    out=prod[:, pairs, :, :],
-                    in0=gq_chunk[:, planes, :].rearrange(in_pairs, e=2),
-                    in1=bank[:].rearrange(in_pairs, e=2),
-                    op=ALU.mult,
-                )
+                for u in range(pairs.start, pairs.stop):
+                    pair = slice(2 * u - planes.start, 2 * u - planes.start + 2)
+                    nc.vector.tensor_tensor(
+                        out=prod[:, u, :, :].rearrange("p (c i) e -> p c e i", i=2),
+                        in0=gq_chunk[:, 2 * u : 2 * u + 2, :].rearrange(by_twos, i=2),
+                        in1=bank[:, pair, :].rearrange(by_twos, i=2),
+                        op=ALU.mult,
+                    )
             return prod, dist
 
         def pair_feature(engine, h_bf, terms):

@@ -27,6 +27,22 @@ BIG = 3.0e38
 STEP = 256
 NARROW = 128
 
+BIG_TILE = 8192
+SCALE_BYTES = S + H + 2 * N
+PLACE = {
+    "gain_recip": 0,
+    "tab2_w": 0,
+    "w1_raw10": 0,
+    "w1_raw11": BIG_TILE,
+    "w1_raw00": 3 * BIG_TILE,
+    "wm_w": 3 * BIG_TILE,
+    "v2_spread": 4 * BIG_TILE - S // 2,
+    "w1_raw01": 4 * BIG_TILE,
+    "tab_w0": 5 * BIG_TILE,
+    "tab_s": 6 * BIG_TILE - T // 2,
+    "tab_w1": 6 * BIG_TILE,
+}
+
 
 def tile_list_entity_merge_scores_kernel(
     tc, tab_words, tab_scales, tab2_words, tab2_scales, offs, offs2, w1, w2_words, w2_scales, gain, wm_words, wm_scales, out
@@ -35,6 +51,7 @@ def tile_list_entity_merge_scores_kernel(
     with ExitStack() as ctx:
         lists = ctx.enter_context(tc.tile_pool(name="lists", bufs=1))
         keep = ctx.enter_context(tc.tile_pool(name="keep", bufs=1))
+        placed_pool = ctx.enter_context(tc.tile_pool(name="placed", bufs=1))
         ring = ctx.enter_context(tc.tile_pool(name="ring", bufs=3))
         psum_p = ctx.enter_context(tc.psum_pool(name="psum_p", bufs=4))
         psum_qo = ctx.enter_context(tc.psum_pool(name="psum_qo", bufs=4))
@@ -42,27 +59,31 @@ def tile_list_entity_merge_scores_kernel(
         def held(name, shape, dtype, slot=None):
             return keep.tile(shape, dtype, name=name, tag=slot or name, align_bytes=64)
 
+        def placed(name, shape, dtype):
+            return placed_pool.tile(shape, dtype, name=name, offset=PLACE[name], align_bytes=64)
+
         idx = lists.tile([P, S // PER_COLUMN], U16, name="idx")
         idx2 = lists.tile([P, S // PER_COLUMN], U16, name="idx2")
 
-        tab2_s = held("tab2_s", [P, T2 // 4], I32, "slot_d")
+        tab2_s = held("tab2_s", [P, T2 // 4], I32)
         v_w = [held("v_w%d" % k, [P, S], U32) for k in range(2)]
         v_s = held("v_s", [P, S], U8)
         v2_w = held("v2_w", [P, S], U32)
-        v2_spread = held("v2_spread", [P, S], U8)
-        v2_s = held("v2_s", [P, S], U8)
-        tab_s = held("tab_s", [P, T // 4], I32, "slot_b")
+        v2_spread = placed("v2_spread", [P, S], U8)
+        planes_in_place = held("planes_in_place", [P, SCALE_BYTES // 4], I32)
+        scale_bytes = planes_in_place[:].bitcast(U8)
+        v2_s, w2_s, wm_s = scale_bytes[:, :S], scale_bytes[:, S : S + H], scale_bytes[:, S + H :]
+        tab_s = placed("tab_s", [P, T // 4], I32)
         w2_raw_w = held("w2_raw_w", [P, H // 2], I32)
         w2_raw_s = held("w2_raw_s", [P, H // 4], I32)
         w2_w = held("w2_w", [P, 2 * H], U8)
-        w2_s = held("w2_s", [P, H], U8)
         w1_bf = [[held("w1_bf%d%d" % (a, k), [P, PACK * PASS], BF16) for k in range(2)] for a in range(2)]
         w1_w = [[held("w1_w%d%d" % (a, k), [P, PASS], U32) for k in range(2)] for a in range(2)]
         h_w = [held("h_w%d" % a, [P, S], U32) for a in range(2)]
         h_s = [[held("h_s%d%d" % (a, half), [P, BANK], U8) for half in range(2)] for a in range(2)]
         w1_s = [[held("w1_s0%d" % k, [P, PASS], U8)[:] for k in range(2)], [h_s[0][0][4:, :], h_s[0][0][8:, :]]]
         gain_sb = held("gain_sb", [P, 2, PACK], F32)
-        gain_recip = held("gain_recip", [P, 2, PACK], F32, "slot_a")
+        gain_recip = placed("gain_recip", [P, 2, PACK], F32)[:]
         gain_inv = held("gain_inv", [P, 2, PACK], F32)
         gq = [[held("gq%d%d" % (a, half), [P, PACK, BANK], F32) for half in range(2)] for a in range(2)]
         late = {}
@@ -71,16 +92,12 @@ def tile_list_entity_merge_scores_kernel(
             for quad in range(QUADS):
                 nc.sync.dma_start(out=tile[32 * quad : 32 * quad + 8], in_=source[:, 4 * quad : 4 * quad + 4, :].bitcast(I32))
 
-        def load_rows_by_place(tile, source):
-            for r in range(4):
-                nc.sync.dma_start(out=tile[r:P:32], in_=source[0, r:16:4, :].bitcast(I32))
-
-        def load_tab(k, slot):
-            late["tab", k] = held("tab_w%d" % k, [P, T], I32, slot)
+        def load_tab(k):
+            late["tab", k] = placed("tab_w%d" % k, [P, T], I32)
             nc.sync.dma_start(out=late["tab", k][:], in_=tab_words[k].rearrange("p t i -> p (t i)").bitcast(I32))
 
         def load_w1(a, k):
-            late["w1", a, k] = held("w1_raw%d%d" % (a, k), [P, PACK, PASS], F32, ("slot_c", "slot_d")[k])
+            late["w1", a, k] = placed("w1_raw%d%d" % (a, k), [P, PACK, PASS], F32)
             rows = w1[k * PASS : (k + 1) * PASS, a * PASS : (a + 1) * PASS]
             nc.sync.dma_start(out=late["w1", a, k][:], in_=rows.rearrange("(p j) r -> p j r", j=PACK))
 
@@ -164,14 +181,14 @@ def tile_list_entity_merge_scores_kernel(
                         in1=bank[:, pair, :].rearrange(by_twos, i=2),
                         op=ALU.mult,
                     )
-            return prod, dist
+            return prod[:], dist[:]
 
         def pair_feature(engine, h_bf, terms):
             prod, dist = terms
             engine.tensor_tensor(
                 out=h_bf.rearrange("p (n u e) -> p n u e", u=2, e=2),
-                in0=prod[:].rearrange("p u n e -> p n u e"),
-                in1=dist[:].rearrange("p u n e -> p n u e"),
+                in0=prod.rearrange("p u n e -> p n u e"),
+                in1=dist.rearrange("p u n e -> p n u e"),
                 op=ALU.mult,
             )
 
@@ -186,7 +203,7 @@ def tile_list_entity_merge_scores_kernel(
                 nc.tensor.matmul_mx(
                     out=bank[:, g, :],
                     lhsT=late["wm"][:, a, ncols].bitcast(FP8X4),
-                    lhsT_scale=late["wm_s"][:].bitcast(U8)[4 * a :, ncols],
+                    lhsT_scale=wm_s[:, a * N + ncols.start : a * N + ncols.stop],
                     rhs=h_w[a][:, j0 : j0 + width].bitcast(FP8X4),
                     rhs_scale=h_s[a][j0 // BANK][:, j0 % BANK : j0 % BANK + width],
                     start=(a == 0 and g == 0),
@@ -207,55 +224,58 @@ def tile_list_entity_merge_scores_kernel(
                     score_pass(bank, a, n0, j0)
                 store_scores(bank, n0, j0, nc.scalar.copy)
 
-        for tile in (tab2_s, tab_s, w2_raw_s):
+        for tile in (tab2_s, w2_raw_s, tab_s, planes_in_place):
             nc.vector.memset(tile[:], 0)
-        nc.vector.memset(v2_s[:].bitcast(I32), 0)
 
-        nc.sync.dma_start(idx[:], offs)
-        nc.sync.dma_start(out=w2_raw_w[:], in_=w2_words[0].bitcast(I32))
-        nc.sync.dma_start(out=gain_sb[:], in_=gain.rearrange("(a p t) -> p a t", a=2, t=PACK))
         nc.sync.dma_start(idx2[:], offs2)
-        load_tab(0, None)
-        load_w1(0, 0)
+        nc.sync.dma_start(out=gain_sb[:], in_=gain.rearrange("(a p t) -> p a t", a=2, t=PACK))
+        nc.sync.dma_start(idx[:], offs)
+        spread = held("spread", [P, SCALE_BYTES // 4], I32)
+        nc.sync.dma_start(
+            out=spread[0:P:8, (S + H) // 4 :].rearrange("p (a n) -> p a n", a=2),
+            in_=wm_scales.rearrange("a q n -> q a n").bitcast(I32),
+        )
+        nc.sync.dma_start(out=w2_raw_w[:], in_=w2_words[0].bitcast(I32))
         nc.sync.dma_start(out=tab2_s[0:P:8], in_=tab2_scales[0].bitcast(I32))
+        nc.sync.dma_start(out=w2_raw_s[0:P:8], in_=w2_scales[0].bitcast(I32))
         load_rows_by_quadrant(tab_s, tab_scales)
-        load_rows_by_place(w2_raw_s, w2_scales)
-        nc.vector.reciprocal(out=gain_recip[:], in_=gain_sb[:])
-        nc.vector.tensor_scalar(out=gain_inv[:], in0=gain_recip[:], scalar1=BIG, scalar2=-BIG, op0=ALU.min, op1=ALU.max)
-        tab2_w = held("tab2_w", [P, T2], I32, "slot_a")
+        nc.vector.reciprocal(out=gain_recip, in_=gain_sb[:])
+        nc.vector.tensor_scalar(out=gain_inv[:], in0=gain_recip, scalar1=BIG, scalar2=-BIG, op0=ALU.min, op1=ALU.max)
+        tab2_w = placed("tab2_w", [P, T2], I32)
         nc.sync.dma_start(out=tab2_w[:], in_=tab2_words[0].rearrange("p t i -> p (t i)").bitcast(I32))
         reorder_w2(w2_w[:].bitcast(U16), w2_raw_w[:].bitcast(U16))
-        gather(v_w[0], late["tab", 0], U32, idx, 0, S)
         gather(v2_spread, tab2_s, U8, idx2, 0, S)
+        reorder_w2(spread[:].bitcast(U8)[:, S : S + H], w2_raw_s[:].bitcast(U8))
+        nc.vector.tensor_copy(out=spread[:, : S // 4], in_=v2_spread[:].bitcast(I32))
         for r in range(4):
-            nc.sync.dma_start(out=v2_s[:].bitcast(I32)[r:P:32], in_=v2_spread[:].bitcast(I32)[8 * r : P : 32])
+            nc.sync.dma_start(out=planes_in_place[r:P:32], in_=spread[8 * r : P : 32])
+        load_w1(0, 0)
         load_w1(0, 1)
-        reorder_w2(w2_s[:], w2_raw_s[:].bitcast(U8))
         gather(v_s, tab_s, U8, idx, 0, S)
-        load_tab(1, "slot_b")
-        round_w1(0, 0, nc.scalar.copy, 1)
-        load_w1(1, 0)
-        quantize_w1(0, 0)
+        load_tab(0)
+        load_tab(1)
         gather(v2_w, tab2_w, U32, idx2, 0, BANK)
-        project_candidates(0, 0)
         gather(v2_w, tab2_w, U32, idx2, BANK, BANK)
-        round_w1(0, 1, nc.vector.tensor_copy, 1)
+        load_w1(1, 0)
         load_w1(1, 1)
+        project_candidates(0, 0)
+        project_candidates(0, 1)
+        project_candidates(1, 0)
+        round_w1(0, 0, nc.vector.tensor_copy, 1)
+        quantize_w1(0, 0)
+        round_w1(0, 1, nc.vector.tensor_copy, 1)
         quantize_w1(0, 1)
-        late["wm_s"] = held("wm_s", [P, N // 4], I32, "slot_a")
-        nc.vector.memset(late["wm_s"][:], 0)
-        load_rows_by_quadrant(late["wm_s"], wm_scales)
-        for j0, width in ((0, STEP), (STEP, STEP), (BANK, BANK)):
-            gather(v_w[1], late["tab", 1], U32, idx, j0, width)
-        late["wm"] = held("wm_w", [P, 2, N], I32, "slot_b")
+        late["wm"] = placed("wm_w", [P, 2, N], I32)
         nc.sync.dma_start(out=late["wm"][:], in_=wm_words.rearrange("a p n i -> p a (n i)").bitcast(I32))
+        gather(v_w[0], late["tab", 0], U32, idx, 0, S)
+        for j0, width in ((0, STEP), (STEP, S - STEP)):
+            gather(v_w[1], late["tab", 1], U32, idx, j0, width)
 
         def h_tile():
             return keep.tile([P, PACK * BANK], BF16, name="h_bf", tag="h_bf", align_bytes=64)
 
         FINAL = nc.gpsimd
         step0 = pair_terms(0, 0, STEP)
-        project_candidates(0, 1)
         step1 = pair_terms(0, STEP, STEP)
         h_bf = h_tile()
         pair_feature(FINAL, h_bf[:, : PACK * STEP], step0)
@@ -267,14 +287,13 @@ def tile_list_entity_merge_scores_kernel(
         for k in range(2):
             quantize_w1(1, k)
         step3 = pair_terms(0, 3 * STEP, STEP)
-        project_candidates(1, 0)
+        project_candidates(1, 1)
         h_bf = h_tile()
         pair_feature(FINAL, h_bf[:, : PACK * STEP], step2)
         step4 = pair_terms(1, 0, STEP)
         pair_feature(FINAL, h_bf[:, PACK * STEP :], step3)
         quantize_h(0, BANK, BANK, h_bf[:])
         step5 = pair_terms(1, STEP, STEP)
-        project_candidates(1, 1)
         h_bf = h_tile()
         pair_feature(FINAL, h_bf[:, : PACK * STEP], step4)
         quantize_h(1, 0, STEP, h_bf[:, : PACK * STEP])
@@ -283,7 +302,8 @@ def tile_list_entity_merge_scores_kernel(
         h_bf = h_tile()
         pair_feature(FINAL, h_bf[:, : PACK * STEP], step5)
         quantize_h(1, STEP, STEP, h_bf[:, : PACK * STEP])
-        last = [pair_terms(1, 3 * STEP + i * NARROW, NARROW) for i in range(2)]
+        step7 = pair_terms(1, 3 * STEP, STEP)
+        last = [[term[:, :, i * NARROW : (i + 1) * NARROW, :] for term in step7] for i in range(2)]
         scores(STEP)
         h_bf = h_tile()
         pair_feature(FINAL, h_bf[:, : PACK * STEP], step6)

@@ -28,19 +28,21 @@ STEP = 256
 NARROW = 128
 
 BIG_TILE = 8192
-SCALE_BYTES = S + H + 2 * N
+SCALE_BYTES = S + H
 PLACE = {
     "gain_recip": 0,
     "tab2_w": 0,
     "w1_raw10": 0,
     "w1_raw11": BIG_TILE,
-    "w1_raw00": 3 * BIG_TILE,
-    "wm_w": 3 * BIG_TILE,
-    "v2_spread": 4 * BIG_TILE - S // 2,
+    "w1_raw00": 2 * BIG_TILE,
+    "wm_s": 2 * BIG_TILE,
+    "wm_w": 2 * BIG_TILE + N,
+    "v2_spread": 3 * BIG_TILE - S // 2,
+    "tab_w0": 3 * BIG_TILE,
     "w1_raw01": 4 * BIG_TILE,
-    "tab_w0": 5 * BIG_TILE,
-    "tab_s": 6 * BIG_TILE - T // 2,
-    "tab_w1": 6 * BIG_TILE,
+    "gq10": 4 * BIG_TILE,
+    "tab_s": 5 * BIG_TILE - T // 2,
+    "tab_w1": 5 * BIG_TILE,
 }
 
 
@@ -72,7 +74,7 @@ def tile_list_entity_merge_scores_kernel(
         v2_spread = placed("v2_spread", [P, S], U8)
         planes_in_place = held("planes_in_place", [P, SCALE_BYTES // 4], I32)
         scale_bytes = planes_in_place[:].bitcast(U8)
-        v2_s, w2_s, wm_s = scale_bytes[:, :S], scale_bytes[:, S : S + H], scale_bytes[:, S + H :]
+        v2_s, w2_s = scale_bytes[:, :S], scale_bytes[:, S:]
         tab_s = placed("tab_s", [P, T // 4], I32)
         w2_raw_w = held("w2_raw_w", [P, H // 2], I32)
         w2_raw_s = held("w2_raw_s", [P, H // 4], I32)
@@ -85,11 +87,11 @@ def tile_list_entity_merge_scores_kernel(
         gain_sb = held("gain_sb", [P, 2, PACK], F32)
         gain_recip = placed("gain_recip", [P, 2, PACK], F32)[:]
         gain_inv = held("gain_inv", [P, 2, PACK], F32)
-        gq = [[held("gq%d%d" % (a, half), [P, PACK, BANK], F32) for half in range(2)] for a in range(2)]
+        gq = {}
         late = {}
 
         def load_rows_by_quadrant(tile, source):
-            for quad in range(QUADS):
+            for quad in (0, 2, 1, 3):
                 nc.sync.dma_start(out=tile[32 * quad : 32 * quad + 8], in_=source[:, 4 * quad : 4 * quad + 4, :].bitcast(I32))
 
         def load_tab(k):
@@ -111,17 +113,20 @@ def tile_list_entity_merge_scores_kernel(
                 in_=loaded.rearrange("p (a m t) -> p a t m", a=2, t=PACK),
             )
 
-        def round_w1(a, k, copy, pieces):
+        def round_w1(a, k, copies):
             rounded = w1_bf[a][k][:].rearrange("p (t m j) -> p m t j", t=PACK, j=PACK)
             loaded = late["w1", a, k][:].rearrange("p j (m t) -> p m t j", t=PACK)
-            for m0 in range(0, P, P // pieces):
-                copy(out=rounded[:, m0 : m0 + P // pieces], in_=loaded[:, m0 : m0 + P // pieces])
+            width = P // len(copies)
+            for i, copy in enumerate(copies):
+                copy(out=rounded[:, i * width : (i + 1) * width], in_=loaded[:, i * width : (i + 1) * width])
 
         def quantize_w1(a, k):
             nc.vector.quantize_mx(out=w1_w[a][k][:].bitcast(FP8X4), scales=w1_s[a][k], in_=w1_bf[a][k][:])
 
         def project_candidates(a, half):
             cols = slice(half * BANK, (half + 1) * BANK)
+            name = "gq%d%d" % (a, half)
+            gq[a, half] = (placed if name in PLACE else held)(name, [P, PACK, BANK], F32)
             for t in range(PACK):
                 r0 = a * PASS + t * P
                 bank = psum_qo.tile([P, BANK], F32, name="qo")
@@ -134,12 +139,12 @@ def tile_list_entity_merge_scores_kernel(
                     start=True,
                     stop=True,
                 )
-                nc.scalar.activation(out=gq[a][half][:, t, :], in_=bank[:], func=ACT.Copy, scale=gain_sb[:, a, t : t + 1])
+                nc.scalar.activation(out=gq[a, half][:, t, :], in_=bank[:], func=ACT.Copy, scale=gain_sb[:, a, t : t + 1])
 
         def pair_terms(a, j0, width):
             cols = slice(j0, j0 + width)
             per_bank = BANK // width
-            gq_chunk = gq[a][j0 // BANK][:, :, j0 % BANK : j0 % BANK + width]
+            gq_chunk = gq[a, j0 // BANK][:, :, j0 % BANK : j0 % BANK + width]
             diff = ring.tile([P, PACK, width], F32, name="diff", align_bytes=64)
             dist = ring.tile([P, 2, width, 2], F32, name="dist", align_bytes=64)
             prod = ring.tile([P, 2, width, 2], F32, name="prod", align_bytes=64)
@@ -203,7 +208,7 @@ def tile_list_entity_merge_scores_kernel(
                 nc.tensor.matmul_mx(
                     out=bank[:, g, :],
                     lhsT=late["wm"][:, a, ncols].bitcast(FP8X4),
-                    lhsT_scale=wm_s[:, a * N + ncols.start : a * N + ncols.stop],
+                    lhsT_scale=late["wm_s"][:].bitcast(U8)[4 * a :, ncols],
                     rhs=h_w[a][:, j0 : j0 + width].bitcast(FP8X4),
                     rhs_scale=h_s[a][j0 // BANK][:, j0 % BANK : j0 % BANK + width],
                     start=(a == 0 and g == 0),
@@ -224,50 +229,48 @@ def tile_list_entity_merge_scores_kernel(
                     score_pass(bank, a, n0, j0)
                 store_scores(bank, n0, j0, nc.scalar.copy)
 
-        for tile in (tab2_s, w2_raw_s, tab_s, planes_in_place):
+        for tile in (tab2_s, tab_s, planes_in_place):
             nc.vector.memset(tile[:], 0)
 
-        nc.sync.dma_start(idx2[:], offs2)
         nc.sync.dma_start(out=gain_sb[:], in_=gain.rearrange("(a p t) -> p a t", a=2, t=PACK))
+        nc.sync.dma_start(idx2[:], offs2)
         nc.sync.dma_start(idx[:], offs)
         spread = held("spread", [P, SCALE_BYTES // 4], I32)
-        nc.sync.dma_start(
-            out=spread[0:P:8, (S + H) // 4 :].rearrange("p (a n) -> p a n", a=2),
-            in_=wm_scales.rearrange("a q n -> q a n").bitcast(I32),
-        )
+        nc.sync.dma_start(out=w2_raw_s[:], in_=w2_scales[0].bitcast(I32).unsqueeze(1).broadcast_to([16, 8, H // 4]))
         nc.sync.dma_start(out=w2_raw_w[:], in_=w2_words[0].bitcast(I32))
         nc.sync.dma_start(out=tab2_s[0:P:8], in_=tab2_scales[0].bitcast(I32))
-        nc.sync.dma_start(out=w2_raw_s[0:P:8], in_=w2_scales[0].bitcast(I32))
         load_rows_by_quadrant(tab_s, tab_scales)
         nc.vector.reciprocal(out=gain_recip, in_=gain_sb[:])
         nc.vector.tensor_scalar(out=gain_inv[:], in0=gain_recip, scalar1=BIG, scalar2=-BIG, op0=ALU.min, op1=ALU.max)
         tab2_w = placed("tab2_w", [P, T2], I32)
         nc.sync.dma_start(out=tab2_w[:], in_=tab2_words[0].rearrange("p t i -> p (t i)").bitcast(I32))
-        reorder_w2(w2_w[:].bitcast(U16), w2_raw_w[:].bitcast(U16))
-        gather(v2_spread, tab2_s, U8, idx2, 0, S)
         reorder_w2(spread[:].bitcast(U8)[:, S : S + H], w2_raw_s[:].bitcast(U8))
+        gather(v2_spread, tab2_s, U8, idx2, 0, S)
         nc.vector.tensor_copy(out=spread[:, : S // 4], in_=v2_spread[:].bitcast(I32))
         for r in range(4):
             nc.sync.dma_start(out=planes_in_place[r:P:32], in_=spread[8 * r : P : 32])
         load_w1(0, 0)
-        load_w1(0, 1)
-        gather(v_s, tab_s, U8, idx, 0, S)
         load_tab(0)
+        reorder_w2(w2_w[:].bitcast(U16), w2_raw_w[:].bitcast(U16))
+        gather(v_s, tab_s, U8, idx, 0, S)
+        load_w1(0, 1)
         load_tab(1)
         gather(v2_w, tab2_w, U32, idx2, 0, BANK)
         gather(v2_w, tab2_w, U32, idx2, BANK, BANK)
         load_w1(1, 0)
         load_w1(1, 1)
         project_candidates(0, 0)
-        project_candidates(0, 1)
-        project_candidates(1, 0)
-        round_w1(0, 0, nc.vector.tensor_copy, 1)
-        quantize_w1(0, 0)
-        round_w1(0, 1, nc.vector.tensor_copy, 1)
-        quantize_w1(0, 1)
+        round_w1(0, 0, [nc.vector.tensor_copy])
         late["wm"] = placed("wm_w", [P, 2, N], I32)
         nc.sync.dma_start(out=late["wm"][:], in_=wm_words.rearrange("a p n i -> p a (n i)").bitcast(I32))
+        late["wm_s"] = placed("wm_s", [P, N // 4], I32)
+        nc.vector.memset(late["wm_s"][:], 0)
+        load_rows_by_quadrant(late["wm_s"], wm_scales)
+        quantize_w1(0, 0)
         gather(v_w[0], late["tab", 0], U32, idx, 0, S)
+        round_w1(0, 1, [nc.scalar.copy, nc.vector.tensor_copy])
+        quantize_w1(0, 1)
+        project_candidates(0, 1)
         for j0, width in ((0, STEP), (STEP, S - STEP)):
             gather(v_w[1], late["tab", 1], U32, idx, j0, width)
 
@@ -279,10 +282,11 @@ def tile_list_entity_merge_scores_kernel(
         step1 = pair_terms(0, STEP, STEP)
         h_bf = h_tile()
         pair_feature(FINAL, h_bf[:, : PACK * STEP], step0)
-        round_w1(1, 0, nc.scalar.copy, 4)
+        round_w1(1, 0, [nc.scalar.copy] * 4)
         step2 = pair_terms(0, 2 * STEP, STEP)
         pair_feature(FINAL, h_bf[:, PACK * STEP :], step1)
-        round_w1(1, 1, nc.scalar.copy, 4)
+        round_w1(1, 1, [nc.scalar.copy] * 4)
+        project_candidates(1, 0)
         quantize_h(0, 0, BANK, h_bf[:])
         for k in range(2):
             quantize_w1(1, k)

@@ -114,8 +114,8 @@ def tile_list_entity_merge_scores_kernel(
             )
 
         def round_w1(a, k, copies):
-            rounded = w1_bf[a][k][:].rearrange("p (t m j) -> p m t j", t=PACK, j=PACK)
-            loaded = late["w1", a, k][:].rearrange("p j (m t) -> p m t j", t=PACK)
+            rounded = w1_bf[a][k][:].rearrange("p (t m j) -> p m j t", t=PACK, j=PACK)
+            loaded = late["w1", a, k][:].rearrange("p j (m t) -> p m j t", t=PACK)
             width = P // len(copies)
             for i, copy in enumerate(copies):
                 copy(out=rounded[:, i * width : (i + 1) * width], in_=loaded[:, i * width : (i + 1) * width])

@@ -21,28 +21,26 @@ PACK = 4
 PASS = P * PACK
 BANK = 512
 PER_COLUMN = 16
-QUADS = 4
+ROWS = 16
+TOP = P - ROWS
 BIG = 3.0e38
 
 STEP = 256
 NARROW = 128
 
-BIG_TILE = 8192
-SCALE_BYTES = S + H
+UNIT = 8192
 PLACE = {
-    "gain_recip": 0,
-    "tab2_w": 0,
-    "w1_raw10": 0,
-    "w1_raw11": BIG_TILE,
-    "w1_raw00": 2 * BIG_TILE,
-    "wm_s": 2 * BIG_TILE,
-    "wm_w": 2 * BIG_TILE + N,
-    "v2_spread": 3 * BIG_TILE - S // 2,
-    "tab_w0": 3 * BIG_TILE,
-    "w1_raw01": 4 * BIG_TILE,
-    "gq10": 4 * BIG_TILE,
-    "tab_s": 5 * BIG_TILE - T // 2,
-    "tab_w1": 5 * BIG_TILE,
+    "w2_raw_s": 0,
+    "tab_w0": 0,
+    "v2_picked": UNIT,
+    "w1_raw00": UNIT,
+    "tab2_w": 2 * UNIT,
+    "w1_raw01": 2 * UNIT,
+    "tab_w1": 3 * UNIT,
+    "tab_s": 4 * UNIT,
+    "w1_raw10": 4 * UNIT,
+    "w1_raw11": 0,
+    "wm_w": 2 * UNIT,
 }
 
 
@@ -54,7 +52,7 @@ def tile_list_entity_merge_scores_kernel(
         lists = ctx.enter_context(tc.tile_pool(name="lists", bufs=1))
         keep = ctx.enter_context(tc.tile_pool(name="keep", bufs=1))
         placed_pool = ctx.enter_context(tc.tile_pool(name="placed", bufs=1))
-        ring = ctx.enter_context(tc.tile_pool(name="ring", bufs=3))
+        ring = ctx.enter_context(tc.tile_pool(name="ring", bufs=4))
         psum_p = ctx.enter_context(tc.psum_pool(name="psum_p", bufs=4))
         psum_qo = ctx.enter_context(tc.psum_pool(name="psum_qo", bufs=4))
 
@@ -68,31 +66,29 @@ def tile_list_entity_merge_scores_kernel(
         idx2 = lists.tile([P, S // PER_COLUMN], U16, name="idx2")
 
         tab2_s = held("tab2_s", [P, T2 // 4], I32)
+        tab_s = placed("tab_s", [P, T // 4], I32)
+        w2_raw_s = placed("w2_raw_s", [P, H // 4], I32)
+        w2_raw_w = held("w2_raw_w", [P, H // 2], I32)
+        v2_picked = placed("v2_picked", [P, S], U8)
+        planes = held("planes", [P, (S + H) // 4], I32)
+        plane_bytes = planes[:].bitcast(U8)
+        v2_s, w2_s = plane_bytes[:, :S], plane_bytes[:, S:]
+        w2_w = held("w2_w", [P, 2 * H], U8)
         v_w = [held("v_w%d" % k, [P, S], U32) for k in range(2)]
         v_s = held("v_s", [P, S], U8)
         v2_w = held("v2_w", [P, S], U32)
-        v2_spread = placed("v2_spread", [P, S], U8)
-        planes_in_place = held("planes_in_place", [P, SCALE_BYTES // 4], I32)
-        scale_bytes = planes_in_place[:].bitcast(U8)
-        v2_s, w2_s = scale_bytes[:, :S], scale_bytes[:, S:]
-        tab_s = placed("tab_s", [P, T // 4], I32)
-        w2_raw_w = held("w2_raw_w", [P, H // 2], I32)
-        w2_raw_s = held("w2_raw_s", [P, H // 4], I32)
-        w2_w = held("w2_w", [P, 2 * H], U8)
-        w1_bf = [[held("w1_bf%d%d" % (a, k), [P, PACK * PASS], BF16) for k in range(2)] for a in range(2)]
-        w1_w = [[held("w1_w%d%d" % (a, k), [P, PASS], U32) for k in range(2)] for a in range(2)]
-        h_w = [held("h_w%d" % a, [P, S], U32) for a in range(2)]
-        h_s = [[held("h_s%d%d" % (a, half), [P, BANK], U8) for half in range(2)] for a in range(2)]
-        w1_s = [[held("w1_s0%d" % k, [P, PASS], U8)[:] for k in range(2)], [h_s[0][0][4:, :], h_s[0][0][8:, :]]]
+        w1_w = [held("w1_w%d" % a, [P, 2, PASS], U32) for a in range(2)]
+        w1_s = [held("w1_s%d" % a, [P, 2, PASS], U8) for a in range(2)]
         gain_sb = held("gain_sb", [P, 2, PACK], F32)
-        gain_recip = placed("gain_recip", [P, 2, PACK], F32)[:]
+        gain_recip = held("gain_recip", [P, 2, PACK], F32)
         gain_inv = held("gain_inv", [P, 2, PACK], F32)
         gq = {}
         late = {}
 
-        def load_rows_by_quadrant(tile, source):
+        def load_rows_by_quadrant(tile, first, source):
             for quad in (0, 2, 1, 3):
-                nc.sync.dma_start(out=tile[32 * quad : 32 * quad + 8], in_=source[:, 4 * quad : 4 * quad + 4, :].bitcast(I32))
+                rows = tile[32 * quad + first : 32 * quad + first + 8]
+                nc.sync.dma_start(out=rows, in_=source[:, 4 * quad : 4 * quad + 4, :].bitcast(I32))
 
         def load_tab(k):
             late["tab", k] = placed("tab_w%d" % k, [P, T], I32)
@@ -113,20 +109,16 @@ def tile_list_entity_merge_scores_kernel(
                 in_=loaded.rearrange("p (a m t) -> p a t m", a=2, t=PACK),
             )
 
-        def round_w1(a, k, copies):
-            rounded = w1_bf[a][k][:].rearrange("p (t m j) -> p m j t", t=PACK, j=PACK)
+        def round_w1(rounded, a, k, copies):
+            rounded = rounded.rearrange("p (t m j) -> p m j t", t=PACK, j=PACK)
             loaded = late["w1", a, k][:].rearrange("p j (m t) -> p m j t", t=PACK)
             width = P // len(copies)
             for i, copy in enumerate(copies):
                 copy(out=rounded[:, i * width : (i + 1) * width], in_=loaded[:, i * width : (i + 1) * width])
 
-        def quantize_w1(a, k):
-            nc.vector.quantize_mx(out=w1_w[a][k][:].bitcast(FP8X4), scales=w1_s[a][k], in_=w1_bf[a][k][:])
-
         def project_candidates(a, half):
             cols = slice(half * BANK, (half + 1) * BANK)
-            name = "gq%d%d" % (a, half)
-            gq[a, half] = (placed if name in PLACE else held)(name, [P, PACK, BANK], F32)
+            gq[a, half] = held("gq%d%d" % (a, half), [P, PACK, BANK], F32)
             for t in range(PACK):
                 r0 = a * PASS + t * P
                 bank = psum_qo.tile([P, BANK], F32, name="qo")
@@ -148,20 +140,17 @@ def tile_list_entity_merge_scores_kernel(
             diff = ring.tile([P, PACK, width], F32, name="diff", align_bytes=64)
             dist = ring.tile([P, 2, width, 2], F32, name="dist", align_bytes=64)
             prod = ring.tile([P, 2, width, 2], F32, name="prod", align_bytes=64)
-            in_pairs = "p (u e) n -> p u n e"
             by_twos = "p e (c i) -> p c e i"
             banks = []
             for t0 in range(0, PACK, per_bank):
-                planes = slice(t0, t0 + per_bank)
-                pairs = slice(t0 // 2, (t0 + per_bank) // 2)
                 bank = psum_p.tile([P, per_bank, width], F32, name="pp")
-                banks.append((bank, planes, pairs))
+                banks.append(bank)
                 for t in range(t0, t0 + per_bank):
                     for k in range(2):
                         nc.tensor.matmul_mx(
                             out=bank[:, t - t0, :],
-                            lhsT=w1_w[a][k][:, t * P : (t + 1) * P].bitcast(FP8X4),
-                            lhsT_scale=w1_s[a][k][:, t * P : (t + 1) * P],
+                            lhsT=w1_w[a][:, k, t * P : (t + 1) * P].bitcast(FP8X4),
+                            lhsT_scale=w1_s[a][:, k, t * P : (t + 1) * P],
                             rhs=v_w[k][:, cols].bitcast(FP8X4),
                             rhs_scale=v_s[4 * k :, cols],
                             start=(k == 0),
@@ -176,16 +165,19 @@ def tile_list_entity_merge_scores_kernel(
                         op0=ALU.mult,
                         op1=ALU.subtract,
                     )
-                nc.scalar.activation(out=dist[:, pairs, :, :], in_=diff[:, planes, :].rearrange(in_pairs, e=2), func=ACT.Abs)
-            for bank, planes, pairs in banks:
-                for u in range(pairs.start, pairs.stop):
-                    pair = slice(2 * u - planes.start, 2 * u - planes.start + 2)
-                    nc.vector.tensor_tensor(
-                        out=prod[:, u, :, :].rearrange("p (c i) e -> p c e i", i=2),
-                        in0=gq_chunk[:, 2 * u : 2 * u + 2, :].rearrange(by_twos, i=2),
-                        in1=bank[:, pair, :].rearrange(by_twos, i=2),
-                        op=ALU.mult,
-                    )
+                nc.scalar.activation(
+                    out=dist[:, t0 // 2 : (t0 + per_bank) // 2, :, :],
+                    in_=diff[:, t0 : t0 + per_bank, :].rearrange("p (u e) n -> p u n e", e=2),
+                    func=ACT.Abs,
+                )
+            for u in range(2):
+                e0 = 2 * u % per_bank
+                nc.vector.tensor_tensor(
+                    out=prod[:, u, :, :].rearrange("p (c i) e -> p c e i", i=2),
+                    in0=gq_chunk[:, 2 * u : 2 * u + 2, :].rearrange(by_twos, i=2),
+                    in1=banks[2 * u // per_bank][:, e0 : e0 + 2, :].rearrange(by_twos, i=2),
+                    op=ALU.mult,
+                )
             return prod[:], dist[:]
 
         def pair_feature(engine, h_bf, terms):
@@ -197,20 +189,30 @@ def tile_list_entity_merge_scores_kernel(
                 op=ALU.mult,
             )
 
-        def quantize_h(a, j0, width, h_bf):
-            scales = h_s[a][j0 // BANK][:, j0 % BANK : j0 % BANK + width]
-            nc.vector.quantize_mx(out=h_w[a][:, j0 : j0 + width].bitcast(FP8X4), scales=scales, in_=h_bf)
+        def rounded_tile(width):
+            return keep.tile([P, width], BF16, name="rounded", tag="rounded", align_bytes=64)
 
-        def score_pass(bank, a, n0, j0):
-            per_bank, width = bank.shape[1], bank.shape[2]
+        h_codes = {}
+
+        def quantize_h(keys, width, h_bf):
+            name = "h" + "_".join("%d_%d" % key for key in keys)
+            words = held(name + "_w", [P, len(keys) * width], U32)
+            scales = held(name + "_s", [P, len(keys) * width], U8)
+            nc.vector.quantize_mx(out=words[:].bitcast(FP8X4), scales=scales[:], in_=h_bf)
+            for i, key in enumerate(keys):
+                h_codes[key] = (words[:, i * width : (i + 1) * width], scales[:, i * width : (i + 1) * width])
+
+        def score_pass(bank, a, n0, codes):
+            per_bank = bank.shape[1]
+            words, scales = codes
             for g in range(per_bank):
                 ncols = slice((n0 + g) * P, (n0 + g + 1) * P)
                 nc.tensor.matmul_mx(
                     out=bank[:, g, :],
                     lhsT=late["wm"][:, a, ncols].bitcast(FP8X4),
-                    lhsT_scale=late["wm_s"][:].bitcast(U8)[4 * a :, ncols],
-                    rhs=h_w[a][:, j0 : j0 + width].bitcast(FP8X4),
-                    rhs_scale=h_s[a][j0 // BANK][:, j0 % BANK : j0 % BANK + width],
+                    lhsT_scale=plane_bytes[4 + 4 * a :, ncols],
+                    rhs=words.bitcast(FP8X4),
+                    rhs_scale=scales,
                     start=(a == 0 and g == 0),
                     stop=(a == 1 and g == per_bank - 1),
                 )
@@ -222,115 +224,108 @@ def tile_list_entity_merge_scores_kernel(
             rows = out[n0 * P : (n0 + per_bank) * P, j0 : j0 + width]
             nc.sync.dma_start(out=rows.rearrange("(g p) j -> p g j", p=P), in_=staged[:])
 
-        def scores(j0):
-            for n0 in (0, 2, 4):
-                bank = psum_qo.tile([P, 2, STEP], F32, name="qo")
+        def scores(j0, width, copies):
+            per_bank = N // P // len(copies)
+            for i, copy in enumerate(copies):
+                bank = psum_qo.tile([P, per_bank, width], F32, name="qo")
                 for a in range(2):
-                    score_pass(bank, a, n0, j0)
-                store_scores(bank, n0, j0, nc.scalar.copy)
+                    score_pass(bank, a, i * per_bank, h_codes[a, j0])
+                store_scores(bank, i * per_bank, j0, copy)
 
-        for tile in (tab2_s, tab_s, planes_in_place):
-            nc.vector.memset(tile[:], 0)
-
-        nc.sync.dma_start(out=gain_sb[:], in_=gain.rearrange("(a p t) -> p a t", a=2, t=PACK))
+        nc.vector.memset(tab_s[:], 0)
+        nc.vector.memset(w2_raw_s[:TOP], 0)
+        nc.vector.memset(tab2_s[:TOP], 0)
         nc.sync.dma_start(idx2[:], offs2)
-        nc.sync.dma_start(idx[:], offs)
-        spread = held("spread", [P, SCALE_BYTES // 4], I32)
-        nc.sync.dma_start(out=w2_raw_s[:], in_=w2_scales[0].bitcast(I32).unsqueeze(1).broadcast_to([16, 8, H // 4]))
+        nc.sync.dma_start(out=tab2_s[TOP:], in_=tab2_scales[0].bitcast(I32))
+        nc.sync.dma_start(out=w2_raw_s[TOP:], in_=w2_scales[0].bitcast(I32))
         nc.sync.dma_start(out=w2_raw_w[:], in_=w2_words[0].bitcast(I32))
-        nc.sync.dma_start(out=tab2_s[0:P:8], in_=tab2_scales[0].bitcast(I32))
-        load_rows_by_quadrant(tab_s, tab_scales)
-        nc.vector.reciprocal(out=gain_recip, in_=gain_sb[:])
-        nc.vector.tensor_scalar(out=gain_inv[:], in0=gain_recip, scalar1=BIG, scalar2=-BIG, op0=ALU.min, op1=ALU.max)
+        nc.sync.dma_start(idx[:], offs)
+        nc.sync.dma_start(out=gain_sb[:], in_=gain.rearrange("(a p t) -> p a t", a=2, t=PACK))
         tab2_w = placed("tab2_w", [P, T2], I32)
         nc.sync.dma_start(out=tab2_w[:], in_=tab2_words[0].rearrange("p t i -> p (t i)").bitcast(I32))
-        reorder_w2(spread[:].bitcast(U8)[:, S : S + H], w2_raw_s[:].bitcast(U8))
-        gather(v2_spread, tab2_s, U8, idx2, 0, S)
-        nc.vector.tensor_copy(out=spread[:, : S // 4], in_=v2_spread[:].bitcast(I32))
-        for r in range(4):
-            nc.sync.dma_start(out=planes_in_place[r:P:32], in_=spread[8 * r : P : 32])
-        load_w1(0, 0)
+        load_rows_by_quadrant(tab_s, 0, tab_scales)
+
+        reorder_w2(w2_s, w2_raw_s[:].bitcast(U8))
         load_tab(0)
+        gather(v2_picked, tab2_s, U8, idx2, 0, S)
+        nc.vector.tensor_copy(out=planes[:, : S // 4], in_=v2_picked[:].bitcast(I32))
+        for quad in (0, 2, 1, 3):
+            nc.sync.dma_start(out=planes[32 * quad : 32 * quad + 4], in_=planes[TOP + 4 * quad : TOP + 4 * quad + 4])
+        load_w1(0, 0)
         reorder_w2(w2_w[:].bitcast(U16), w2_raw_w[:].bitcast(U16))
-        gather(v_s, tab_s, U8, idx, 0, S)
-        load_w1(0, 1)
-        load_tab(1)
+        nc.vector.reciprocal(out=gain_recip[:], in_=gain_sb[:])
+        nc.vector.tensor_scalar(out=gain_inv[:], in0=gain_recip[:], scalar1=BIG, scalar2=-BIG, op0=ALU.min, op1=ALU.max)
         gather(v2_w, tab2_w, U32, idx2, 0, BANK)
         gather(v2_w, tab2_w, U32, idx2, BANK, BANK)
-        load_w1(1, 0)
-        load_w1(1, 1)
+        load_w1(0, 1)
+        load_tab(1)
         project_candidates(0, 0)
-        round_w1(0, 0, [nc.vector.tensor_copy])
+        gather(v_s, tab_s, U8, idx, 0, S)
+        load_w1(1, 0)
+        gather(v_w[0], late["tab", 0], U32, idx, 0, S)
+        load_w1(1, 1)
+        first = [held("w1_bf0%d" % k, [P, PACK * PASS], BF16) for k in range(2)]
+        round_w1(first[0][:], 0, 0, [nc.scalar.copy] * 4)
+        round_w1(first[1][:], 0, 1, [nc.vector.tensor_copy])
         late["wm"] = placed("wm_w", [P, 2, N], I32)
         nc.sync.dma_start(out=late["wm"][:], in_=wm_words.rearrange("a p n i -> p a (n i)").bitcast(I32))
-        late["wm_s"] = placed("wm_s", [P, N // 4], I32)
-        nc.vector.memset(late["wm_s"][:], 0)
-        load_rows_by_quadrant(late["wm_s"], wm_scales)
-        quantize_w1(0, 0)
-        gather(v_w[0], late["tab", 0], U32, idx, 0, S)
-        round_w1(0, 1, [nc.scalar.copy, nc.vector.tensor_copy])
-        quantize_w1(0, 1)
-        project_candidates(0, 1)
+        for k in range(2):
+            nc.vector.quantize_mx(out=w1_w[0][:, k, :].bitcast(FP8X4), scales=w1_s[0][:, k, :], in_=first[k][:])
         for j0, width in ((0, STEP), (STEP, S - STEP)):
             gather(v_w[1], late["tab", 1], U32, idx, j0, width)
 
-        def h_tile():
-            return keep.tile([P, PACK * BANK], BF16, name="h_bf", tag="h_bf", align_bytes=64)
-
         FINAL = nc.gpsimd
-        step0 = pair_terms(0, 0, STEP)
-        step1 = pair_terms(0, STEP, STEP)
-        h_bf = h_tile()
-        pair_feature(FINAL, h_bf[:, : PACK * STEP], step0)
-        round_w1(1, 0, [nc.scalar.copy] * 4)
-        step2 = pair_terms(0, 2 * STEP, STEP)
-        pair_feature(FINAL, h_bf[:, PACK * STEP :], step1)
-        round_w1(1, 1, [nc.scalar.copy] * 4)
+        WIDE = PACK * STEP
+        SLIM = PACK * NARROW
+        c0, c1, c2, c3, c4 = 0, STEP, 2 * STEP, 3 * STEP, 3 * STEP + NARROW
+        by_scalar = nc.scalar.copy
+        a0 = pair_terms(0, c0, STEP)
+        project_candidates(0, 1)
+        a1 = pair_terms(0, c1, STEP)
+        second = held("w1_bf1", [P, 2 * PACK * PASS], BF16)
+        round_w1(second[:, : PACK * PASS], 1, 0, [by_scalar] * 4)
+        round_w1(second[:, PACK * PASS :], 1, 1, [by_scalar] * 4)
+        a2 = pair_terms(0, c2, STEP)
         project_candidates(1, 0)
-        quantize_h(0, 0, BANK, h_bf[:])
-        for k in range(2):
-            quantize_w1(1, k)
-        step3 = pair_terms(0, 3 * STEP, STEP)
+        h_bf = rounded_tile(2 * WIDE)
+        pair_feature(FINAL, h_bf[:, :WIDE], a0)
+        pair_feature(FINAL, h_bf[:, WIDE:], a1)
+        nc.vector.quantize_mx(
+            out=w1_w[1][:].rearrange("p k c -> p (k c)").bitcast(FP8X4),
+            scales=w1_s[1][:].rearrange("p k c -> p (k c)"),
+            in_=second[:],
+        )
+        quantize_h([(0, c0), (0, c1)], STEP, h_bf[:])
+        a3 = pair_terms(0, c3, NARROW)
+        b0 = pair_terms(1, c0, STEP)
         project_candidates(1, 1)
-        h_bf = h_tile()
-        pair_feature(FINAL, h_bf[:, : PACK * STEP], step2)
-        step4 = pair_terms(1, 0, STEP)
-        pair_feature(FINAL, h_bf[:, PACK * STEP :], step3)
-        quantize_h(0, BANK, BANK, h_bf[:])
-        step5 = pair_terms(1, STEP, STEP)
-        h_bf = h_tile()
-        pair_feature(FINAL, h_bf[:, : PACK * STEP], step4)
-        quantize_h(1, 0, STEP, h_bf[:, : PACK * STEP])
-        step6 = pair_terms(1, 2 * STEP, STEP)
-        scores(0)
-        h_bf = h_tile()
-        pair_feature(FINAL, h_bf[:, : PACK * STEP], step5)
-        quantize_h(1, STEP, STEP, h_bf[:, : PACK * STEP])
-        step7 = pair_terms(1, 3 * STEP, STEP)
-        last = [[term[:, :, i * NARROW : (i + 1) * NARROW, :] for term in step7] for i in range(2)]
-        scores(STEP)
-        h_bf = h_tile()
-        pair_feature(FINAL, h_bf[:, : PACK * STEP], step6)
-        wide = [(psum_qo.tile([P, 2, STEP], F32, name="qo"), n0) for n0 in (0, 2, 4)]
-        narrow = [
-            [(psum_qo.tile([P, 3, NARROW], F32, name="qo"), 0), (psum_p.tile([P, 3, NARROW], F32, name="pp"), 3)],
-            [(psum_p.tile([P, 3, NARROW], F32, name="pp"), n0) for n0 in (0, 3)],
-        ]
-        for bank, n0 in wide:
-            score_pass(bank, 0, n0, 2 * STEP)
-        for i in range(2):
-            for bank, n0 in narrow[i]:
-                score_pass(bank, 0, n0, 3 * STEP + i * NARROW)
-        quantize_h(1, 2 * STEP, STEP, h_bf[:, : PACK * STEP])
-        for bank, n0 in wide:
-            score_pass(bank, 1, n0, 2 * STEP)
-            store_scores(bank, n0, 2 * STEP, nc.scalar.copy)
-        h_bf = h_tile()
-        for i in range(2):
-            pair_feature(nc.vector, h_bf[:, i * PACK * NARROW : (i + 1) * PACK * NARROW], last[i])
-        for i in range(2):
-            j0 = 3 * STEP + i * NARROW
-            quantize_h(1, j0, NARROW, h_bf[:, i * PACK * NARROW : (i + 1) * PACK * NARROW])
-            for bank, n0 in narrow[i]:
-                score_pass(bank, 1, n0, j0)
-                store_scores(bank, n0, j0, nc.vector.tensor_copy if n0 == 3 else nc.scalar.copy)
+        load_rows_by_quadrant(planes[:, : N // 4], 4, wm_scales)
+        h_bf = rounded_tile(2 * WIDE + SLIM)
+        pair_feature(FINAL, h_bf[:, :WIDE], a2)
+        pair_feature(FINAL, h_bf[:, 2 * WIDE :], a3)
+        b1 = pair_terms(1, c1, STEP)
+        pair_feature(FINAL, h_bf[:, WIDE : 2 * WIDE], b0)
+        quantize_h([(0, c2), (1, c0)], STEP, h_bf[:, : 2 * WIDE])
+        quantize_h([(0, c3)], NARROW, h_bf[:, 2 * WIDE :])
+        b2 = pair_terms(1, c2, STEP)
+        scores(c0, STEP, [by_scalar] * 3)
+        h_bf = rounded_tile(WIDE)
+        pair_feature(FINAL, h_bf[:], b1)
+        quantize_h([(1, c1)], STEP, h_bf[:])
+        b3 = pair_terms(1, c3, NARROW)
+        a4 = pair_terms(0, c4, NARROW)
+        scores(c1, STEP, [by_scalar] * 3)
+        h_bf = rounded_tile(WIDE)
+        pair_feature(FINAL, h_bf[:], b2)
+        quantize_h([(1, c2)], STEP, h_bf[:])
+        b4 = pair_terms(1, c4, NARROW)
+        scores(c2, STEP, [by_scalar] * 3)
+        h_bf = rounded_tile(SLIM)
+        pair_feature(FINAL, h_bf[:], b3)
+        quantize_h([(1, c3)], NARROW, h_bf[:])
+        h_bf = rounded_tile(2 * SLIM)
+        pair_feature(nc.vector, h_bf[:, :SLIM], a4)
+        pair_feature(nc.vector, h_bf[:, SLIM:], b4)
+        quantize_h([(0, c4), (1, c4)], NARROW, h_bf[:])
+        scores(c3, NARROW, [by_scalar, nc.vector.tensor_copy])
+        scores(c4, NARROW, [by_scalar, nc.vector.tensor_copy])

@@ -30,17 +30,17 @@ NARROW = 128
 
 UNIT = 8192
 PLACE = {
-    "w2_raw_s": 0,
-    "tab_w0": 0,
-    "v2_picked": UNIT,
-    "w1_raw00": UNIT,
-    "tab2_w": 2 * UNIT,
-    "w1_raw01": 2 * UNIT,
-    "tab_w1": 3 * UNIT,
-    "tab_s": 4 * UNIT,
-    "w1_raw10": 4 * UNIT,
-    "w1_raw11": 0,
-    "wm_w": 2 * UNIT,
+    "tab2_w": 0,
+    "w1_raw10": 0,
+    "w1_raw11": UNIT,
+    "w1_raw00": 2 * UNIT,
+    "v2_picked": 3 * UNIT,
+    "tab_w0": 3 * UNIT,
+    "w1_raw01": 4 * UNIT,
+    "wm_w": 3 * UNIT,
+    "gq10": 4 * UNIT,
+    "tab_s": 5 * UNIT - T // 2,
+    "tab_w1": 5 * UNIT,
 }
 
 
@@ -67,7 +67,7 @@ def tile_list_entity_merge_scores_kernel(
 
         tab2_s = held("tab2_s", [P, T2 // 4], I32)
         tab_s = placed("tab_s", [P, T // 4], I32)
-        w2_raw_s = placed("w2_raw_s", [P, H // 4], I32)
+        w2_raw_s = held("w2_raw_s", [P, H // 4], I32)
         w2_raw_w = held("w2_raw_w", [P, H // 2], I32)
         v2_picked = placed("v2_picked", [P, S], U8)
         planes = held("planes", [P, (S + H) // 4], I32)
@@ -75,10 +75,13 @@ def tile_list_entity_merge_scores_kernel(
         v2_s, w2_s = plane_bytes[:, :S], plane_bytes[:, S:]
         w2_w = held("w2_w", [P, 2 * H], U8)
         v_w = [held("v_w%d" % k, [P, S], U32) for k in range(2)]
-        v_s = held("v_s", [P, S], U8)
+        v_picked = held("v_picked", [P, S // 4], I32)
+        v_planes = held("v_planes", [P, S // 4], I32)
+        v_s = v_planes[:].bitcast(U8)
         v2_w = held("v2_w", [P, S], U32)
         w1_w = [held("w1_w%d" % a, [P, 2, PASS], U32) for a in range(2)]
-        w1_s = [held("w1_s%d" % a, [P, 2, PASS], U8) for a in range(2)]
+        first_scales = held("first_scales", [P, BANK], U8)
+        w1_s = [[held("w1_s0%d" % k, [P, PASS], U8)[:] for k in range(2)], [first_scales[4:, :], first_scales[8:, :]]]
         gain_sb = held("gain_sb", [P, 2, PACK], F32)
         gain_recip = held("gain_recip", [P, 2, PACK], F32)
         gain_inv = held("gain_inv", [P, 2, PACK], F32)
@@ -118,7 +121,8 @@ def tile_list_entity_merge_scores_kernel(
 
         def project_candidates(a, half):
             cols = slice(half * BANK, (half + 1) * BANK)
-            gq[a, half] = held("gq%d%d" % (a, half), [P, PACK, BANK], F32)
+            name = "gq%d%d" % (a, half)
+            gq[a, half] = (placed if name in PLACE else held)(name, [P, PACK, BANK], F32)
             for t in range(PACK):
                 r0 = a * PASS + t * P
                 bank = psum_qo.tile([P, BANK], F32, name="qo")
@@ -145,16 +149,16 @@ def tile_list_entity_merge_scores_kernel(
             for t0 in range(0, PACK, per_bank):
                 bank = psum_p.tile([P, per_bank, width], F32, name="pp")
                 banks.append(bank)
-                for t in range(t0, t0 + per_bank):
-                    for k in range(2):
+                for k in range(2):
+                    for t in range(t0, t0 + per_bank):
                         nc.tensor.matmul_mx(
                             out=bank[:, t - t0, :],
                             lhsT=w1_w[a][:, k, t * P : (t + 1) * P].bitcast(FP8X4),
-                            lhsT_scale=w1_s[a][:, k, t * P : (t + 1) * P],
+                            lhsT_scale=w1_s[a][k][:, t * P : (t + 1) * P],
                             rhs=v_w[k][:, cols].bitcast(FP8X4),
                             rhs_scale=v_s[4 * k :, cols],
-                            start=(k == 0),
-                            stop=(k == 1),
+                            start=(k == 0 and t == t0),
+                            stop=(k == 1 and t == t0 + per_bank - 1),
                         )
                 for t in range(t0, t0 + per_bank):
                     nc.vector.scalar_tensor_tensor(
@@ -194,10 +198,10 @@ def tile_list_entity_merge_scores_kernel(
 
         h_codes = {}
 
-        def quantize_h(keys, width, h_bf):
+        def quantize_h(keys, width, h_bf, scales=None):
             name = "h" + "_".join("%d_%d" % key for key in keys)
             words = held(name + "_w", [P, len(keys) * width], U32)
-            scales = held(name + "_s", [P, len(keys) * width], U8)
+            scales = scales if scales is not None else held(name + "_s", [P, len(keys) * width], U8)
             nc.vector.quantize_mx(out=words[:].bitcast(FP8X4), scales=scales[:], in_=h_bf)
             for i, key in enumerate(keys):
                 h_codes[key] = (words[:, i * width : (i + 1) * width], scales[:, i * width : (i + 1) * width])
@@ -232,47 +236,66 @@ def tile_list_entity_merge_scores_kernel(
                     score_pass(bank, a, i * per_bank, h_codes[a, j0])
                 store_scores(bank, i * per_bank, j0, copy)
 
-        nc.vector.memset(tab_s[:], 0)
+        LOW = P - 2 * ROWS
+
+        def move_v_scales(k):
+            for quad in (0, 2, 1, 3):
+                source = LOW + ROWS * k + 4 * quad
+                nc.sync.dma_start(out=v_planes[32 * quad + 4 * k : 32 * quad + 4 * k + 4], in_=v_picked[source : source + 4])
+
+        def quantize_w1(a, k, rounded):
+            nc.vector.quantize_mx(out=w1_w[a][:, k, :].bitcast(FP8X4), scales=w1_s[a][k], in_=rounded)
+
         nc.vector.memset(w2_raw_s[:TOP], 0)
         nc.vector.memset(tab2_s[:TOP], 0)
+        nc.vector.memset(tab_s[:LOW], 0)
+        nc.vector.memset(v_planes[:], 0)
         nc.sync.dma_start(idx2[:], offs2)
         nc.sync.dma_start(out=tab2_s[TOP:], in_=tab2_scales[0].bitcast(I32))
         nc.sync.dma_start(out=w2_raw_s[TOP:], in_=w2_scales[0].bitcast(I32))
-        nc.sync.dma_start(out=w2_raw_w[:], in_=w2_words[0].bitcast(I32))
         nc.sync.dma_start(idx[:], offs)
+        nc.sync.dma_start(out=tab_s[LOW:], in_=tab_scales.rearrange("a q t -> (a q) t").bitcast(I32))
+        nc.sync.dma_start(out=w2_raw_w[:], in_=w2_words[0].bitcast(I32))
         nc.sync.dma_start(out=gain_sb[:], in_=gain.rearrange("(a p t) -> p a t", a=2, t=PACK))
+        load_w1(0, 0)
         tab2_w = placed("tab2_w", [P, T2], I32)
         nc.sync.dma_start(out=tab2_w[:], in_=tab2_words[0].rearrange("p t i -> p (t i)").bitcast(I32))
-        load_rows_by_quadrant(tab_s, 0, tab_scales)
 
         reorder_w2(w2_s, w2_raw_s[:].bitcast(U8))
-        load_tab(0)
         gather(v2_picked, tab2_s, U8, idx2, 0, S)
         nc.vector.tensor_copy(out=planes[:, : S // 4], in_=v2_picked[:].bitcast(I32))
         for quad in (0, 2, 1, 3):
             nc.sync.dma_start(out=planes[32 * quad : 32 * quad + 4], in_=planes[TOP + 4 * quad : TOP + 4 * quad + 4])
-        load_w1(0, 0)
+        load_tab(0)
+        gather(v_picked[:].bitcast(U8), tab_s, U8, idx, 0, S)
+        move_v_scales(0)
+        load_tab(1)
+        move_v_scales(1)
+        load_w1(0, 1)
         reorder_w2(w2_w[:].bitcast(U16), w2_raw_w[:].bitcast(U16))
         nc.vector.reciprocal(out=gain_recip[:], in_=gain_sb[:])
         nc.vector.tensor_scalar(out=gain_inv[:], in0=gain_recip[:], scalar1=BIG, scalar2=-BIG, op0=ALU.min, op1=ALU.max)
+        rounded = {(a, k): held("w1_bf%d%d" % (a, k), [P, PACK * PASS], BF16)[:] for a in range(2) for k in range(2)}
+        round_w1(rounded[0, 0], 0, 0, [nc.scalar.copy])
+        quantize_w1(0, 0, rounded[0, 0])
         gather(v2_w, tab2_w, U32, idx2, 0, BANK)
         gather(v2_w, tab2_w, U32, idx2, BANK, BANK)
-        load_w1(0, 1)
-        load_tab(1)
-        project_candidates(0, 0)
-        gather(v_s, tab_s, U8, idx, 0, S)
         load_w1(1, 0)
-        gather(v_w[0], late["tab", 0], U32, idx, 0, S)
         load_w1(1, 1)
-        first = [held("w1_bf0%d" % k, [P, PACK * PASS], BF16) for k in range(2)]
-        round_w1(first[0][:], 0, 0, [nc.scalar.copy] * 4)
-        round_w1(first[1][:], 0, 1, [nc.vector.tensor_copy])
+        project_candidates(0, 0)
+        gather(v_w[0], late["tab", 0], U32, idx, 0, S)
         late["wm"] = placed("wm_w", [P, 2, N], I32)
         nc.sync.dma_start(out=late["wm"][:], in_=wm_words.rearrange("a p n i -> p a (n i)").bitcast(I32))
-        for k in range(2):
-            nc.vector.quantize_mx(out=w1_w[0][:, k, :].bitcast(FP8X4), scales=w1_s[0][:, k, :], in_=first[k][:])
-        for j0, width in ((0, STEP), (STEP, S - STEP)):
-            gather(v_w[1], late["tab", 1], U32, idx, j0, width)
+        gather(v_w[1], late["tab", 1], U32, idx, 0, S)
+        round_w1(rounded[0, 1], 0, 1, [nc.scalar.copy, nc.vector.tensor_copy])
+        for half in range(2):
+            cols = slice(half * PASS // 2, (half + 1) * PASS // 2)
+            nc.vector.quantize_mx(
+                out=w1_w[0][:, 1, cols].bitcast(FP8X4),
+                scales=w1_s[0][1][:, cols],
+                in_=rounded[0, 1][:, half * 2 * PASS : (half + 1) * 2 * PASS],
+            )
+        project_candidates(0, 1)
 
         FINAL = nc.gpsimd
         WIDE = PACK * STEP
@@ -280,52 +303,56 @@ def tile_list_entity_merge_scores_kernel(
         c0, c1, c2, c3, c4 = 0, STEP, 2 * STEP, 3 * STEP, 3 * STEP + NARROW
         by_scalar = nc.scalar.copy
         a0 = pair_terms(0, c0, STEP)
-        project_candidates(0, 1)
         a1 = pair_terms(0, c1, STEP)
-        second = held("w1_bf1", [P, 2 * PACK * PASS], BF16)
-        round_w1(second[:, : PACK * PASS], 1, 0, [by_scalar] * 4)
-        round_w1(second[:, PACK * PASS :], 1, 1, [by_scalar] * 4)
-        a2 = pair_terms(0, c2, STEP)
-        project_candidates(1, 0)
         h_bf = rounded_tile(2 * WIDE)
         pair_feature(FINAL, h_bf[:, :WIDE], a0)
+        round_w1(rounded[1, 0], 1, 0, [by_scalar] * 4)
+        a2 = pair_terms(0, c2, STEP)
         pair_feature(FINAL, h_bf[:, WIDE:], a1)
-        nc.vector.quantize_mx(
-            out=w1_w[1][:].rearrange("p k c -> p (k c)").bitcast(FP8X4),
-            scales=w1_s[1][:].rearrange("p k c -> p (k c)"),
-            in_=second[:],
-        )
-        quantize_h([(0, c0), (0, c1)], STEP, h_bf[:])
-        a3 = pair_terms(0, c3, NARROW)
-        b0 = pair_terms(1, c0, STEP)
+        round_w1(rounded[1, 1], 1, 1, [by_scalar] * 4)
+        project_candidates(1, 0)
+        quantize_h([(0, c0), (0, c1)], STEP, h_bf[:], first_scales)
+        for k in range(2):
+            quantize_w1(1, k, rounded[1, k])
+        a3 = pair_terms(0, c3, STEP)
         project_candidates(1, 1)
         load_rows_by_quadrant(planes[:, : N // 4], 4, wm_scales)
-        h_bf = rounded_tile(2 * WIDE + SLIM)
+        h_bf = rounded_tile(2 * WIDE)
         pair_feature(FINAL, h_bf[:, :WIDE], a2)
-        pair_feature(FINAL, h_bf[:, 2 * WIDE :], a3)
-        b1 = pair_terms(1, c1, STEP)
-        pair_feature(FINAL, h_bf[:, WIDE : 2 * WIDE], b0)
-        quantize_h([(0, c2), (1, c0)], STEP, h_bf[:, : 2 * WIDE])
-        quantize_h([(0, c3)], NARROW, h_bf[:, 2 * WIDE :])
-        b2 = pair_terms(1, c2, STEP)
-        scores(c0, STEP, [by_scalar] * 3)
-        h_bf = rounded_tile(WIDE)
-        pair_feature(FINAL, h_bf[:], b1)
-        quantize_h([(1, c1)], STEP, h_bf[:])
-        b3 = pair_terms(1, c3, NARROW)
-        a4 = pair_terms(0, c4, NARROW)
-        scores(c1, STEP, [by_scalar] * 3)
-        h_bf = rounded_tile(WIDE)
-        pair_feature(FINAL, h_bf[:], b2)
+        terms = pair_terms(1, c0, STEP)
+        pair_feature(FINAL, h_bf[:, WIDE:], a3)
+        quantize_h([(0, c2), (0, c3)], STEP, h_bf[:])
+        for j0 in (c0, c1, c2):
+            ahead = pair_terms(1, j0 + STEP, STEP)
+            if j0 > c0:
+                scores(j0 - STEP, STEP, [by_scalar] * 3)
+            h_bf = rounded_tile(WIDE)
+            pair_feature(FINAL, h_bf[:], terms)
+            if j0 < c2:
+                quantize_h([(1, j0)], STEP, h_bf[:])
+            terms = ahead
+        wide = [(psum_qo.tile([P, 2, STEP], F32, name="qo"), n0) for n0 in (0, 2, 4)]
+        narrow = [
+            [(psum_qo.tile([P, 3, NARROW], F32, name="qo"), 0), (psum_p.tile([P, 3, NARROW], F32, name="pp"), 3)],
+            [(psum_p.tile([P, 3, NARROW], F32, name="pp"), n0) for n0 in (0, 3)],
+        ]
+        for bank, n0 in wide:
+            score_pass(bank, 0, n0, h_codes[0, c2])
+        words, scales = h_codes[0, c3]
+        for i in range(2):
+            half = slice(i * NARROW, (i + 1) * NARROW)
+            for bank, n0 in narrow[i]:
+                score_pass(bank, 0, n0, (words[:, half], scales[:, half]))
         quantize_h([(1, c2)], STEP, h_bf[:])
-        b4 = pair_terms(1, c4, NARROW)
-        scores(c2, STEP, [by_scalar] * 3)
-        h_bf = rounded_tile(SLIM)
-        pair_feature(FINAL, h_bf[:], b3)
-        quantize_h([(1, c3)], NARROW, h_bf[:])
-        h_bf = rounded_tile(2 * SLIM)
-        pair_feature(nc.vector, h_bf[:, :SLIM], a4)
-        pair_feature(nc.vector, h_bf[:, SLIM:], b4)
-        quantize_h([(0, c4), (1, c4)], NARROW, h_bf[:])
-        scores(c3, NARROW, [by_scalar, nc.vector.tensor_copy])
-        scores(c4, NARROW, [by_scalar, nc.vector.tensor_copy])
+        for bank, n0 in wide:
+            score_pass(bank, 1, n0, h_codes[1, c2])
+            store_scores(bank, n0, c2, by_scalar)
+        h_bf = rounded_tile(WIDE)
+        for i in range(2):
+            half_terms = [term[:, :, i * NARROW : (i + 1) * NARROW, :] for term in terms]
+            pair_feature(nc.vector, h_bf[:, i * SLIM : (i + 1) * SLIM], half_terms)
+        for i, j0 in enumerate((c3, c4)):
+            quantize_h([(1, j0)], NARROW, h_bf[:, i * SLIM : (i + 1) * SLIM])
+            for bank, n0 in narrow[i]:
+                score_pass(bank, 1, n0, h_codes[1, j0])
+                store_scores(bank, n0, j0, nc.vector.tensor_copy if n0 == 3 else by_scalar)

@@ -38,7 +38,9 @@ PLACE = {
     "tab_w0": 3 * UNIT,
     "w1_raw01": 4 * UNIT,
     "wm_w": 3 * UNIT,
-    "gq10": 4 * UNIT,
+    "gq100": 4 * UNIT,
+    "gq101": UNIT,
+    "gq110": UNIT + UNIT // 2,
     "tab_s": 5 * UNIT - T // 2,
     "tab_w1": 5 * UNIT,
 }
@@ -80,8 +82,8 @@ def tile_list_entity_merge_scores_kernel(
         v_s = v_planes[:].bitcast(U8)
         v2_w = held("v2_w", [P, S], U32)
         w1_w = [held("w1_w%d" % a, [P, 2, PASS], U32) for a in range(2)]
-        first_scales = held("first_scales", [P, BANK], U8)
-        w1_s = [[held("w1_s0%d" % k, [P, PASS], U8)[:] for k in range(2)], [first_scales[4:, :], first_scales[8:, :]]]
+        w1_scales = [held("w1_s%d" % a, [P, 2, PASS], U8) for a in range(2)]
+        w1_s = [[w1_scales[a][:, k, :] for k in range(2)] for a in range(2)]
         gain_sb = held("gain_sb", [P, 2, PACK], F32)
         gain_recip = held("gain_recip", [P, 2, PACK], F32)
         gain_inv = held("gain_inv", [P, 2, PACK], F32)
@@ -121,9 +123,10 @@ def tile_list_entity_merge_scores_kernel(
 
         def project_candidates(a, half):
             cols = slice(half * BANK, (half + 1) * BANK)
-            name = "gq%d%d" % (a, half)
-            gq[a, half] = (placed if name in PLACE else held)(name, [P, PACK, BANK], F32)
             for t in range(PACK):
+                if t % 2 == 0:
+                    name = "gq%d%d%d" % (a, half, t // 2)
+                    gq[a, half, t // 2] = (placed if name in PLACE else held)(name, [P, 2, BANK], F32)
                 r0 = a * PASS + t * P
                 bank = psum_qo.tile([P, BANK], F32, name="qo")
                 nc.tensor.matmul_mx(
@@ -135,12 +138,12 @@ def tile_list_entity_merge_scores_kernel(
                     start=True,
                     stop=True,
                 )
-                nc.scalar.activation(out=gq[a, half][:, t, :], in_=bank[:], func=ACT.Copy, scale=gain_sb[:, a, t : t + 1])
+                nc.scalar.activation(out=gq[a, half, t // 2][:, t % 2, :], in_=bank[:], func=ACT.Copy, scale=gain_sb[:, a, t : t + 1])
 
         def pair_terms(a, j0, width):
             cols = slice(j0, j0 + width)
             per_bank = BANK // width
-            gq_chunk = gq[a, j0 // BANK][:, :, j0 % BANK : j0 % BANK + width]
+            gq_pair = [gq[a, j0 // BANK, u][:, :, j0 % BANK : j0 % BANK + width] for u in range(2)]
             diff = ring.tile([P, PACK, width], F32, name="diff", align_bytes=64)
             dist = ring.tile([P, 2, width, 2], F32, name="dist", align_bytes=64)
             prod = ring.tile([P, 2, width, 2], F32, name="prod", align_bytes=64)
@@ -163,7 +166,7 @@ def tile_list_entity_merge_scores_kernel(
                 for t in range(t0, t0 + per_bank):
                     nc.vector.scalar_tensor_tensor(
                         out=diff[:, t, :],
-                        in0=gq_chunk[:, t, :],
+                        in0=gq_pair[t // 2][:, t % 2, :],
                         scalar=gain_inv[:, a, t : t + 1],
                         in1=bank[:, t - t0, :],
                         op0=ALU.mult,
@@ -178,7 +181,7 @@ def tile_list_entity_merge_scores_kernel(
                 e0 = 2 * u % per_bank
                 nc.vector.tensor_tensor(
                     out=prod[:, u, :, :].rearrange("p (c i) e -> p c e i", i=2),
-                    in0=gq_chunk[:, 2 * u : 2 * u + 2, :].rearrange(by_twos, i=2),
+                    in0=gq_pair[u].rearrange(by_twos, i=2),
                     in1=banks[2 * u // per_bank][:, e0 : e0 + 2, :].rearrange(by_twos, i=2),
                     op=ALU.mult,
                 )
@@ -198,10 +201,10 @@ def tile_list_entity_merge_scores_kernel(
 
         h_codes = {}
 
-        def quantize_h(keys, width, h_bf, scales=None):
+        def quantize_h(keys, width, h_bf, slot=None):
             name = "h" + "_".join("%d_%d" % key for key in keys)
-            words = held(name + "_w", [P, len(keys) * width], U32)
-            scales = scales if scales is not None else held(name + "_s", [P, len(keys) * width], U8)
+            words = held(name + "_w", [P, len(keys) * width], U32, slot)
+            scales = held(name + "_s", [P, len(keys) * width], U8)
             nc.vector.quantize_mx(out=words[:].bitcast(FP8X4), scales=scales[:], in_=h_bf)
             for i, key in enumerate(keys):
                 h_codes[key] = (words[:, i * width : (i + 1) * width], scales[:, i * width : (i + 1) * width])
@@ -275,7 +278,9 @@ def tile_list_entity_merge_scores_kernel(
         reorder_w2(w2_w[:].bitcast(U16), w2_raw_w[:].bitcast(U16))
         nc.vector.reciprocal(out=gain_recip[:], in_=gain_sb[:])
         nc.vector.tensor_scalar(out=gain_inv[:], in0=gain_recip[:], scalar1=BIG, scalar2=-BIG, op0=ALU.min, op1=ALU.max)
-        rounded = {(a, k): held("w1_bf%d%d" % (a, k), [P, PACK * PASS], BF16)[:] for a in range(2) for k in range(2)}
+        second = held("w1_bf1", [P, 2, PACK * PASS], BF16)
+        rounded = {(0, k): held("w1_bf0%d" % k, [P, PACK * PASS], BF16)[:] for k in range(2)}
+        rounded.update({(1, k): second[:, k, :] for k in range(2)})
         round_w1(rounded[0, 0], 0, 0, [nc.scalar.copy])
         quantize_w1(0, 0, rounded[0, 0])
         gather(v2_w, tab2_w, U32, idx2, 0, BANK)
@@ -307,13 +312,16 @@ def tile_list_entity_merge_scores_kernel(
         h_bf = rounded_tile(2 * WIDE)
         pair_feature(FINAL, h_bf[:, :WIDE], a0)
         round_w1(rounded[1, 0], 1, 0, [by_scalar] * 4)
+        round_w1(rounded[1, 1], 1, 1, [by_scalar] * 4)
         a2 = pair_terms(0, c2, STEP)
         pair_feature(FINAL, h_bf[:, WIDE:], a1)
-        round_w1(rounded[1, 1], 1, 1, [by_scalar] * 4)
         project_candidates(1, 0)
-        quantize_h([(0, c0), (0, c1)], STEP, h_bf[:], first_scales)
-        for k in range(2):
-            quantize_w1(1, k, rounded[1, k])
+        nc.vector.quantize_mx(
+            out=w1_w[1][:].rearrange("p k c -> p (k c)").bitcast(FP8X4),
+            scales=w1_scales[1][:].rearrange("p k c -> p (k c)"),
+            in_=second[:].rearrange("p k c -> p (k c)"),
+        )
+        quantize_h([(0, c0), (0, c1)], STEP, h_bf[:], slot="w1_bf1")
         a3 = pair_terms(0, c3, STEP)
         project_candidates(1, 1)
         load_rows_by_quadrant(planes[:, : N // 4], 4, wm_scales)

@@ -322,45 +322,36 @@ def tile_list_entity_merge_scores_kernel(
             in_=second[:].rearrange("p k c -> p (k c)"),
         )
         quantize_h([(0, c0), (0, c1)], STEP, h_bf[:], slot="w1_bf1")
-        a3 = pair_terms(0, c3, STEP)
+        a3 = pair_terms(0, c3, NARROW)
+        b0 = pair_terms(1, c0, STEP)
         project_candidates(1, 1)
         load_rows_by_quadrant(planes[:, : N // 4], 4, wm_scales)
-        h_bf = rounded_tile(2 * WIDE)
+        h_bf = rounded_tile(2 * WIDE + SLIM)
         pair_feature(FINAL, h_bf[:, :WIDE], a2)
-        terms = pair_terms(1, c0, STEP)
-        pair_feature(FINAL, h_bf[:, WIDE:], a3)
-        quantize_h([(0, c2), (0, c3)], STEP, h_bf[:])
-        for j0 in (c0, c1, c2):
-            ahead = pair_terms(1, j0 + STEP, STEP)
-            if j0 > c0:
-                scores(j0 - STEP, STEP, [by_scalar] * 3)
-            h_bf = rounded_tile(WIDE)
-            pair_feature(FINAL, h_bf[:], terms)
-            if j0 < c2:
-                quantize_h([(1, j0)], STEP, h_bf[:])
-            terms = ahead
-        wide = [(psum_qo.tile([P, 2, STEP], F32, name="qo"), n0) for n0 in (0, 2, 4)]
-        narrow = [
-            [(psum_qo.tile([P, 3, NARROW], F32, name="qo"), 0), (psum_p.tile([P, 3, NARROW], F32, name="pp"), 3)],
-            [(psum_p.tile([P, 3, NARROW], F32, name="pp"), n0) for n0 in (0, 3)],
-        ]
-        for bank, n0 in wide:
-            score_pass(bank, 0, n0, h_codes[0, c2])
-        words, scales = h_codes[0, c3]
-        for i in range(2):
-            half = slice(i * NARROW, (i + 1) * NARROW)
-            for bank, n0 in narrow[i]:
-                score_pass(bank, 0, n0, (words[:, half], scales[:, half]))
-        quantize_h([(1, c2)], STEP, h_bf[:])
-        for bank, n0 in wide:
-            score_pass(bank, 1, n0, h_codes[1, c2])
-            store_scores(bank, n0, c2, by_scalar)
+        pair_feature(FINAL, h_bf[:, 2 * WIDE :], a3)
+        b1 = pair_terms(1, c1, STEP)
+        pair_feature(FINAL, h_bf[:, WIDE : 2 * WIDE], b0)
+        quantize_h([(0, c2), (1, c0)], STEP, h_bf[:, : 2 * WIDE])
+        quantize_h([(0, c3)], NARROW, h_bf[:, 2 * WIDE :])
+        b2 = pair_terms(1, c2, STEP)
+        scores(c0, STEP, [by_scalar] * 3)
         h_bf = rounded_tile(WIDE)
-        for i in range(2):
-            half_terms = [term[:, :, i * NARROW : (i + 1) * NARROW, :] for term in terms]
-            pair_feature(nc.vector, h_bf[:, i * SLIM : (i + 1) * SLIM], half_terms)
-        for i, j0 in enumerate((c3, c4)):
-            quantize_h([(1, j0)], NARROW, h_bf[:, i * SLIM : (i + 1) * SLIM])
-            for bank, n0 in narrow[i]:
-                score_pass(bank, 1, n0, h_codes[1, j0])
-                store_scores(bank, n0, j0, nc.vector.tensor_copy if n0 == 3 else by_scalar)
+        pair_feature(FINAL, h_bf[:], b1)
+        quantize_h([(1, c1)], STEP, h_bf[:])
+        b3 = pair_terms(1, c3, NARROW)
+        a4 = pair_terms(0, c4, NARROW)
+        scores(c1, STEP, [by_scalar] * 3)
+        h_bf = rounded_tile(WIDE)
+        pair_feature(FINAL, h_bf[:], b2)
+        quantize_h([(1, c2)], STEP, h_bf[:])
+        b4 = pair_terms(1, c4, NARROW)
+        scores(c2, STEP, [by_scalar] * 3)
+        h_bf = rounded_tile(SLIM)
+        pair_feature(FINAL, h_bf[:], b3)
+        quantize_h([(1, c3)], NARROW, h_bf[:])
+        h_bf = rounded_tile(2 * SLIM)
+        pair_feature(nc.vector, h_bf[:, :SLIM], a4)
+        pair_feature(nc.vector, h_bf[:, SLIM:], b4)
+        quantize_h([(0, c4), (1, c4)], NARROW, h_bf[:])
+        scores(c3, NARROW, [by_scalar, nc.vector.tensor_copy])
+        scores(c4, NARROW, [by_scalar, nc.vector.tensor_copy])

@@ -40,7 +40,15 @@ PLACE = {
     "wm_w": 3 * UNIT,
     "gq100": 4 * UNIT,
     "gq101": UNIT,
-    "gq110": UNIT + UNIT // 2,
+    "gq110a": UNIT + UNIT // 2,
+    "h0_256_w": UNIT + UNIT // 2,
+    "gq110b": UNIT + 3 * UNIT // 4,
+    "h_last": UNIT + 3 * UNIT // 4,
+    "h0_768_w": 4 * UNIT,
+    "h0_0_w": 4 * UNIT + UNIT // 4,
+    "w1_w10": 6 * UNIT,
+    "gq010a": 6 * UNIT + UNIT // 8,
+    "w1_w11": 6 * UNIT + UNIT // 4,
     "tab_s": 5 * UNIT - T // 2,
     "tab_w1": 5 * UNIT,
 }
@@ -81,9 +89,8 @@ def tile_list_entity_merge_scores_kernel(
         v_planes = held("v_planes", [P, S // 4], I32)
         v_s = v_planes[:].bitcast(U8)
         v2_w = held("v2_w", [P, S], U32)
-        w1_w = [held("w1_w%d" % a, [P, 2, PASS], U32) for a in range(2)]
-        w1_scales = [held("w1_s%d" % a, [P, 2, PASS], U8) for a in range(2)]
-        w1_s = [[w1_scales[a][:, k, :] for k in range(2)] for a in range(2)]
+        w1_w = {(0, k): held("w1_w0%d" % k, [P, PASS], U32) for k in range(2)}
+        w1_s = [[held("w1_s%d%d" % (a, k), [P, PASS], U8)[:] for k in range(2)] for a in range(2)]
         gain_sb = held("gain_sb", [P, 2, PACK], F32)
         gain_recip = held("gain_recip", [P, 2, PACK], F32)
         gain_inv = held("gain_inv", [P, 2, PACK], F32)
@@ -124,9 +131,14 @@ def tile_list_entity_merge_scores_kernel(
         def project_candidates(a, half):
             cols = slice(half * BANK, (half + 1) * BANK)
             for t in range(PACK):
+                pieces = 2 if (half, t // 2) == (1, 0) else 1
+                width = BANK // pieces
                 if t % 2 == 0:
-                    name = "gq%d%d%d" % (a, half, t // 2)
-                    gq[a, half, t // 2] = (placed if name in PLACE else held)(name, [P, 2, BANK], F32)
+                    for i in range(pieces):
+                        name = "gq%d%d%d" % (a, half, t // 2) + "ab"[i] * (pieces - 1)
+                        tile = (placed if name in PLACE else held)(name, [P, 2, width], F32)
+                        for j0 in range(0, width, NARROW):
+                            gq[a, half * BANK + i * width + j0, t // 2] = tile[:, :, j0:]
                 r0 = a * PASS + t * P
                 bank = psum_qo.tile([P, BANK], F32, name="qo")
                 nc.tensor.matmul_mx(
@@ -138,12 +150,18 @@ def tile_list_entity_merge_scores_kernel(
                     start=True,
                     stop=True,
                 )
-                nc.scalar.activation(out=gq[a, half, t // 2][:, t % 2, :], in_=bank[:], func=ACT.Copy, scale=gain_sb[:, a, t : t + 1])
+                for j0 in range(0, BANK, width):
+                    nc.scalar.activation(
+                        out=gq[a, half * BANK + j0, t // 2][:, t % 2, :],
+                        in_=bank[:, j0 : j0 + width],
+                        func=ACT.Copy,
+                        scale=gain_sb[:, a, t : t + 1],
+                    )
 
         def pair_terms(a, j0, width):
             cols = slice(j0, j0 + width)
             per_bank = BANK // width
-            gq_pair = [gq[a, j0 // BANK, u][:, :, j0 % BANK : j0 % BANK + width] for u in range(2)]
+            gq_pair = [gq[a, j0, u][:, :, :width] for u in range(2)]
             diff = ring.tile([P, PACK, width], F32, name="diff", align_bytes=64)
             dist = ring.tile([P, 2, width, 2], F32, name="dist", align_bytes=64)
             prod = ring.tile([P, 2, width, 2], F32, name="prod", align_bytes=64)
@@ -156,7 +174,7 @@ def tile_list_entity_merge_scores_kernel(
                     for t in range(t0, t0 + per_bank):
                         nc.tensor.matmul_mx(
                             out=bank[:, t - t0, :],
-                            lhsT=w1_w[a][:, k, t * P : (t + 1) * P].bitcast(FP8X4),
+                            lhsT=w1_w[a, k][:, t * P : (t + 1) * P].bitcast(FP8X4),
                             lhsT_scale=w1_s[a][k][:, t * P : (t + 1) * P],
                             rhs=v_w[k][:, cols].bitcast(FP8X4),
                             rhs_scale=v_s[4 * k :, cols],
@@ -196,14 +214,12 @@ def tile_list_entity_merge_scores_kernel(
                 op=ALU.mult,
             )
 
-        def rounded_tile(width):
-            return keep.tile([P, width], BF16, name="rounded", tag="rounded", align_bytes=64)
-
         h_codes = {}
 
         def quantize_h(keys, width, h_bf, slot=None):
             name = "h" + "_".join("%d_%d" % key for key in keys)
-            words = held(name + "_w", [P, len(keys) * width], U32, slot)
+            shape = [P, len(keys) * width]
+            words = placed(name + "_w", shape, U32) if name + "_w" in PLACE else held(name + "_w", shape, U32, slot)
             scales = held(name + "_s", [P, len(keys) * width], U8)
             nc.vector.quantize_mx(out=words[:].bitcast(FP8X4), scales=scales[:], in_=h_bf)
             for i, key in enumerate(keys):
@@ -247,7 +263,7 @@ def tile_list_entity_merge_scores_kernel(
                 nc.sync.dma_start(out=v_planes[32 * quad + 4 * k : 32 * quad + 4 * k + 4], in_=v_picked[source : source + 4])
 
         def quantize_w1(a, k, rounded):
-            nc.vector.quantize_mx(out=w1_w[a][:, k, :].bitcast(FP8X4), scales=w1_s[a][k], in_=rounded)
+            nc.vector.quantize_mx(out=w1_w[a, k][:].bitcast(FP8X4), scales=w1_s[a][k], in_=rounded)
 
         nc.vector.memset(w2_raw_s[:TOP], 0)
         nc.vector.memset(tab2_s[:TOP], 0)
@@ -278,9 +294,7 @@ def tile_list_entity_merge_scores_kernel(
         reorder_w2(w2_w[:].bitcast(U16), w2_raw_w[:].bitcast(U16))
         nc.vector.reciprocal(out=gain_recip[:], in_=gain_sb[:])
         nc.vector.tensor_scalar(out=gain_inv[:], in0=gain_recip[:], scalar1=BIG, scalar2=-BIG, op0=ALU.min, op1=ALU.max)
-        second = held("w1_bf1", [P, 2, PACK * PASS], BF16)
-        rounded = {(0, k): held("w1_bf0%d" % k, [P, PACK * PASS], BF16)[:] for k in range(2)}
-        rounded.update({(1, k): second[:, k, :] for k in range(2)})
+        rounded = {(a, k): held("w1_bf%d%d" % (a, k), [P, PACK * PASS], BF16)[:] for a in range(2) for k in range(2)}
         round_w1(rounded[0, 0], 0, 0, [nc.scalar.copy])
         quantize_w1(0, 0, rounded[0, 0])
         gather(v2_w, tab2_w, U32, idx2, 0, BANK)
@@ -296,7 +310,7 @@ def tile_list_entity_merge_scores_kernel(
         for half in range(2):
             cols = slice(half * PASS // 2, (half + 1) * PASS // 2)
             nc.vector.quantize_mx(
-                out=w1_w[0][:, 1, cols].bitcast(FP8X4),
+                out=w1_w[0, 1][:, cols].bitcast(FP8X4),
                 scales=w1_s[0][1][:, cols],
                 in_=rounded[0, 1][:, half * 2 * PASS : (half + 1) * 2 * PASS],
             )
@@ -307,51 +321,52 @@ def tile_list_entity_merge_scores_kernel(
         SLIM = PACK * NARROW
         c0, c1, c2, c3, c4 = 0, STEP, 2 * STEP, 3 * STEP, 3 * STEP + NARROW
         by_scalar = nc.scalar.copy
+
+        def feature(engine, name, terms, width, slot=None):
+            h_bf = held(name, [P, PACK * width], BF16, slot)[:]
+            pair_feature(engine, h_bf, terms)
+            return h_bf
+
         a0 = pair_terms(0, c0, STEP)
         a1 = pair_terms(0, c1, STEP)
-        h_bf = rounded_tile(2 * WIDE)
-        pair_feature(FINAL, h_bf[:, :WIDE], a0)
+        h_a0 = feature(FINAL, "h_a0", a0, STEP)
         round_w1(rounded[1, 0], 1, 0, [by_scalar] * 4)
         round_w1(rounded[1, 1], 1, 1, [by_scalar] * 4)
         a2 = pair_terms(0, c2, STEP)
-        pair_feature(FINAL, h_bf[:, WIDE:], a1)
+        h_a1 = feature(FINAL, "h_a1", a1, STEP)
         project_candidates(1, 0)
-        nc.vector.quantize_mx(
-            out=w1_w[1][:].rearrange("p k c -> p (k c)").bitcast(FP8X4),
-            scales=w1_scales[1][:].rearrange("p k c -> p (k c)"),
-            in_=second[:].rearrange("p k c -> p (k c)"),
-        )
-        quantize_h([(0, c0), (0, c1)], STEP, h_bf[:], slot="w1_bf1")
+        for k in range(2):
+            w1_w[1, k] = placed("w1_w1%d" % k, [P, PASS], U32)
+            quantize_w1(1, k, rounded[1, k])
+        h_a2 = feature(FINAL, "h_a2", a2, STEP, "w1_bf10")
         a3 = pair_terms(0, c3, NARROW)
         b0 = pair_terms(1, c0, STEP)
         project_candidates(1, 1)
         load_rows_by_quadrant(planes[:, : N // 4], 4, wm_scales)
-        h_bf = rounded_tile(2 * WIDE + SLIM)
-        pair_feature(FINAL, h_bf[:, :WIDE], a2)
-        pair_feature(FINAL, h_bf[:, 2 * WIDE :], a3)
+        h_a3 = feature(FINAL, "h_a3", a3, NARROW)
         b1 = pair_terms(1, c1, STEP)
-        pair_feature(FINAL, h_bf[:, WIDE : 2 * WIDE], b0)
-        quantize_h([(0, c2), (1, c0)], STEP, h_bf[:, : 2 * WIDE])
-        quantize_h([(0, c3)], NARROW, h_bf[:, 2 * WIDE :])
+        h_b0 = feature(FINAL, "h_b0", b0, STEP)
+        quantize_h([(0, c3)], NARROW, h_a3)
+        quantize_h([(0, c0)], STEP, h_a0)
+        quantize_h([(1, c0)], STEP, h_b0)
+        h_b1 = feature(FINAL, "h_b1", b1, STEP, "h_a0")
         b2 = pair_terms(1, c2, STEP)
         scores(c0, STEP, [by_scalar] * 3)
-        h_bf = rounded_tile(WIDE)
-        pair_feature(FINAL, h_bf[:], b1)
-        quantize_h([(1, c1)], STEP, h_bf[:])
+        quantize_h([(0, c1)], STEP, h_a1)
+        quantize_h([(1, c1)], STEP, h_b1)
+        h_b2 = feature(FINAL, "h_b2", b2, STEP, "h_a1")
         b3 = pair_terms(1, c3, NARROW)
         a4 = pair_terms(0, c4, NARROW)
         scores(c1, STEP, [by_scalar] * 3)
-        h_bf = rounded_tile(WIDE)
-        pair_feature(FINAL, h_bf[:], b2)
-        quantize_h([(1, c2)], STEP, h_bf[:])
+        quantize_h([(0, c2)], STEP, h_a2, "gq010b")
+        quantize_h([(1, c2)], STEP, h_b2)
+        h_b3 = feature(FINAL, "h_b3", b3, NARROW, "w1_bf10")
         b4 = pair_terms(1, c4, NARROW)
         scores(c2, STEP, [by_scalar] * 3)
-        h_bf = rounded_tile(SLIM)
-        pair_feature(FINAL, h_bf[:], b3)
-        quantize_h([(1, c3)], NARROW, h_bf[:])
-        h_bf = rounded_tile(2 * SLIM)
-        pair_feature(nc.vector, h_bf[:, :SLIM], a4)
-        pair_feature(nc.vector, h_bf[:, SLIM:], b4)
-        quantize_h([(0, c4), (1, c4)], NARROW, h_bf[:])
+        h_last = placed("h_last", [P, 2 * SLIM], BF16)
+        pair_feature(nc.vector, h_last[:, :SLIM], a4)
+        quantize_h([(1, c3)], NARROW, h_b3)
+        pair_feature(nc.vector, h_last[:, SLIM:], b4)
+        quantize_h([(0, c4), (1, c4)], NARROW, h_last[:])
         scores(c3, NARROW, [by_scalar, nc.vector.tensor_copy])
         scores(c4, NARROW, [by_scalar, nc.vector.tensor_copy])

@@ -43,7 +43,7 @@ PLACE = {
     "gq110a": UNIT + UNIT // 2,
     "h0_256_w": UNIT + UNIT // 2,
     "gq110b": UNIT + 3 * UNIT // 4,
-    "h_last": UNIT + 3 * UNIT // 4,
+    "h0_512_w": UNIT + 3 * UNIT // 4,
     "h0_768_w": 4 * UNIT,
     "h0_0_w": 4 * UNIT + UNIT // 4,
     "w1_w10": 6 * UNIT,
@@ -127,6 +127,16 @@ def tile_list_entity_merge_scores_kernel(
             width = P // len(copies)
             for i, copy in enumerate(copies):
                 copy(out=rounded[:, i * width : (i + 1) * width], in_=loaded[:, i * width : (i + 1) * width])
+
+        def round_on_gpsimd(out, in_):
+            nc.gpsimd.tensor_scalar(
+                out=out.rearrange("p m j t -> p m t j"),
+                in0=in_.rearrange("p m j t -> p m t j"),
+                scalar1=1.0,
+                scalar2=0.0,
+                op0=ALU.mult,
+                op1=ALU.add,
+            )
 
         def project_candidates(a, half):
             cols = slice(half * BANK, (half + 1) * BANK)
@@ -225,7 +235,7 @@ def tile_list_entity_merge_scores_kernel(
             for i, key in enumerate(keys):
                 h_codes[key] = (words[:, i * width : (i + 1) * width], scales[:, i * width : (i + 1) * width])
 
-        def score_pass(bank, a, n0, codes):
+        def score_pass(bank, a, n0, codes, opening=0):
             per_bank = bank.shape[1]
             words, scales = codes
             for g in range(per_bank):
@@ -236,8 +246,8 @@ def tile_list_entity_merge_scores_kernel(
                     lhsT_scale=plane_bytes[4 + 4 * a :, ncols],
                     rhs=words.bitcast(FP8X4),
                     rhs_scale=scales,
-                    start=(a == 0 and g == 0),
-                    stop=(a == 1 and g == per_bank - 1),
+                    start=(a == opening and g == 0),
+                    stop=(a != opening and g == per_bank - 1),
                 )
 
         def store_scores(bank, n0, j0, copy):
@@ -290,11 +300,14 @@ def tile_list_entity_merge_scores_kernel(
         move_v_scales(0)
         load_tab(1)
         move_v_scales(1)
-        load_w1(0, 1)
+        late["w1", 0, 1] = placed("w1_raw01", [P, 2, PACK, PASS // 2], F32)
+        for half in range(2):
+            rows = w1[PASS:, half * PASS // 2 : (half + 1) * PASS // 2]
+            nc.sync.dma_start(out=late["w1", 0, 1][:, half], in_=rows.rearrange("(p j) r -> p j r", j=PACK))
         reorder_w2(w2_w[:].bitcast(U16), w2_raw_w[:].bitcast(U16))
         nc.vector.reciprocal(out=gain_recip[:], in_=gain_sb[:])
         nc.vector.tensor_scalar(out=gain_inv[:], in0=gain_recip[:], scalar1=BIG, scalar2=-BIG, op0=ALU.min, op1=ALU.max)
-        rounded = {(a, k): held("w1_bf%d%d" % (a, k), [P, PACK * PASS], BF16)[:] for a in range(2) for k in range(2)}
+        rounded = {(a, k): held("w1_bf%d%d" % (a, k), [P, PACK * PASS], BF16)[:] for a, k in ((0, 0), (0, 1), (1, 1))}
         round_w1(rounded[0, 0], 0, 0, [nc.scalar.copy])
         quantize_w1(0, 0, rounded[0, 0])
         gather(v2_w, tab2_w, U32, idx2, 0, BANK)
@@ -306,7 +319,11 @@ def tile_list_entity_merge_scores_kernel(
         late["wm"] = placed("wm_w", [P, 2, N], I32)
         nc.sync.dma_start(out=late["wm"][:], in_=wm_words.rearrange("a p n i -> p a (n i)").bitcast(I32))
         gather(v_w[1], late["tab", 1], U32, idx, 0, S)
-        round_w1(rounded[0, 1], 0, 1, [nc.scalar.copy, nc.vector.tensor_copy])
+        for half, copy in enumerate((nc.scalar.copy, nc.vector.tensor_copy)):
+            copy(
+                out=rounded[0, 1].rearrange("p (t m j) -> p m j t", t=PACK, j=PACK)[:, half * P // 2 : (half + 1) * P // 2],
+                in_=late["w1", 0, 1][:, half].rearrange("p j (m t) -> p m j t", t=PACK),
+            )
         for half in range(2):
             cols = slice(half * PASS // 2, (half + 1) * PASS // 2)
             nc.vector.quantize_mx(
@@ -329,8 +346,9 @@ def tile_list_entity_merge_scores_kernel(
 
         a0 = pair_terms(0, c0, STEP)
         a1 = pair_terms(0, c1, STEP)
+        rounded[1, 0] = held("w1_bf10", [P, PACK * PASS], BF16, "w1_bf01")[:]
+        round_w1(rounded[1, 0], 1, 0, [round_on_gpsimd] * 2 + [by_scalar] * 2)
         h_a0 = feature(FINAL, "h_a0", a0, STEP)
-        round_w1(rounded[1, 0], 1, 0, [by_scalar] * 4)
         round_w1(rounded[1, 1], 1, 1, [by_scalar] * 4)
         a2 = pair_terms(0, c2, STEP)
         h_a1 = feature(FINAL, "h_a1", a1, STEP)
@@ -338,7 +356,7 @@ def tile_list_entity_merge_scores_kernel(
         for k in range(2):
             w1_w[1, k] = placed("w1_w1%d" % k, [P, PASS], U32)
             quantize_w1(1, k, rounded[1, k])
-        h_a2 = feature(FINAL, "h_a2", a2, STEP, "w1_bf10")
+        h_a2 = feature(FINAL, "h_a2", a2, STEP, "w1_bf01")
         a3 = pair_terms(0, c3, NARROW)
         b0 = pair_terms(1, c0, STEP)
         project_candidates(1, 1)
@@ -355,18 +373,28 @@ def tile_list_entity_merge_scores_kernel(
         quantize_h([(0, c1)], STEP, h_a1)
         quantize_h([(1, c1)], STEP, h_b1)
         h_b2 = feature(FINAL, "h_b2", b2, STEP, "h_a1")
-        b3 = pair_terms(1, c3, NARROW)
-        a4 = pair_terms(0, c4, NARROW)
+        b3 = pair_terms(1, c3, STEP)
+        b3, b4 = [[term[:, :, i * NARROW : (i + 1) * NARROW, :] for term in b3] for i in range(2)]
         scores(c1, STEP, [by_scalar] * 3)
-        quantize_h([(0, c2)], STEP, h_a2, "gq010b")
+        quantize_h([(0, c2)], STEP, h_a2)
         quantize_h([(1, c2)], STEP, h_b2)
-        h_b3 = feature(FINAL, "h_b3", b3, NARROW, "w1_bf10")
-        b4 = pair_terms(1, c4, NARROW)
+        h_b3 = feature(FINAL, "h_b3", b3, NARROW, "w1_bf01")
+        a4 = pair_terms(0, c4, NARROW)
         scores(c2, STEP, [by_scalar] * 3)
-        h_last = placed("h_last", [P, 2 * SLIM], BF16)
-        pair_feature(nc.vector, h_last[:, :SLIM], a4)
+        fourth = [(psum_p.tile([P, 3, NARROW], F32, name="pp"), n0) for n0 in (0, 3)]
+        fifth = [(psum_p.tile([P, 3, NARROW], F32, name="pp"), 0), (psum_qo.tile([P, 3, NARROW], F32, name="qo"), 3)]
+        for bank, n0 in fourth:
+            score_pass(bank, 0, n0, h_codes[0, c3])
+        h_b4 = feature(nc.vector, "h_b4", b4, NARROW, "gq010b")
         quantize_h([(1, c3)], NARROW, h_b3)
-        pair_feature(nc.vector, h_last[:, SLIM:], b4)
-        quantize_h([(0, c4), (1, c4)], NARROW, h_last[:])
-        scores(c3, NARROW, [by_scalar, nc.vector.tensor_copy])
-        scores(c4, NARROW, [by_scalar, nc.vector.tensor_copy])
+        quantize_h([(1, c4)], NARROW, h_b4)
+        h_a4 = feature(nc.vector, "h_a4", a4, NARROW)
+        for bank, n0 in fourth:
+            score_pass(bank, 1, n0, h_codes[1, c3])
+            store_scores(bank, n0, c3, by_scalar)
+        for bank, n0 in fifth:
+            score_pass(bank, 1, n0, h_codes[1, c4], 1)
+        quantize_h([(0, c4)], NARROW, h_a4)
+        for (bank, n0), copy in zip(fifth, (by_scalar, nc.vector.tensor_copy)):
+            score_pass(bank, 0, n0, h_codes[0, c4], 1)
+            store_scores(bank, n0, c4, copy)

@@ -41,11 +41,11 @@ PLACE = {
     "gq100": 4 * UNIT,
     "gq101": UNIT,
     "gq110a": UNIT + UNIT // 2,
-    "h0_256_w": UNIT + UNIT // 2,
+    "h0_512_w": UNIT + UNIT // 2,
     "gq110b": UNIT + 3 * UNIT // 4,
-    "h0_512_w": UNIT + 3 * UNIT // 4,
-    "h0_768_w": 4 * UNIT,
-    "h0_0_w": 4 * UNIT + UNIT // 4,
+    "h0_768_w": UNIT + 3 * UNIT // 4,
+    "h0_0_w": 4 * UNIT,
+    "h0_256_w": 4 * UNIT + UNIT // 4,
     "w1_w10": 6 * UNIT,
     "gq010a": 6 * UNIT + UNIT // 8,
     "w1_w11": 6 * UNIT + UNIT // 4,
@@ -250,9 +250,9 @@ def tile_list_entity_merge_scores_kernel(
                     stop=(a != opening and g == per_bank - 1),
                 )
 
-        def store_scores(bank, n0, j0, copy):
+        def store_scores(bank, n0, j0, copy, slot=None):
             per_bank, width = bank.shape[1], bank.shape[2]
-            staged = held("staged%d_%d" % (j0, n0), [P, per_bank, width], F32)
+            staged = held("staged%d_%d" % (j0, n0), [P, per_bank, width], F32, slot)
             copy(out=staged[:], in_=bank[:])
             rows = out[n0 * P : (n0 + per_bank) * P, j0 : j0 + width]
             nc.sync.dma_start(out=rows.rearrange("(g p) j -> p g j", p=P), in_=staged[:])
@@ -279,17 +279,19 @@ def tile_list_entity_merge_scores_kernel(
         nc.vector.memset(tab2_s[:TOP], 0)
         nc.vector.memset(tab_s[:LOW], 0)
         nc.vector.memset(v_planes[:], 0)
+        nc.sync.dma_start(out=gain_sb[:], in_=gain.rearrange("(a p t) -> p a t", a=2, t=PACK))
         nc.sync.dma_start(idx2[:], offs2)
         nc.sync.dma_start(out=tab2_s[TOP:], in_=tab2_scales[0].bitcast(I32))
         nc.sync.dma_start(out=w2_raw_s[TOP:], in_=w2_scales[0].bitcast(I32))
         nc.sync.dma_start(idx[:], offs)
         nc.sync.dma_start(out=tab_s[LOW:], in_=tab_scales.rearrange("a q t -> (a q) t").bitcast(I32))
         nc.sync.dma_start(out=w2_raw_w[:], in_=w2_words[0].bitcast(I32))
-        nc.sync.dma_start(out=gain_sb[:], in_=gain.rearrange("(a p t) -> p a t", a=2, t=PACK))
         load_w1(0, 0)
         tab2_w = placed("tab2_w", [P, T2], I32)
         nc.sync.dma_start(out=tab2_w[:], in_=tab2_words[0].rearrange("p t i -> p (t i)").bitcast(I32))
 
+        nc.vector.reciprocal(out=gain_recip[:], in_=gain_sb[:])
+        nc.vector.tensor_scalar(out=gain_inv[:], in0=gain_recip[:], scalar1=BIG, scalar2=-BIG, op0=ALU.min, op1=ALU.max)
         reorder_w2(w2_s, w2_raw_s[:].bitcast(U8))
         gather(v2_picked, tab2_s, U8, idx2, 0, S)
         nc.vector.tensor_copy(out=planes[:, : S // 4], in_=v2_picked[:].bitcast(I32))
@@ -305,8 +307,6 @@ def tile_list_entity_merge_scores_kernel(
             rows = w1[PASS:, half * PASS // 2 : (half + 1) * PASS // 2]
             nc.sync.dma_start(out=late["w1", 0, 1][:, half], in_=rows.rearrange("(p j) r -> p j r", j=PACK))
         reorder_w2(w2_w[:].bitcast(U16), w2_raw_w[:].bitcast(U16))
-        nc.vector.reciprocal(out=gain_recip[:], in_=gain_sb[:])
-        nc.vector.tensor_scalar(out=gain_inv[:], in0=gain_recip[:], scalar1=BIG, scalar2=-BIG, op0=ALU.min, op1=ALU.max)
         rounded = {(a, k): held("w1_bf%d%d" % (a, k), [P, PACK * PASS], BF16)[:] for a, k in ((0, 0), (0, 1), (1, 1))}
         round_w1(rounded[0, 0], 0, 0, [nc.scalar.copy])
         quantize_w1(0, 0, rounded[0, 0])
@@ -364,25 +364,26 @@ def tile_list_entity_merge_scores_kernel(
         h_a3 = feature(FINAL, "h_a3", a3, NARROW)
         b1 = pair_terms(1, c1, STEP)
         h_b0 = feature(FINAL, "h_b0", b0, STEP)
-        quantize_h([(0, c3)], NARROW, h_a3)
         quantize_h([(0, c0)], STEP, h_a0)
+        quantize_h([(0, c1)], STEP, h_a1)
         quantize_h([(1, c0)], STEP, h_b0)
-        h_b1 = feature(FINAL, "h_b1", b1, STEP, "h_a0")
+        h_b1 = feature(FINAL, "h_b1", b1, STEP, "h_a1")
         b2 = pair_terms(1, c2, STEP)
         scores(c0, STEP, [by_scalar] * 3)
-        quantize_h([(0, c1)], STEP, h_a1)
+        quantize_h([(0, c2)], STEP, h_a2)
         quantize_h([(1, c1)], STEP, h_b1)
-        h_b2 = feature(FINAL, "h_b2", b2, STEP, "h_a1")
+        h_b2 = feature(FINAL, "h_b2", b2, STEP, "w1_bf01")
         b3 = pair_terms(1, c3, STEP)
         b3, b4 = [[term[:, :, i * NARROW : (i + 1) * NARROW, :] for term in b3] for i in range(2)]
         scores(c1, STEP, [by_scalar] * 3)
-        quantize_h([(0, c2)], STEP, h_a2)
+        quantize_h([(0, c3)], NARROW, h_a3)
         quantize_h([(1, c2)], STEP, h_b2)
-        h_b3 = feature(FINAL, "h_b3", b3, NARROW, "w1_bf01")
+        h_b3 = feature(FINAL, "h_b3", b3, NARROW, "h_a3")
         a4 = pair_terms(0, c4, NARROW)
         scores(c2, STEP, [by_scalar] * 3)
         fourth = [(psum_p.tile([P, 3, NARROW], F32, name="pp"), n0) for n0 in (0, 3)]
-        fifth = [(psum_p.tile([P, 3, NARROW], F32, name="pp"), 0), (psum_qo.tile([P, 3, NARROW], F32, name="qo"), 3)]
+        fifth = [(psum_p.tile([P, 2, NARROW], F32, name="pp"), 0)]
+        fifth += [(psum_qo.tile([P, 2, NARROW], F32, name="qo"), n0) for n0 in (2, 4)]
         for bank, n0 in fourth:
             score_pass(bank, 0, n0, h_codes[0, c3])
         h_b4 = feature(nc.vector, "h_b4", b4, NARROW, "gq010b")
@@ -391,10 +392,11 @@ def tile_list_entity_merge_scores_kernel(
         h_a4 = feature(nc.vector, "h_a4", a4, NARROW)
         for bank, n0 in fourth:
             score_pass(bank, 1, n0, h_codes[1, c3])
-            store_scores(bank, n0, c3, by_scalar)
+        store_scores(*fourth[0], c3, by_scalar)
         for bank, n0 in fifth:
             score_pass(bank, 1, n0, h_codes[1, c4], 1)
         quantize_h([(0, c4)], NARROW, h_a4)
-        for (bank, n0), copy in zip(fifth, (by_scalar, nc.vector.tensor_copy)):
+        store_scores(*fourth[1], c3, nc.vector.tensor_copy, "h_a4")
+        for (bank, n0), copy in zip(fifth, (by_scalar, nc.vector.tensor_copy, by_scalar)):
             score_pass(bank, 0, n0, h_codes[0, c4], 1)
             store_scores(bank, n0, c4, copy)

@@ -46,11 +46,12 @@ PLACE = {
     "h0_768_w": UNIT + 3 * UNIT // 4,
     "h0_0_w": 4 * UNIT,
     "h0_256_w": 4 * UNIT + UNIT // 4,
-    "w1_w10": 6 * UNIT,
-    "gq010a": 6 * UNIT + UNIT // 8,
-    "w1_w11": 6 * UNIT + UNIT // 4,
-    "tab_s": 5 * UNIT - T // 2,
-    "tab_w1": 5 * UNIT,
+    "w1_w10": 7 * UNIT,
+    "gq010a": 7 * UNIT + UNIT // 8,
+    "w1_w11": 7 * UNIT + UNIT // 4,
+    "tab_s": 5 * UNIT - 64,
+    "w2_raw_w1": 5 * UNIT,
+    "tab_w1": 5 * UNIT + T - 128,
 }
 
 
@@ -78,12 +79,12 @@ def tile_list_entity_merge_scores_kernel(
         tab2_s = held("tab2_s", [P, T2 // 4], I32)
         tab_s = placed("tab_s", [P, T // 4], I32)
         w2_raw_s = held("w2_raw_s", [P, H // 4], I32)
-        w2_raw_w = held("w2_raw_w", [P, H // 2], I32)
+        w2_raw_w = {0: held("w2_raw_w0", [P, H // 4], I32)}
         v2_picked = placed("v2_picked", [P, S], U8)
         planes = held("planes", [P, (S + H) // 4], I32)
         plane_bytes = planes[:].bitcast(U8)
         v2_s, w2_s = plane_bytes[:, :S], plane_bytes[:, S:]
-        w2_w = held("w2_w", [P, 2 * H], U8)
+        w2_w = {a: held("w2_w%d" % a, [P, H], U8) for a in range(2)}
         v_w = [held("v_w%d" % k, [P, S], U32) for k in range(2)]
         v_picked = held("v_picked", [P, S // 4], I32)
         v_planes = held("v_planes", [P, S // 4], I32)
@@ -115,10 +116,10 @@ def tile_list_entity_merge_scores_kernel(
             window = table[:].bitcast(dtype).indirect(offsets[:, j0 // PER_COLUMN : (j0 + width) // PER_COLUMN])
             nc.vector.tensor_copy(out=picked[:, j0 : j0 + width], in_=window)
 
-        def reorder_w2(ordered, loaded):
+        def reorder_w2(ordered, loaded, passes):
             nc.vector.tensor_copy(
-                out=ordered.rearrange("p (a t m) -> p a t m", a=2, t=PACK),
-                in_=loaded.rearrange("p (a m t) -> p a t m", a=2, t=PACK),
+                out=ordered.rearrange("p (a t m) -> p a t m", a=passes, t=PACK),
+                in_=loaded.rearrange("p (a m t) -> p a t m", a=passes, t=PACK),
             )
 
         def round_w1(rounded, a, k, copies):
@@ -153,7 +154,7 @@ def tile_list_entity_merge_scores_kernel(
                 bank = psum_qo.tile([P, BANK], F32, name="qo")
                 nc.tensor.matmul_mx(
                     out=bank[:],
-                    lhsT=w2_w[:, 2 * r0 : 2 * (r0 + P)].bitcast(FP4X4),
+                    lhsT=w2_w[a][:, 2 * t * P : 2 * (t + 1) * P].bitcast(FP4X4),
                     lhsT_scale=w2_s[:, r0 : r0 + P],
                     rhs=v2_w[:, cols].bitcast(FP8X4),
                     rhs_scale=v2_s[:, cols],
@@ -187,7 +188,7 @@ def tile_list_entity_merge_scores_kernel(
                             lhsT=w1_w[a, k][:, t * P : (t + 1) * P].bitcast(FP8X4),
                             lhsT_scale=w1_s[a][k][:, t * P : (t + 1) * P],
                             rhs=v_w[k][:, cols].bitcast(FP8X4),
-                            rhs_scale=v_s[4 * k :, cols],
+                            rhs_scale=v_s[4 + 4 * k :, cols],
                             start=(k == 0 and t == t0),
                             stop=(k == 1 and t == t0 + per_bank - 1),
                         )
@@ -270,7 +271,7 @@ def tile_list_entity_merge_scores_kernel(
         def move_v_scales(k):
             for quad in (0, 2, 1, 3):
                 source = LOW + ROWS * k + 4 * quad
-                nc.sync.dma_start(out=v_planes[32 * quad + 4 * k : 32 * quad + 4 * k + 4], in_=v_picked[source : source + 4])
+                nc.sync.dma_start(out=v_planes[32 * quad + 4 * k + 4 : 32 * quad + 4 * k + 8], in_=v_picked[source : source + 4])
 
         def quantize_w1(a, k, rounded):
             nc.vector.quantize_mx(out=w1_w[a, k][:].bitcast(FP8X4), scales=w1_s[a][k], in_=rounded)
@@ -285,14 +286,14 @@ def tile_list_entity_merge_scores_kernel(
         nc.sync.dma_start(out=w2_raw_s[TOP:], in_=w2_scales[0].bitcast(I32))
         nc.sync.dma_start(idx[:], offs)
         nc.sync.dma_start(out=tab_s[LOW:], in_=tab_scales.rearrange("a q t -> (a q) t").bitcast(I32))
-        nc.sync.dma_start(out=w2_raw_w[:], in_=w2_words[0].bitcast(I32))
+        nc.sync.dma_start(out=w2_raw_w[0][:], in_=w2_words[0][:, :H].bitcast(I32))
         load_w1(0, 0)
         tab2_w = placed("tab2_w", [P, T2], I32)
         nc.sync.dma_start(out=tab2_w[:], in_=tab2_words[0].rearrange("p t i -> p (t i)").bitcast(I32))
 
         nc.vector.reciprocal(out=gain_recip[:], in_=gain_sb[:])
         nc.vector.tensor_scalar(out=gain_inv[:], in0=gain_recip[:], scalar1=BIG, scalar2=-BIG, op0=ALU.min, op1=ALU.max)
-        reorder_w2(w2_s, w2_raw_s[:].bitcast(U8))
+        reorder_w2(w2_s, w2_raw_s[:].bitcast(U8), 2)
         gather(v2_picked, tab2_s, U8, idx2, 0, S)
         nc.vector.tensor_copy(out=planes[:, : S // 4], in_=v2_picked[:].bitcast(I32))
         for quad in (0, 2, 1, 3):
@@ -306,7 +307,9 @@ def tile_list_entity_merge_scores_kernel(
         for half in range(2):
             rows = w1[PASS:, half * PASS // 2 : (half + 1) * PASS // 2]
             nc.sync.dma_start(out=late["w1", 0, 1][:, half], in_=rows.rearrange("(p j) r -> p j r", j=PACK))
-        reorder_w2(w2_w[:].bitcast(U16), w2_raw_w[:].bitcast(U16))
+        w2_raw_w[1] = placed("w2_raw_w1", [P, H // 4], I32)
+        nc.sync.dma_start(out=w2_raw_w[1][:], in_=w2_words[0][:, H:].bitcast(I32))
+        reorder_w2(w2_w[0][:].bitcast(U16), w2_raw_w[0][:].bitcast(U16), 1)
         rounded = {(a, k): held("w1_bf%d%d" % (a, k), [P, PACK * PASS], BF16)[:] for a, k in ((0, 0), (0, 1), (1, 1))}
         round_w1(rounded[0, 0], 0, 0, [nc.scalar.copy])
         quantize_w1(0, 0, rounded[0, 0])
@@ -331,6 +334,7 @@ def tile_list_entity_merge_scores_kernel(
                 scales=w1_s[0][1][:, cols],
                 in_=rounded[0, 1][:, half * 2 * PASS : (half + 1) * 2 * PASS],
             )
+        reorder_w2(w2_w[1][:].bitcast(U16), w2_raw_w[1][:].bitcast(U16), 1)
         project_candidates(0, 1)
 
         FINAL = nc.gpsimd

from contextlib import ExitStack

import concourse.mybir as mybir

K, K2, T, T2, S, H, N = 1024, 512, 2048, 4096, 1024, 1024, 768
FLOPS = 2 * S * (K * H + K2 * H + H * N)

F32 = mybir.dt.float32
BF16 = mybir.dt.bfloat16
I32 = mybir.dt.int32
U32 = mybir.dt.uint32
U16 = mybir.dt.uint16
U8 = mybir.dt.uint8
FP8X4 = mybir.dt.float8_e4m3fn_x4
FP4X4 = mybir.dt.float4_e2m1fn_x4
ALU = mybir.AluOpType
ACT = mybir.ActivationFunctionType

P = 128
PACK = 4
PASS = P * PACK
BANK = 512
PER_COLUMN = 16
ROWS = 16
TOP = P - ROWS
BIG = 3.0e38

STEP = 256
NARROW = 128

UNIT = 8192
PLACE = {
    "tab2_w": 0,
    "w1_raw10": 0,
    "w1_raw11": UNIT,
    "w1_raw00": 2 * UNIT,
    "v2_picked": 3 * UNIT,
    "tab_w0": 3 * UNIT,
    "w1_raw01": 4 * UNIT,
    "wm_w": 3 * UNIT,
    "gq100": 4 * UNIT,
    "gq101": UNIT,
    "gq110a": UNIT + UNIT // 2,
    "h0_512_w": UNIT + UNIT // 2,
    "gq110b": UNIT + 3 * UNIT // 4,
    "h0_768_w": UNIT + 3 * UNIT // 4,
    "h0_0_w": 4 * UNIT,
    "h0_256_w": 4 * UNIT + UNIT // 4,
    "w1_w10": 7 * UNIT,
    "gq010a": 7 * UNIT + UNIT // 8,
    "w1_w11": 7 * UNIT + UNIT // 4,
    "tab_s": 5 * UNIT - 64,
    "w2_raw_w1": 5 * UNIT,
    "tab_w1": 5 * UNIT + T - 128,
}


def tile_list_entity_merge_scores_kernel(
    tc, tab_words, tab_scales, tab2_words, tab2_scales, offs, offs2, w1, w2_words, w2_scales, gain, wm_words, wm_scales, out
):
    nc = tc.nc
    with ExitStack() as ctx:
        lists = ctx.enter_context(tc.tile_pool(name="lists", bufs=1))
        keep = ctx.enter_context(tc.tile_pool(name="keep", bufs=1))
        placed_pool = ctx.enter_context(tc.tile_pool(name="placed", bufs=1))
        ring = ctx.enter_context(tc.tile_pool(name="ring", bufs=4))
        psum_p = ctx.enter_context(tc.psum_pool(name="psum_p", bufs=4))
        psum_qo = ctx.enter_context(tc.psum_pool(name="psum_qo", bufs=4))

        def held(name, shape, dtype, slot=None):
            return keep.tile(shape, dtype, name=name, tag=slot or name, align_bytes=64)

        def placed(name, shape, dtype):
            return placed_pool.tile(shape, dtype, name=name, offset=PLACE[name], align_bytes=64)

        idx = lists.tile([P, S // PER_COLUMN], U16, name="idx")
        idx2 = lists.tile([P, S // PER_COLUMN], U16, name="idx2")

        tab2_s = held("tab2_s", [P, T2 // 4], I32)
        tab_s = placed("tab_s", [P, T // 4], I32)
        w2_raw_s = held("w2_raw_s", [P, H // 4], I32)
        w2_raw_w = {0: held("w2_raw_w0", [P, H // 4], I32)}
        v2_picked = placed("v2_picked", [P, S], U8)
        planes = held("planes", [P, (S + H) // 4], I32)
        plane_bytes = planes[:].bitcast(U8)
        v2_s, w2_s = plane_bytes[:, :S], plane_bytes[:, S:]
        w2_w = {a: held("w2_w%d" % a, [P, H], U8) for a in range(2)}
        v_w = [held("v_w%d" % k, [P, S], U32) for k in range(2)]
        v_picked = held("v_picked", [P, S // 4], I32)
        v_planes = held("v_planes", [P, S // 4], I32)
        v_s = v_planes[:].bitcast(U8)
        v2_w = held("v2_w", [P, S], U32)
        w1_w = {(0, k): held("w1_w0%d" % k, [P, PASS], U32) for k in range(2)}
        w1_s = [[held("w1_s%d%d" % (a, k), [P, PASS], U8)[:] for k in range(2)] for a in range(2)]
        gain_sb = held("gain_sb", [P, 2, PACK], F32)
        gain_recip = held("gain_recip", [P, 2, PACK], F32)
        gain_inv = held("gain_inv", [P, 2, PACK], F32)
        gq = {}
        late = {}

        def load_rows_by_quadrant(tile, first, source):
            for quad in (0, 2, 1, 3):
                rows = tile[32 * quad + first : 32 * quad + first + 8]
                nc.sync.dma_start(out=rows, in_=source[:, 4 * quad : 4 * quad + 4, :].bitcast(I32))

        def load_tab(k):
            late["tab", k] = placed("tab_w%d" % k, [P, T], I32)
            nc.sync.dma_start(out=late["tab", k][:], in_=tab_words[k].rearrange("p t i -> p (t i)").bitcast(I32))

        def load_w1(a, k):
            late["w1", a, k] = placed("w1_raw%d%d" % (a, k), [P, PACK, PASS], F32)
            rows = w1[k * PASS : (k + 1) * PASS, a * PASS : (a + 1) * PASS]
            nc.sync.dma_start(out=late["w1", a, k][:], in_=rows.rearrange("(p j) r -> p j r", j=PACK))

        def gather(picked, table, dtype, offsets, j0, width):
            window = table[:].bitcast(dtype).indirect(offsets[:, j0 // PER_COLUMN : (j0 + width) // PER_COLUMN])
            nc.vector.tensor_copy(out=picked[:, j0 : j0 + width], in_=window)

        def reorder_w2(ordered, loaded, passes):
            nc.vector.tensor_copy(
                out=ordered.rearrange("p (a t m) -> p a t m", a=passes, t=PACK),
                in_=loaded.rearrange("p (a m t) -> p a t m", a=passes, t=PACK),
            )

        def round_w1(rounded, a, k, copies):
            rounded = rounded.rearrange("p (t m j) -> p m j t", t=PACK, j=PACK)
            loaded = late["w1", a, k][:].rearrange("p j (m t) -> p m j t", t=PACK)
            width = P // len(copies)
            for i, copy in enumerate(copies):
                copy(out=rounded[:, i * width : (i + 1) * width], in_=loaded[:, i * width : (i + 1) * width])

        def round_on_gpsimd(out, in_):
            nc.gpsimd.tensor_scalar(
                out=out.rearrange("p m j t -> p m t j"),
                in0=in_.rearrange("p m j t -> p m t j"),
                scalar1=1.0,
                scalar2=0.0,
                op0=ALU.mult,
                op1=ALU.add,
            )

        def project_candidates(a, half):
            cols = slice(half * BANK, (half + 1) * BANK)
            for t in range(PACK):
                pieces = 2 if (half, t // 2) == (1, 0) else 1
                width = BANK // pieces
                if t % 2 == 0:
                    for i in range(pieces):
                        name = "gq%d%d%d" % (a, half, t // 2) + "ab"[i] * (pieces - 1)
                        tile = (placed if name in PLACE else held)(name, [P, 2, width], F32)
                        for j0 in range(0, width, NARROW):
                            gq[a, half * BANK + i * width + j0, t // 2] = tile[:, :, j0:]
                r0 = a * PASS + t * P
                bank = psum_qo.tile([P, BANK], F32, name="qo")
                nc.tensor.matmul_mx(
                    out=bank[:],
                    lhsT=w2_w[a][:, 2 * t * P : 2 * (t + 1) * P].bitcast(FP4X4),
                    lhsT_scale=w2_s[:, r0 : r0 + P],
                    rhs=v2_w[:, cols].bitcast(FP8X4),
                    rhs_scale=v2_s[:, cols],
                    start=True,
                    stop=True,
                )
                for j0 in range(0, BANK, width):
                    nc.scalar.activation(
                        out=gq[a, half * BANK + j0, t // 2][:, t % 2, :],
                        in_=bank[:, j0 : j0 + width],
                        func=ACT.Copy,
                        scale=gain_sb[:, a, t : t + 1],
                    )

        def pair_terms(a, j0, width):
            cols = slice(j0, j0 + width)
            per_bank = BANK // width
            gq_pair = [gq[a, j0, u][:, :, :width] for u in range(2)]
            diff = ring.tile([P, PACK, width], F32, name="diff", align_bytes=64)
            dist = ring.tile([P, 2, width, 2], F32, name="dist", align_bytes=64)
            prod = ring.tile([P, 2, width, 2], F32, name="prod", align_bytes=64)
            by_twos = "p e (c i) -> p c e i"
            banks = []
            for t0 in range(0, PACK, per_bank):
                bank = psum_p.tile([P, per_bank, width], F32, name="pp")
                banks.append(bank)
                for k in range(2):
                    for t in range(t0, t0 + per_bank):
                        nc.tensor.matmul_mx(
                            out=bank[:, t - t0, :],
                            lhsT=w1_w[a, k][:, t * P : (t + 1) * P].bitcast(FP8X4),
                            lhsT_scale=w1_s[a][k][:, t * P : (t + 1) * P],
                            rhs=v_w[k][:, cols].bitcast(FP8X4),
                            rhs_scale=v_s[4 + 4 * k :, cols],
                            start=(k == 0 and t == t0),
                            stop=(k == 1 and t == t0 + per_bank - 1),
                        )
                for t in range(t0, t0 + per_bank):
                    nc.vector.scalar_tensor_tensor(
                        out=diff[:, t, :],
                        in0=gq_pair[t // 2][:, t % 2, :],
                        scalar=gain_inv[:, a, t : t + 1],
                        in1=bank[:, t - t0, :],
                        op0=ALU.mult,
                        op1=ALU.subtract,
                    )
                nc.scalar.activation(
                    out=dist[:, t0 // 2 : (t0 + per_bank) // 2, :, :],
                    in_=diff[:, t0 : t0 + per_bank, :].rearrange("p (u e) n -> p u n e", e=2),
                    func=ACT.Abs,
                )
            for u in range(2):
                e0 = 2 * u % per_bank
                nc.vector.tensor_tensor(
                    out=prod[:, u, :, :].rearrange("p (c i) e -> p c e i", i=2),
                    in0=gq_pair[u].rearrange(by_twos, i=2),
                    in1=banks[2 * u // per_bank][:, e0 : e0 + 2, :].rearrange(by_twos, i=2),
                    op=ALU.mult,
                )
            return prod[:], dist[:]

        def pair_feature(engine, h_bf, terms):
            prod, dist = terms
            engine.tensor_tensor(
                out=h_bf.rearrange("p (n u e) -> p n u e", u=2, e=2),
                in0=prod.rearrange("p u n e -> p n u e"),
                in1=dist.rearrange("p u n e -> p n u e"),
                op=ALU.mult,
            )

        h_codes = {}

        def quantize_h(keys, width, h_bf, slot=None):
            name = "h" + "_".join("%d_%d" % key for key in keys)
            shape = [P, len(keys) * width]
            words = placed(name + "_w", shape, U32) if name + "_w" in PLACE else held(name + "_w", shape, U32, slot)
            scales = held(name + "_s", [P, len(keys) * width], U8)
            nc.vector.quantize_mx(out=words[:].bitcast(FP8X4), scales=scales[:], in_=h_bf)
            for i, key in enumerate(keys):
                h_codes[key] = (words[:, i * width : (i + 1) * width], scales[:, i * width : (i + 1) * width])

        def score_pass(bank, a, n0, codes, opening=0):
            per_bank = bank.shape[1]
            words, scales = codes
            for g in range(per_bank):
                ncols = slice((n0 + g) * P, (n0 + g + 1) * P)
                nc.tensor.matmul_mx(
                    out=bank[:, g, :],
                    lhsT=late["wm"][:, a, ncols].bitcast(FP8X4),
                    lhsT_scale=plane_bytes[4 + 4 * a :, ncols],
                    rhs=words.bitcast(FP8X4),
                    rhs_scale=scales,
                    start=(a == opening and g == 0),
                    stop=(a != opening and g == per_bank - 1),
                )

        def store_scores(bank, n0, j0, copy, slot=None):
            per_bank, width = bank.shape[1], bank.shape[2]
            staged = held("staged%d_%d" % (j0, n0), [P, per_bank, width], F32, slot)
            copy(out=staged[:], in_=bank[:])
            rows = out[n0 * P : (n0 + per_bank) * P, j0 : j0 + width]
            nc.sync.dma_start(out=rows.rearrange("(g p) j -> p g j", p=P), in_=staged[:])

        def scores(j0, width, copies):
            per_bank = N // P // len(copies)
            for i, copy in enumerate(copies):
                bank = psum_qo.tile([P, per_bank, width], F32, name="qo")
                for a in range(2):
                    score_pass(bank, a, i * per_bank, h_codes[a, j0])
                store_scores(bank, i * per_bank, j0, copy)

        LOW = P - 2 * ROWS

        def move_v_scales(k):
            for quad in (0, 2, 1, 3):
                source = LOW + ROWS * k + 4 * quad
                nc.sync.dma_start(out=v_planes[32 * quad + 4 * k + 4 : 32 * quad + 4 * k + 8], in_=v_picked[source : source + 4])

        def quantize_w1(a, k, rounded):
            nc.vector.quantize_mx(out=w1_w[a, k][:].bitcast(FP8X4), scales=w1_s[a][k], in_=rounded)

        nc.vector.memset(w2_raw_s[:TOP], 0)
        nc.vector.memset(tab2_s[:TOP], 0)
        nc.vector.memset(tab_s[:LOW], 0)
        nc.vector.memset(v_planes[:], 0)
        nc.sync.dma_start(out=gain_sb[:], in_=gain.rearrange("(a p t) -> p a t", a=2, t=PACK))
        nc.sync.dma_start(idx2[:], offs2)
        nc.sync.dma_start(out=tab2_s[TOP:], in_=tab2_scales[0].bitcast(I32))
        nc.sync.dma_start(out=w2_raw_s[TOP:], in_=w2_scales[0].bitcast(I32))
        nc.sync.dma_start(idx[:], offs)
        nc.sync.dma_start(out=tab_s[LOW:], in_=tab_scales.rearrange("a q t -> (a q) t").bitcast(I32))
        nc.sync.dma_start(out=w2_raw_w[0][:], in_=w2_words[0][:, :H].bitcast(I32))
        load_w1(0, 0)
        tab2_w = placed("tab2_w", [P, T2], I32)
        nc.sync.dma_start(out=tab2_w[:], in_=tab2_words[0].rearrange("p t i -> p (t i)").bitcast(I32))

        nc.vector.reciprocal(out=gain_recip[:], in_=gain_sb[:])
        nc.vector.tensor_scalar(out=gain_inv[:], in0=gain_recip[:], scalar1=BIG, scalar2=-BIG, op0=ALU.min, op1=ALU.max)
        reorder_w2(w2_s, w2_raw_s[:].bitcast(U8), 2)
        gather(v2_picked, tab2_s, U8, idx2, 0, S)
        nc.vector.tensor_copy(out=planes[:, : S // 4], in_=v2_picked[:].bitcast(I32))
        for quad in (0, 2, 1, 3):
            nc.sync.dma_start(out=planes[32 * quad : 32 * quad + 4], in_=planes[TOP + 4 * quad : TOP + 4 * quad + 4])
        load_tab(0)
        gather(v_picked[:].bitcast(U8), tab_s, U8, idx, 0, S)
        move_v_scales(0)
        load_tab(1)
        move_v_scales(1)
        late["w1", 0, 1] = placed("w1_raw01", [P, 2, PACK, PASS // 2], F32)
        for half in range(2):
            rows = w1[PASS:, half * PASS // 2 : (half + 1) * PASS // 2]
            nc.sync.dma_start(out=late["w1", 0, 1][:, half], in_=rows.rearrange("(p j) r -> p j r", j=PACK))
        w2_raw_w[1] = placed("w2_raw_w1", [P, H // 4], I32)
        nc.sync.dma_start(out=w2_raw_w[1][:], in_=w2_words[0][:, H:].bitcast(I32))
        reorder_w2(w2_w[0][:].bitcast(U16), w2_raw_w[0][:].bitcast(U16), 1)
        rounded = {(a, k): held("w1_bf%d%d" % (a, k), [P, PACK * PASS], BF16)[:] for a, k in ((0, 0), (0, 1), (1, 1))}
        round_w1(rounded[0, 0], 0, 0, [nc.scalar.copy])
        quantize_w1(0, 0, rounded[0, 0])
        gather(v2_w, tab2_w, U32, idx2, 0, BANK)
        gather(v2_w, tab2_w, U32, idx2, BANK, BANK)
        load_w1(1, 0)
        load_w1(1, 1)
        project_candidates(0, 0)
        gather(v_w[0], late["tab", 0], U32, idx, 0, S)
        late["wm"] = placed("wm_w", [P, 2, N], I32)
        nc.sync.dma_start(out=late["wm"][:], in_=wm_words.rearrange("a p n i -> p a (n i)").bitcast(I32))
        gather(v_w[1], late["tab", 1], U32, idx, 0, S)
        for half, copy in enumerate((nc.scalar.copy, nc.vector.tensor_copy)):
            copy(
                out=rounded[0, 1].rearrange("p (t m j) -> p m j t", t=PACK, j=PACK)[:, half * P // 2 : (half + 1) * P // 2],
                in_=late["w1", 0, 1][:, half].rearrange("p j (m t) -> p m j t", t=PACK),
            )
        for half in range(2):
            cols = slice(half * PASS // 2, (half + 1) * PASS // 2)
            nc.vector.quantize_mx(
                out=w1_w[0, 1][:, cols].bitcast(FP8X4),
                scales=w1_s[0][1][:, cols],
                in_=rounded[0, 1][:, half * 2 * PASS : (half + 1) * 2 * PASS],
            )
        reorder_w2(w2_w[1][:].bitcast(U16), w2_raw_w[1][:].bitcast(U16), 1)
        project_candidates(0, 1)

        FINAL = nc.gpsimd
        WIDE = PACK * STEP
        SLIM = PACK * NARROW
        c0, c1, c2, c3, c4 = 0, STEP, 2 * STEP, 3 * STEP, 3 * STEP + NARROW
        by_scalar = nc.scalar.copy

        def feature(engine, name, terms, width, slot=None):
            h_bf = held(name, [P, PACK * width], BF16, slot)[:]
            pair_feature(engine, h_bf, terms)
            return h_bf

        a0 = pair_terms(0, c0, STEP)
        a1 = pair_terms(0, c1, STEP)
        rounded[1, 0] = held("w1_bf10", [P, PACK * PASS], BF16, "w1_bf01")[:]
        round_w1(rounded[1, 0], 1, 0, [round_on_gpsimd] * 2 + [by_scalar] * 2)
        h_a0 = feature(FINAL, "h_a0", a0, STEP)
        round_w1(rounded[1, 1], 1, 1, [by_scalar] * 4)
        a2 = pair_terms(0, c2, STEP)
        h_a1 = feature(FINAL, "h_a1", a1, STEP)
        project_candidates(1, 0)
        for k in range(2):
            w1_w[1, k] = placed("w1_w1%d" % k, [P, PASS], U32)
            quantize_w1(1, k, rounded[1, k])
        h_a2 = feature(FINAL, "h_a2", a2, STEP, "w1_bf01")
        a3 = pair_terms(0, c3, NARROW)
        b0 = pair_terms(1, c0, STEP)
        project_candidates(1, 1)
        load_rows_by_quadrant(planes[:, : N // 4], 4, wm_scales)
        h_a3 = feature(FINAL, "h_a3", a3, NARROW)
        b1 = pair_terms(1, c1, STEP)
        h_b0 = feature(FINAL, "h_b0", b0, STEP)
        quantize_h([(0, c0)], STEP, h_a0)
        quantize_h([(0, c1)], STEP, h_a1)
        quantize_h([(1, c0)], STEP, h_b0)
        h_b1 = feature(FINAL, "h_b1", b1, STEP, "h_a1")
        b2 = pair_terms(1, c2, STEP)
        scores(c0, STEP, [by_scalar] * 3)
        quantize_h([(0, c2)], STEP, h_a2)
        quantize_h([(1, c1)], STEP, h_b1)
        h_b2 = feature(FINAL, "h_b2", b2, STEP, "w1_bf01")
        b3 = pair_terms(1, c3, STEP)
        b3, b4 = [[term[:, :, i * NARROW : (i + 1) * NARROW, :] for term in b3] for i in range(2)]
        scores(c1, STEP, [by_scalar] * 3)
        quantize_h([(0, c3)], NARROW, h_a3)
        quantize_h([(1, c2)], STEP, h_b2)
        h_b3 = feature(FINAL, "h_b3", b3, NARROW, "h_a3")
        a4 = pair_terms(0, c4, NARROW)
        scores(c2, STEP, [by_scalar] * 3)
        fourth = [(psum_p.tile([P, 3, NARROW], F32, name="pp"), n0) for n0 in (0, 3)]
        fifth = [(psum_p.tile([P, 2, NARROW], F32, name="pp"), 0)]
        fifth += [(psum_qo.tile([P, 2, NARROW], F32, name="qo"), n0) for n0 in (2, 4)]
        for bank, n0 in fourth:
            score_pass(bank, 0, n0, h_codes[0, c3])
        h_b4 = feature(nc.vector, "h_b4", b4, NARROW, "gq010b")
        quantize_h([(1, c3)], NARROW, h_b3)
        quantize_h([(1, c4)], NARROW, h_b4)
        h_a4 = feature(nc.vector, "h_a4", a4, NARROW)
        for bank, n0 in fourth:
            score_pass(bank, 1, n0, h_codes[1, c3])
        store_scores(*fourth[0], c3, by_scalar)
        for bank, n0 in fifth:
            score_pass(bank, 1, n0, h_codes[1, c4], 1)
        quantize_h([(0, c4)], NARROW, h_a4)
        store_scores(*fourth[1], c3, nc.vector.tensor_copy, "h_a4")
        for (bank, n0), copy in zip(fifth, (by_scalar, nc.vector.tensor_copy, by_scalar)):
            score_pass(bank, 0, n0, h_codes[0, c4], 1)
            store_scores(bank, n0, c4, copy)
